import numpy as np, ml_dtypes
CORES = [9,25,41,57]
N = 4
import mx_ref
BF = ml_dtypes.bfloat16
def pick(q, e):
    c = np.concatenate([q[0].reshape(128, -1, 4), np.zeros((128, 1, 4), np.uint8)], axis=1); s = np.concatenate([q[1], np.ones((16, 1), np.uint8)], axis=1)
    return (np.ascontiguousarray(c[:, e].reshape(128, -1)), np.ascontiguousarray(s[:, e]))
def join(*qs):
    return (np.concatenate([q[0] for q in qs], axis=1), np.concatenate([q[1] for q in qs], axis=1))
def put(q, e, v):
    c, s = q[0].reshape(128, -1, 4).copy(), q[1].copy(); c[:, e] = v[0].reshape(128, -1, 4); s[:, e] = v[1]
    return (c.reshape(128, -1), s)
def pk(c, s):
    return (np.ascontiguousarray(c), mx_ref.live(s))
def emit(q):
    return q[0], q[1]
def decode(q):
    o = []
    for b in range(4):
        e = np.zeros((128, 128, 4), np.float32); e[np.arange(128), np.arange(128), b] = 1
        o.append(mx_ref.matmul(mx_ref.quantize(e.reshape(128, 512).astype(BF)), q))
    return np.stack(o, axis=2).reshape(128, -1)
def cut(t, i, w=512):
    return t[:, w * i:w * i + w]
def f(rng, *shape):
    return mx_ref.flush((rng.standard_normal(shape, dtype=np.float32) * np.exp2(rng.integers(-2, 3, shape[:-1] + (1,)))).astype(BF))
def wide(rng, *shape, cols=0):
    v = rng.standard_normal(shape, dtype=np.float32) * np.exp2(rng.integers(-12, 13, shape)).astype(np.float32)
    if cols: v *= np.repeat(np.exp2(rng.integers(-cols, cols + 1, shape[:-2] + (1, shape[-1] // 4))) * (rng.random(shape[:-2] + (1, shape[-1] // 4)) > 0.0625), 4, axis=-1).astype(np.float32)
    return mx_ref.flush(v.astype(BF))
P, K, O, L = 512, 192, 2, 2
def times(t, v):
    v = t.astype(np.float32) * np.asarray(v, np.float32)
    return np.where(np.abs(v) < 2.0 ** -16, 0, v).astype(np.float32).astype(BF)
def loud(u, e):
    v = u.astype(np.float32) * np.float32(2.0 ** e)
    return np.where(np.abs(v) < 2.0 ** -30, 0, v).astype(np.float32).astype(BF)
def strong(rng, u, n):
    return np.sign(u[0, :, None, :4].astype(np.float32)) * (1 + rng.random((128, n, 4))) * 128
def near(rng, u):
    ku, v = mx_ref.quantize(np.ascontiguousarray(u[0])), np.repeat(strong(rng, u, 1), 12, axis=1).astype(np.float32)
    v[127] = 0
    z = size(ku, mx_ref.quantize(np.ascontiguousarray(v.reshape(128, -1).astype(BF))))
    v[127, 1:, 0] = np.exp2(np.floor(np.log2(z[0])) - 23 + np.arange(11))
    z = size(ku, mx_ref.quantize(np.ascontiguousarray(v.reshape(128, -1).astype(BF))))
    return v[:, [0, int(np.argmax(z > z[0]))]]
def plain(rng):
    k = np.exp2(6 * rng.random(P) - 3) * np.exp2(rng.random((N, P)) - 0.5)
    u = np.zeros((N, 128, 512), BF)
    u[:, :, :4] = f(rng, 128, 4)
    return {"gr": times(f(rng, N, 128, 4 * P), np.repeat(k, 4, axis=1)[:, None]), "u": u, "w": f(rng, N, 128, 512 * O)}
def setup_inputs(rng):
    return plain(rng)
def setup_inputs_apart(rng):
    d, h = plain(rng), K // 2
    d["u"][:, :8] = 0
    d["u"][:, 120:] = 0
    d["u"][:, 127, 0] = 1
    g = d["gr"].astype(np.float32).reshape(N, 128, P, 4) * np.float32(2.0 ** -8)
    x = rng.permutation(P)[:N // 2 * K].reshape(N // 2, 2, h)
    c = near(rng, d["u"])
    for j in range(N // 2):
        rest = rng.permutation(np.setdiff1d(np.arange(P), x[j].reshape(-1)))[:K].reshape(2, h)
        for i in range(2):
            v = c[:, (x[j, i] >= P // 2).astype(int)]
            v[:8] = (1 + rng.random((8, h, 4))) * 128 * rng.choice([-1.0, 1.0], (8, h, 4))
            g[2 * j + i][:, x[j, i]] = v * np.exp2(rng.integers(0, 3, h))[:, None]
            g[2 * j + i][:, rest[i]] = strong(rng, d["u"], h) * 2.0 ** -4
    d["gr"] = times(g.reshape(N, 128, -1), 1)
    return d
def setup_inputs_cancel(rng):
    d, m = plain(rng), K // 8
    g = d["gr"].astype(np.float32).reshape(N, 128, P, 4)
    e = rng.permutation(P)[:3 * L * m].reshape(L, 3, m)
    g[:, :, e.reshape(-1)] = 0
    for b in range(L):
        for r in range(N):
            h = (r >> b) & 1
            g[r][:, e[b, 1 + h]] = strong(rng, d["u"], m)
            if r % (1 << b) == 0:
                g[r][:, e[b, 0]] = -g[r - (1 << b)][:, e[b, 0]] if h else strong(rng, d["u"], m)
    d["gr"] = times(g.reshape(N, 128, -1), 2.0 ** -10)
    d["u"] = loud(d["u"], -26)
    return d
def setup_inputs_few(rng):
    d, m, h = plain(rng), K // 8, N // 2
    d["u"][:, :64] = 0
    g = d["gr"].astype(np.float32).reshape(N, 128, P, 4)
    g[:, 64:] = 0
    g *= (np.arange(P) % 4 != rng.integers(0, 4, (N, 1)))[:, None, :, None]
    low, e = rng.permutation(K // 4)[:m], K + rng.permutation(P - K)[:(h + 3) * m].reshape(h + 3, m)
    c = np.concatenate([low, e[0]])
    for r in range(N):
        own = e[3 + r] if r < h else e[1:3].reshape(-1)
        g[r][:, own] += strong(rng, d["u"], own.size)
        if r % 2: g[r][:, c] = -g[r - 1][:, c]
        else: g[r][:, c] += strong(rng, d["u"], c.size)
    d["gr"] = times(g.reshape(N, 128, -1), 1)
    d["u"] = loud(d["u"], 24)
    return d
def setup_inputs_spread(rng):
    d = plain(rng)
    e = rng.permutation(P)[:K]
    k = np.exp2(rng.integers(-12, -5, (N, P))) * (rng.random((N, P)) > 0.0625)
    k[:, e] = np.exp2(rng.integers(0, 7, (N, K))) * rng.choice([-1.0, 1.0], (N, K))
    g = wide(rng, N, 128, 4 * P).astype(np.float32).reshape(N, 128, P, 4)
    g[:, :, e] = np.abs(g[:, :, e]) * np.sign(d["u"][0, :, None, :4].astype(np.float32))
    d["gr"] = times(g.reshape(N, 128, -1), np.repeat(k, 4, axis=1)[:, None])
    return d
def setup_inputs_ties(rng):
    d = plain(rng)
    x = f(rng, 128, 24).astype(np.float32).reshape(128, 6, 4)
    h = np.stack([rng.permutation(P) % 6 for r in range(N)])
    sign = rng.choice([-1.0, 1.0], (N, 1, P, 1))
    d["gr"] = times((np.moveaxis(x[:, h], 1, 0) * sign).reshape(N, 128, -1), 1)
    return d
def check_inputs(d):
    b = []
    for k, lo, hi in (("gr", -16, 24), ("u", -30, 30), ("w", -30, 30)):
        v = np.abs(d[k].astype(np.float32))
        if not (np.isfinite(v).all() and ((v == 0) | (v >= 2.0 ** lo) & (v <= 2.0 ** hi)).all()): b.append("a value of " + k)
    v = d["u"].astype(np.float32)
    if (v[:, :, 4:] != 0).any(): b.append("u has numbers behind its column 0")
    if (v != v[:1]).any(): b.append("u isn't the same on all ranks")
    return b
def size(ku, q):
    return np.abs(mx_ref.matmul(ku, q)[0])
def best(s):
    return np.sort(np.argsort(-s, kind="stable")[:K])
def merge(ku, a, b):
    i, j = np.intersect1d(a[0], b[0], return_indices=True)[1:]
    q = join(a[1], b[1])
    v = decode(q).reshape(128, 2 * K, 4)
    v[:, i] = v[:, i] + v[:, K + j]
    q = put(q, i, pick(mx_ref.quantize(np.ascontiguousarray(v.reshape(128, -1).astype(BF))), i))
    n = np.concatenate([a[0], b[0]])
    e = np.setdiff1d(np.arange(2 * K), K + j)
    e = e[np.argsort(n[e])]
    e = e[best(size(ku, q)[e])]
    return n[e], pick(q, e)
def reference(gr, u, w):
    ku, S = [mx_ref.quantize(np.ascontiguousarray(u[r])) for r in range(N)], []
    for r in range(N):
        q = mx_ref.quantize(np.ascontiguousarray(gr[r]))
        e = best(size(ku[r], q))
        S.append((e, pick(q, e)))
    for b in range(L):
        new = list(S)
        for r in range(N):
            p = r ^ (1 << b)
            if r < p: new[r] = new[p] = merge(ku[r], S[r], S[p])
        S = new
    oc, osc = np.zeros((N, 128, 4 * K), np.uint8), np.zeros((N, 16, K), np.uint8)
    nb, y = np.zeros((N, 1, K), np.float32), np.zeros((N, 128, O * K), np.float32)
    for r in range(N):
        oc[r], osc[r] = emit(S[r][1])
        nb[r, 0] = S[r][0]
        for o in range(O): y[r, :, o * K:o * K + K] = mx_ref.matmul(mx_ref.quantize(np.ascontiguousarray(cut(w[r], o))), S[r][1])
    return {"oc": oc, "osc": osc, "nb": nb, "y": y}

@@ -1,0 +1,597 @@
+from concourse.mybir import dt, AluOpType as OP, ActivationFunctionType as AF
+
+P, K, O = 512, 192, 2
+WZ, WA, WB, WY, WM, WE = 0, 32, 224, 416, 480, 672
+NSEM = 40
+BF, F32, I32, U16, CODE, U8 = "bfloat16", "float32", "int32", "uint16", "float8_e4m3fn_x4", "uint8"
+SCRATCH = {"ps": ("psum", [128, 4096], F32)}
+PLACE = {}
+_TOP = {}
+_ALIGN = {BF: 16, F32: 8, I32: 8, U16: 16}
+_ALONE = ("ut", "urt", "grt", "wt", "nbt", "nbw", "yb")
+_CONST = ("one", "zt", "i16", "i128", "i192", "i4", "ni", "nl", "nf", "nlf", "nx", "nrept", "idt", "et", "kw", "kwb", "jv", "jw", "jf", "jwf", "dl", "dh0", "isa", "nisa", "basea", "b511")
+
+
+def _buf(name, n, t):
+    assert name not in PLACE, name
+    if t in _ALIGN and name not in _ALONE:
+        home = ("k" if name in _CONST else "m") + t
+        top = _TOP.get(home, 0)
+        PLACE[name] = (home, top, n)
+        _TOP[home] = -(-(top + n) // _ALIGN[t]) * _ALIGN[t]
+        SCRATCH[home] = ("sbuf", [128, _TOP[home]], t)
+    else:
+        SCRATCH[name] = ("sbuf", [128, n], t)
+        PLACE[name] = (name, 0, n)
+
+
+def _mx(name, n):
+    _buf(name, n, CODE)
+    _buf(name + "s", n, U8)
+
+
+for _n, _w, _t in (
+        ("ut", 4, BF), ("urt", 512, BF), ("grt", 4 * P, BF), ("wt", 1024, BF), ("one", 512, BF), ("zt", 512, BF),
+        ("i16", 128, BF), ("i128", 128, BF), ("i192", K, BF), ("i4", 4, BF), ("ni", 4, I32), ("nl", 4, I32), ("nf", 4, F32), ("nlf", 4, F32), ("nx", 4, F32),
+        ("nrept", 1024, BF), ("idt", 128, BF), ("et", 2048, BF), ("kw", 16, F32), ("kwb", 16, F32),
+        ("jv", 3, I32), ("jw", 3, I32), ("jf", 3, F32), ("jwf", 3, F32), ("dl", 3, F32), ("dh0", 3, F32), ("isa", 3, F32), ("nisa", 3, F32), ("basea", 3, F32),
+        ("srow", P, F32), ("scol", 4, F32), ("c0t", 4 * P, BF), ("p0", 16, F32), ("junk", 128, BF), ("b511", 4, F32),
+        ("x0", 4, F32), ("x1", 4, F32), ("x2", 4, F32), ("x3", 4, F32)):
+    _buf(_n, _w, _t)
+for _n, _w in (("ur", 128), ("q0", P), ("wq", 256), ("oneq", 128), ("zq", 128), ("nrep", 256), ("eq", 512), ("c0q", P), ("fin", K)):
+    _mx(_n, _w)
+for _s in "012":
+    for _n, _w, _t in (("ri", 4, I32), ("hli", 8, I32), ("hl", 8, F32), ("lt", 640, BF), ("off", 16, U16)):
+        _buf(_n + _s, _w, _t)
+    _mx("lq" + _s, 288)
+for _s in "01":
+    for _n, _w, _t in (
+            ("ta", 8, F32), ("in_a", 4, F32), ("h16", 4, F32), ("h16b", 4, F32), ("sla", 4, F32), ("slat", 4, F32), ("tbt", 512, BF), ("tb", 8, F32),
+            ("slb", 4, F32), ("slbt", 4, F32), ("in_b", 4, F32), ("sh", 4, F32), ("at", 640, BF), ("off1", 16, U16), ("ub", 16, F32), ("ub2", 16, F32), ("offb", 16, U16),
+            ("ot", 4 * 384, BF), ("o2t", 1024, BF), ("sht", 4 * 264, BF), ("mrow", K, F32), ("nr", 384, BF),
+            ("nc", 3, F32), ("nl1", 3, F32), ("nh1", 3, F32), ("fl", 3, F32), ("fa", 3, F32), ("fo", 3, F32), ("fk", 3, F32), ("bs", 3, F32), ("bs2", 3, F32), ("bs3", 3, F32), ("fb", 3, F32), ("fb2", 3, F32), ("dhr", 3, F32),
+            ("tau", 3 * K, BF), ("ht", 4 * K, BF), ("arow", K, F32), ("acol", 3, F32), ("v", 3 * K, BF), ("ct", 1024, BF), ("cj", 2 * K, BF), ("rs", 3, F32), ("rb", 3, F32)):
+        _buf(_n + _s, _w, _t)
+    for _n, _w in (("tq", 128), ("tl", 128), ("aq", 288), ("win", WE), ("ash", K), ("bun", 256), ("oq", 384), ("o2q", 256), ("shq", 264), ("cq", 256)):
+        _mx(_n + _s, _w)
+for _n, _w, _t in (("pjt", 512, BF), ("tj", 3, F32), ("tj2", 3, F32), ("pj", 3, F32), ("pj0", 3, F32), ("rtt", 512, BF), ("rtm", 3, F32), ("nnc", 3, F32),
+                   ("trit", 4 * 384, BF), ("xt", 512, BF), ("rf", 3, F32), ("ntk", 3, F32), ("ntk2", 3, F32), ("nbt0", 512, BF), ("nbw", 32, F32), ("nbt", 32, F32), ("yb", O * K, F32)):
+    _buf(_n, _w, _t)
+for _n, _w in (("pjq", 128), ("nbq", 160), ("rtq", 128), ("triq", 384), ("xq", 128)):
+    _mx(_n, _w)
+ARR = ["tc0", "ts0", "wc0", "ws0", "tc1", "ts1", "wc1", "ws1"]
+SEMAPHORES = ["q_v", "q_s", "q_t", "q_g"] + ["d%d" % i for i in range(NSEM)] + ["l_" + a for a in ARR] + ["a_" + a for a in ARR]
+
+
+def rank_program(g, core, T, topo):
+    rank = T.rank_of(core)
+    if rank is None:
+        return
+    ENG = {"v": g.vector, "s": g.scalar, "t": g.tensor, "g": g, "y": g.sync}
+    prog, acc, nd, sent = [], {}, [0], []
+
+    def v(name, a=0, b=None, s=1, p=0, e=128, cast=None):
+        if name == "ps":
+            return (name, a, b, s, p, e, cast)
+        home, o, n = PLACE[name]
+        return (home, o + a, o + (n if b is None else b), s, p, e, cast)
+
+    def ap(x):
+        if not isinstance(x, tuple):
+            return x
+        name, a, b, s, p, e, cast = x
+        t = T[name]
+        r = t[p:e, a:b] if s == 1 else t[p:e, a:b:s]
+        if cast is None:
+            return r
+        return r.bitcast(dt.uint8 if cast == 8 else dt.uint32)
+
+    def overlap(x, y):
+        if x[0] == "ps":
+            f = lambda r: set(c // 512 for c in range(r[1], r[2], r[3] if r[3] == 512 else 1))
+            return bool(f(x) & f(y))
+        if x[1] >= y[2] or y[1] >= x[2]:
+            return False
+        if x[3] == y[3] and x[3] > 1:
+            return (x[1] - y[1]) % x[3] == 0
+        return True
+
+    def rec(q, fn, reads, writes, kind="c", sem=None, amount=0, after=()):
+        i = len(prog)
+        deps = set(after)
+        for regs, w in ((reads, False), (writes, True)):
+            for x in regs:
+                for (y, yw, j) in acc.get(x[0], ()):
+                    if not overlap(x, y):
+                        continue
+                    if prog[j]["q"] == q and prog[j]["kind"] == "c" and kind == "c":
+                        if q == "t" and x[0] == "ps":
+                            continue
+                        if yw:
+                            deps.add(j)
+                    elif w or yw or x[0] == "ps":
+                        deps.add(j)
+        prog.append({"q": q, "fn": fn, "deps": deps, "kind": kind, "sem": sem, "amount": amount})
+        for x in reads:
+            acc.setdefault(x[0], []).append((x, False, i))
+        for x in writes:
+            acc.setdefault(x[0], []).append((x, True, i))
+        return i
+
+    tens = lambda *xs: [x for x in xs if isinstance(x, tuple)]
+
+    def ts(out, in0, s1, op0, s2=None, op1=None):
+        if op1 is None:
+            fn = lambda: g.vector.tensor_scalar(out=ap(out), in0=ap(in0), scalar1=ap(s1), scalar2=None, op0=op0)
+        else:
+            fn = lambda: g.vector.tensor_scalar(out=ap(out), in0=ap(in0), scalar1=ap(s1), scalar2=ap(s2), op0=op0, op1=op1)
+        return rec("v", fn, tens(in0, s1, s2), [out])
+
+    def tt(out, a, b, op):
+        rec("v", lambda: g.vector.tensor_tensor(out=ap(out), in0=ap(a), in1=ap(b), op=op), [a, b], [out])
+
+    def cp(out, a):
+        rec("v", lambda: g.vector.tensor_copy(ap(out), ap(a)), [a], [out])
+
+    def fill(out, c=0.0):
+        rec("v", lambda: g.vector.memset(ap(out), c), [], [out])
+
+    def act(out, a, func, bias=None, scale=None, accum=None):
+        kw = {}
+        if bias is not None:
+            kw["bias"] = bias
+        if scale is not None:
+            kw["scale"] = scale
+        if accum is not None:
+            kw["accum_out"] = accum
+        rec("s", lambda: g.scalar.activation(ap(out), ap(a), func, **{k: ap(x) for k, x in kw.items()}), tens(a, bias, scale), tens(out, accum))
+
+    def zero(out):
+        act(out, v("zt", 0, len(range(out[1], out[2], out[3]))), AF.Copy)
+
+    def pl(x):
+        return (x[0] + "s",) + x[1:6] + (None,)
+
+    def quant(out, a):
+        return rec("v", lambda: g.vector.quantize_mx(ap(out), ap(pl(out)), ap(a)), [a], [out, pl(out)])
+
+    def mm(bank, l, r, start=True, stop=True):
+        out = v("ps", 512 * bank, 512 * bank + r[2] - r[1])
+        rec("t", lambda: g.tensor.matmul_mx(ap(out), ap(l), ap(pl(l)), ap(r), ap(pl(r)), start, stop), [l, pl(l), r, pl(r)], [out])
+
+    def pick(out, win, off):
+        c = lambda x: x[:6] + (32,)
+        rec("v", lambda: g.vector.tensor_copy(ap(c(out)), ap(c(win)).indirect(ap(off))), [win, off], [out])
+        rec("s", lambda: g.scalar.activation(ap(pl(out)), ap(pl(win)).indirect(ap(off)), AF.Copy), [pl(win), off], [pl(out)])
+
+    def dma(q, out, in_, reads, writes, after=()):
+        n = nd[0]
+        nd[0] += 1
+        rec(q, lambda: ENG[q].dma_start(out() if not isinstance(out, tuple) else ap(out), in_() if not isinstance(in_, tuple) else ap(in_)), reads, writes, "d", "d%d" % n, 16, after)
+
+    def mxcopy(q, out, in_, after=()):
+        c = lambda x: x[:6] + (8,)
+        dma(q, c(out), c(in_), [in_], [out], after)
+        dma(q, pl(out), pl(in_), [pl(in_)], [pl(out)], after)
+
+    def send(peer, out, in_, key):
+        dst = T.cores[peer]
+        rid, pid, _ = topo.addr(dst)
+        m, n = topo.mask(core, dst), len(topo.engines(core, dst))
+        rec("g", lambda: g.remote_dma(ap(out), ap(in_), T.sem["a_" + key], T.sem["l_" + key], pid, rid, m), [in_], [], "r", "l_" + key, n)
+        sent.append((key, out, len(topo.engines(dst, core))))
+
+    def sendmx(peer, out, in_, kc, ks):
+        c = lambda x: x[:6] + (8,)
+        send(peer, c(out), c(in_), kc)
+        send(peer, pl(out), pl(in_), ks)
+
+    def arrive(key):
+        for k, out, n in sent:
+            if k == key:
+                rec(None, None, [], [out], "a", "a_" + key, n)
+
+    ps = lambda bank, a, b: v("ps", 512 * bank + a, 512 * bank + b)
+    pst = lambda bank, n, c: v("ps", 512 * bank + c, 512 * (bank + n - 1) + c + 1, 512)
+    col = lambda name, o=0: (lambda t: v(name, o + t, o + t + 1))
+    one = v("one", 0, 128)
+
+    def iota(out, pattern, base, cm, flag=True):
+        kw = {"allow_small_or_imprecise_dtypes": True} if flag else {}
+        rec("g", lambda: g.iota(ap(out), pattern, base, cm, **kw), [], [out])
+
+    dma("y", v("ut"), lambda: T.u[:, 0:4], [], [v("ut")])
+    for c in range(4):
+        x = v("grt", 512 * c, 512 * c + 512)
+        dma("sy"[c % 2], x, (lambda c=c: T.gr[:, 512 * c:512 * c + 512]), [], [x])
+
+    iota(v("ni"), [[128, 4]], 0, 1, False)
+    iota(v("i16"), [[0, 8], [1, 16]], 0, 0)
+    fill(v("zt"))
+    fill(v("one"), 1.0)
+    ts(v("nl"), v("ni"), 15, OP.bitwise_and)
+    cp(v("nf"), v("ni"))
+    cp(v("nlf"), v("nl"))
+    ts(v("b511"), v("nf"), -1.0, OP.mult, 511.0, OP.add)
+    tt(v("nx"), v("nf"), v("nlf"), OP.subtract)
+    ts(v("nx"), v("nx"), -256.0, OP.add)
+    rec("g", lambda: g.affine_select(ap(v("idt")), ap(one), [[-1, 128]], OP.is_equal, 0.0, 0, 1), [one], [v("idt")])
+    for b in range(4):
+        zero(v("et", 512 * b, 512 * b + 512))
+        act(v("et", 512 * b + b, 512 * b + 512, 4), v("idt"), AF.Copy)
+    iota(v("i192"), [[1, K]], 0, 0)
+    iota(v("jv"), [[128, 3]], 0, 1, False)
+    iota(v("jw"), [[128, 3]], WA + 16, 1, False)
+    iota(v("kw"), [[16, 16]], 0, 0)
+    iota(v("i128"), [[1, 128]], 0, 0)
+    iota(v("i4"), [[1, 4]], -2, 0)
+    iota(v("sht0", 512, 1056), [[0, 544]], 0, 0)
+    for t in (1, 2, 3):
+        fill(v("c0t", t, 512 * t, 4))
+    fill(v("p0"))
+    quant(v("oneq"), v("one"))
+    quant(v("zq"), v("zt"))
+    quant(v("lq0", 160, 288), v("zt"))
+    fill(v("hli1"))
+    fill(v("hli2"))
+    fill(v("nbw"))
+    ts(v("kw"), v("kw"), v("nlf", 0, 1), OP.add)
+    ts(v("kwb"), v("kw"), float(WB), OP.add)
+    cp(v("jf"), v("jv"))
+    ts(v("jw"), v("jw"), 31, OP.bitwise_and)
+    cp(v("jwf"), v("jw"))
+    ts(v("dl"), v("jwf"), -16.0, OP.add)
+    tt(v("dh0"), v("jf"), v("dl"), OP.subtract)
+    ts(v("dh0"), v("dh0"), float(WA - 320), OP.add)
+    ts(v("isa"), v("jf"), K - 0.5, OP.is_lt)
+    ts(v("nisa"), v("isa"), -1.0, OP.mult)
+    ts(v("basea"), v("jf"), float(K), OP.add)
+    tt(v("basea"), v("basea"), v("isa"), OP.mult)
+    fill(v("tbt0"))
+    fill(v("o2t0", 4 * K, 1024))
+    for t in range(4):
+        ts(v("urt", t, 512, 4), one, v("ut", t, t + 1), OP.mult)
+    quant(v("ur"), v("urt"))
+
+    def sizes(c):
+        qc = v("q0", 128 * c, 128 * c + 128)
+        quant(qc, v("grt", 512 * c, 512 * c + 512))
+        mm(4 + c, qc, v("ur"))
+        mm(c, v("ur"), qc)
+        act(v("scol", c, c + 1), ps(4 + c, 0, 1), AF.Abs)
+        act(v("srow", 128 * c, 128 * c + 128), ps(c, 0, 128), AF.Abs)
+
+    def upper(blk):
+        rec("g", lambda: g.affine_select(ap(blk), ap(blk), [[1, 128]], OP.is_gt, 0.0, 0, -1), [blk], [blk])
+
+    def compare(c):
+        for t in [c] + list(range(c)):
+            blk = v("c0t", 512 * c + t, 512 * c + 512, 4)
+            ts(blk, v("srow", 128 * c, 128 * c + 128), v("scol", t, t + 1), OP.is_le)
+            if t == c:
+                upper(blk)
+
+    def count(c):
+        for t in range(c + 1):
+            act(v("junk"), v("c0t", 512 * c + t, 512 * c + 512, 4), AF.Copy, accum=v("p0", 4 * c + t, 4 * c + t + 1))
+        quant(v("c0q", 128 * c, 128 * c + 128), v("c0t", 512 * c, 512 * c + 512))
+        mm(c, v("c0q", 128 * c, 128 * c + 128), v("oneq"))
+
+    def countx(c):
+        tt(v("x%d" % c), v("b511") if c == 0 else v("x%d" % (c - 1)), v("p0", 4 * c, 4 * c + 4), OP.subtract)
+
+    sizes(0)
+    sizes(1)
+    compare(0)
+    sizes(2)
+    compare(1)
+    sizes(3)
+    compare(2)
+    count(0)
+    compare(3)
+    count(1)
+    count(2)
+    countx(0)
+    countx(1)
+    count(3)
+    countx(2)
+    countx(3)
+    tt(v("ri0"), pst(0, 4, 0), v("x3"), OP.add)
+
+    def hilo(s, n):
+        ts(v("hli" + s, 0, n), v("ri" + s, 0, n), 4, OP.arith_shift_right)
+        ts(v("hli" + s, 4, 4 + n), v("ri" + s, 0, n), 15, OP.bitwise_and)
+        cp(v("hl" + s), v("hli" + s))
+
+    def listtile(tile, n, hi, lo, values):
+        for t in range(n):
+            ts(v(tile, t, 512, 4), v("i16"), lo(t), OP.is_equal)
+        for k, val in enumerate(values):
+            for t in range(n):
+                ts(v(tile, 512 + 64 * k + t, 576 + 64 * k, 4), v("i16", 0, 16), hi(t), OP.is_equal, val(t), OP.mult)
+
+    def listmm(bank, q):
+        mm(bank, v(q, 0, 128), v(q, 128, 256), True, False)
+        mm(bank, v(q, 0, 128), v(q, 144, 272), False, True)
+
+    hilo("0", 4)
+    listtile("lt0", 4, col("hl0"), col("hl0", 4), [col("nx"), col("nlf")])
+    quant(v("lq0", 0, 160), v("lt0"))
+    listmm(4, "lq0")
+    ts(v("ta0", 0, 4), v("hl0", 0, 4), 12.0, OP.min)
+    cp(v("ta0", 4, 8), v("hl0", 4, 8))
+    cp(v("tbt0", 0, 8), v("ta0"))
+    ts(v("off0"), ps(4, 0, 16), 256.0, OP.add)
+    mark = quant(v("tq0"), v("tbt0"))
+    pick(v("win0", WA, WB), v("q0"), v("off0", 0, 12))
+    peer = rank ^ 1
+    sendmx(peer, v("tl0", 0, 2), v("tq0", 0, 2), "tc0", "ts0")
+    sendmx(peer, v("win0", WB, WY), v("win0", WA, WB), "wc0", "ws0")
+    for s in "01":
+        mxcopy("y", v("tl" + s, 2, 128), v("zq", 2, 128), [mark])
+        mxcopy("y", v("win" + s, WZ, WA), v("zq", 0, 32), [mark])
+        mxcopy("y", v("win" + s, WY, WM), v("zq", 0, 64), [mark])
+    dma("y", v("wt"), lambda: T.w[:, :], [], [v("wt")], [mark])
+
+    def own(s):
+        ha, la = v("ta" + s, 0, 4), v("ta" + s, 4, 8)
+        ts(v("in_a" + s), ha, 11.5, OP.is_lt)
+        ts(v("h16" + s), ha, 16.0, OP.mult, float(WA), OP.add)
+        ts(v("slat" + s), ha, 16.0, OP.mult)
+        tt(v("h16b" + s), v("h16" + s), v("in_a" + s), OP.mult)
+        tt(v("sla" + s), v("slat" + s), la, OP.add)
+        for t in range(4):
+            ts(v("ot" + s, t, 4 * K, 4), v("i192"), v("sla" + s, t, t + 1), OP.is_equal)
+            ts(v("o2t" + s, t, 4 * K, 4), v("i192"), v("sla" + s, t, t + 1), OP.is_gt)
+        quant(v("oq" + s, 0, K), v("ot" + s, 0, 4 * K))
+        quant(v("o2q" + s), v("o2t" + s))
+
+    def numbers(s, bank, a):
+        mm(bank, v("nrep", 0, 128), v("oq" + s, a, a + K), True, False)
+        mm(bank, v("nrep", 128, 256), v("oq" + s, a, a + K), False, True)
+        act(v("nr" + s, a, a + K), ps(bank, 0, K), AF.Copy)
+
+    def before(s, last):
+        arrive("tc" + s)
+        arrive("ts" + s)
+        for b in range(4):
+            mm(b, v("eq", 128 * b, 128 * b + 128), v("tl" + s))
+        hb = v("tb" + s, 0, 4)
+        listtile("at" + s, 4, lambda t: ps(t, 0, 1), lambda t: ps(t, 1, 2), [col("h16b" + s), col("ta" + s, 4)])
+        quant(v("aq" + s, 0, 160), v("at" + s))
+        cp(hb, pst(0, 4, 0))
+        cp(v("tb" + s, 4, 8), pst(0, 4, 1))
+        listmm(7, "aq" + s)
+        ts(v("in_b" + s), hb, 11.5, OP.is_lt)
+        ts(v("slbt" + s), hb, 16.0, OP.mult)
+        tt(v("sh" + s), v("in_a" + s), v("in_b" + s), OP.mult)
+        tt(v("slb" + s), v("slbt" + s), v("tb" + s, 4, 8), OP.add)
+        cp(v("sht" + s, 528, 532), v("sh" + s))
+        for t in range(4):
+            act(v("sht" + s, t, 512, 4), one, AF.Identity, scale=v("sh" + s, t, t + 1))
+        cp(v("off1" + s), ps(7, 0, 16))
+        ts(v("ub" + s), ps(7, 0, 16), WA - 0.5, OP.is_lt)
+        pick(v("ash" + s), v("win" + s, 0, WB), v("off1" + s, 0, 12))
+        for b in range(4):
+            mm(b, v("eq", 128 * b, 128 * b + 128), v("ash" + s), True, False)
+        tt(v("ub2" + s), v("ub" + s), v("kwb"), OP.mult)
+        for t in range(4):
+            ts(v("ot" + s, 4 * K + t, 8 * K, 4), v("i192"), v("slb" + s, t, t + 1), OP.is_equal)
+        cp(v("offb" + s), v("ub2" + s))
+        quant(v("oq" + s, K, 2 * K), v("ot" + s, 4 * K, 8 * K))
+        quant(v("shq" + s), v("sht" + s))
+        mm(7, v("shq" + s, 0, 128), v("oq" + s, K, 2 * K))
+        act(v("mrow" + s), ps(7, 0, K), AF.Copy)
+        if last:
+            numbers(s, 6, K)
+        for t in range(3):
+            mm(4 + t, v("oq" + s, 128 * t, 128 * t + 128), v("shq" + s, 128, 256), True, t == 2)
+            if t < 2:
+                mm(4 + t, v("o2q" + s, 128 * t, 128 * t + 128), v("shq" + s, 130, 258), False, True)
+        act(v("nh1" + s), pst(4, 3, 0), AF.Copy)
+        act(v("nl1" + s), pst(4, 3, 1), AF.Copy)
+        act(v("fl" + s), pst(4, 3, 4), AF.Copy)
+        act(v("bs" + s), pst(4, 3, 2), AF.Copy)
+        if last:
+            mxcopy("y", v("nbq", 128, 160), v("zq", 0, 32))
+        else:
+            act(v("tj"), pst(4, 3, 14), AF.Copy)
+        mxcopy("y", v("bun" + s, 0, 64), v("win" + s, WA + 128, WB))
+
+    def merge(s, last):
+        w, bun = "win" + s, "bun" + s
+        arrive("wc" + s)
+        arrive("ws" + s)
+        for b in range(4):
+            mm(b, v("eq", 128 * b, 128 * b + 128), v(w, WB, WY), False, True)
+        pick(v(bun, 64, 256), v(w, 0, WY), v("offb" + s, 0, 12))
+        tt(v("nc" + s), v("nh1" + s), v("nl1" + s), OP.add)
+        if last:
+            ts(v("nnc"), v("nc" + s), -1.0, OP.mult)
+            for t in range(3):
+                act(v("trit", t, 4 * 384, 4), v("nr1"), AF.Sign, bias=v("nnc", t, t + 1))
+            zero(v("nbt0"))
+        for b in range(4):
+            tt(v("ht" + s, b, 4 * K, 4), ps(b, 0, K), v("mrow" + s), OP.mult)
+        mm(7, v("ur"), v(bun, 64, 256), True, False)
+        mm(0, v(w, WA, WA + 128), v("ur"))
+        act(v("acol" + s, 0, 1), ps(0, 0, 1), AF.Abs)
+        if not last:
+            numbers(s, 3, K)
+        quant(v(w, WM, WE), v("ht" + s))
+        mm(7, v("ur"), v(w, WM, WE), False, True)
+        mm(1, v(bun, 0, 128), v("ur"), True, False)
+        mm(1, v(w, WY, WY + 128), v("ur"), False, True)
+        mm(2, v(bun, 128, 256), v("ur"), True, False)
+        mm(2, v(w, WY + 128, WE), v("ur"), False, True)
+        tt(v("fa" + s), v("fl" + s), v("isa"), OP.mult)
+        ts(v("fo" + s), v("fa" + s), 2.0, OP.mult, -0.5, OP.add)
+        for t in range(3):
+            ts(v("tau" + s, K * t, K * t + K), v("nr" + s, K, 2 * K), v("nc" + s, t, t + 1), OP.is_le, v("fo" + s, t, t + 1), OP.add)
+        ts(v("fk" + s), v("fa" + s), 1000.0, OP.mult)
+        tt(v("fb" + s), v("fl" + s), v("fa" + s), OP.subtract)
+        tt(v("bs3" + s), v("basea"), v("bs" + s), OP.subtract)
+        tt(v("bs2" + s), v("fk" + s), v("bs3" + s), OP.add)
+        ts(v("fb2" + s), v("fb" + s), float(WM - WB), OP.mult)
+        tt(v("dhr" + s), v("fb2" + s), v("dh0"), OP.add)
+        if not last:
+            ts(v("tj2"), v("tj"), -128.0, OP.mult)
+            ts(v("pj0"), v("fa0"), -4096.0, OP.mult)
+            tt(v("tj2"), v("tj2"), v("nc0"), OP.add)
+            tt(v("pj"), v("tj2"), v("pj0"), OP.add)
+        act(v("arow" + s), ps(7, 0, K), AF.Abs)
+        act(v("acol" + s, 1, 3), pst(1, 2, 0), AF.Abs)
+        for t in range(3):
+            act(v("v" + s, K * t, K * t + K), v("arow" + s), AF.Sign, bias=v("acol" + s, t, t + 1), scale=-1.0)
+            tt(v("ct" + s, 256 + t, 1024, 4), v("v" + s, K * t, K * t + K), v("tau" + s, K * t, K * t + K), OP.is_gt)
+        for t in range(2):
+            act(v("cj" + s, K * t, K * t + K), v("ct" + s, 256 + t, 1024, 4), AF.Identity, scale=v("nisa", t, t + 1), accum=v("rs" + s, t, t + 1))
+        quant(v("cq" + s), v("ct" + s))
+        mm(5, v("cq" + s, 0, 128), v("oneq"))
+        mm(6, v("cq" + s, 128, 256), v("oneq"))
+        if not last:
+            for t in range(3):
+                ts(v("pjt", t, 512, 4), v("i128"), v("pj", t, t + 1), OP.is_equal)
+            quant(v("pjq"), v("pjt"))
+        tt(v("rb" + s, 0, 2), v("bs2" + s, 0, 2), v("rs" + s, 0, 2), OP.add)
+        cp(v("rb" + s, 2, 3), v("bs2" + s, 2, 3))
+        if last:
+            quant(v("triq"), v("trit"))
+
+    for t in range(4):
+        act(v("nrept", t, 512, 4), one, AF.Identity, scale=v("nx", t, t + 1))
+        act(v("nrept", 512 + t, 1024, 4), one, AF.Identity, scale=v("nlf", t, t + 1))
+    act(v("sht0", 512, 516), v("nx"), AF.Copy)
+    act(v("sht0", 516, 520), v("nlf"), AF.Copy)
+    zero(v("ct0", 3, 1024, 4))
+    zero(v("ct0", 0, 256))
+    zero(v("rtt"))
+    zero(v("pjt", 3, 512, 4))
+    zero(v("lt1", 3, 640, 4))
+    zero(v("tbt1"))
+    zero(v("o2t1", 4 * K, 1024))
+    quant(v("eq"), v("et"))
+    own("0")
+    quant(v("aq0", 160, 288), v("zt"))
+    quant(v("nrep"), v("nrept"))
+    for t in range(4):
+        fill(v("sht0", 568 + t, 569 + t), t - 2.0)
+    quant(v("lq1", 160, 288), v("zt"))
+    before("0", False)
+    merge("0", False)
+
+    cp(v("ri1", 0, 1), v("rb0", 0, 1))
+    tt(v("ri1", 1, 3), pst(5, 2, 0), v("rb0", 1, 3), OP.add)
+    hilo("1", 3)
+    listtile("lt1", 3, col("hl1"), col("hl1", 4), [col("dhr0"), col("dl")])
+    quant(v("lq1", 0, 160), v("lt1"))
+    listmm(3, "lq1")
+    ts(v("rtm"), v("hl1", 0, 3), -12.0, OP.add, 0.0, OP.min)
+    for t in range(3):
+        ts(v("rtt", t, 16, 4), v("i4"), v("tj", t, t + 1), OP.is_equal, v("rtm", t, t + 1), OP.mult)
+        ts(v("rtt", 16 + t, 32, 4), v("i4"), v("tj", t, t + 1), OP.is_equal, v("hl1", 4 + t, 5 + t), OP.mult)
+    ts(v("off1"), ps(3, 0, 16), 320.0, OP.add)
+    quant(v("rtq"), v("rtt"))
+    pick(v("win1", WA, WB), v("win0"), v("off1", 0, 12))
+    mm(4, v("pjq"), v("rtq"))
+    ts(v("ta1", 0, 4), ps(4, 0, 4), 12.0, OP.add)
+    cp(v("ta1", 4, 8), ps(4, 4, 8))
+    cp(v("tbt1", 0, 8), v("ta1"))
+    quant(v("tq1"), v("tbt1"))
+    peer = rank ^ 2
+    sendmx(peer, v("tl1", 0, 2), v("tq1", 0, 2), "tc1", "ts1")
+    sendmx(peer, v("win1", WB, WY), v("win1", WA, WB), "wc1", "ws1")
+    act(v("sht1", 512, 1056), v("sht0", 512, 1056), AF.Copy)
+    zero(v("xt"))
+    zero(v("trit", 3, 4 * 384, 4))
+    zero(v("ct1", 3, 1024, 4))
+    zero(v("ct1", 0, 256))
+    zero(v("lt2", 3, 640, 4))
+    own("1")
+    numbers("1", 6, 0)
+    quant(v("aq1", 160, 288), v("zt"))
+    quant(v("wq"), v("wt"))
+    quant(v("lq2", 160, 288), v("zt"))
+    before("1", True)
+    merge("1", True)
+
+    cp(v("rf", 0, 1), v("rb1", 0, 1))
+    tt(v("rf", 1, 3), pst(5, 2, 0), v("rb1", 1, 3), OP.add)
+    ts(v("xt", 0, 3), v("rf"), K - 0.5, OP.is_lt, 0.5, OP.mult)
+    quant(v("xq"), v("xt"))
+    ts(v("ntk"), v("rf"), K - 0.5, OP.is_gt, 1024.0, OP.mult)
+    for c in range(3):
+        mm(4 + c, v("triq", 128 * c, 128 * c + 128), v("xq"))
+    ts(v("ntk2"), v("ntk"), (K - 1) / 2, OP.add)
+    tt(v("ri2", 0, 3), pst(4, 3, 0), v("ntk2"), OP.add)
+    hilo("2", 3)
+    listtile("lt2", 3, col("hl2"), col("hl2", 4), [col("dhr1"), col("dl")])
+    quant(v("lq2", 0, 160), v("lt2"))
+    listmm(3, "lq2")
+    for k, val in enumerate((col("nh11"), col("nl11"))):
+        for t in range(3):
+            ts(v("nbt0", 64 * k + t, 64 * k + 64, 4), v("i16", 0, 16), v("hl2", t, t + 1), OP.is_equal, val(t), OP.mult)
+    ts(v("off2"), ps(3, 0, 16), 320.0, OP.add)
+    fin = v("fin")
+    pick(fin, v("win1"), v("off2", 0, 12))
+    quant(v("nbq", 0, 128), v("nbt0"))
+    dma("y", lambda: T.oc[:, :], lambda: T.fin[:, :].bitcast(dt.uint8), [fin], [])
+    for k in range(4):
+        dma("sy"[k % 2], (lambda k=k: T.osc[4 * k:4 * k + 4, :]), (lambda k=k: T.fins[32 * k:32 * k + 4, :]), [pl(fin)], [])
+    for o in range(O):
+        mm(o, v("wq", 128 * o, 128 * o + 128), fin)
+    mm(7, v("lq2", 0, 128), v("nbq", 0, 128), True, False)
+    mm(7, v("lq2", 0, 128), v("nbq", 16, 144), False, True)
+    act(v("yb", 0, K), ps(0, 0, K), AF.Copy)
+    dma("s", lambda: T.y[:, 0:K], v("yb", 0, K), [v("yb", 0, K)], [])
+    ts(v("nbw", 0, 16, 1, 0, 32), v("ps", 7 * 512, 7 * 512 + 16, 1, 0, 32), 256.0, OP.add)
+    rec("v", lambda: g.vector.transpose(T.nbt[0:32, :], T.nbw[0:32, :]), [v("nbw")], [v("nbt")])
+    cp(v("yb", K, 2 * K), ps(1, 0, K))
+    dma("y", lambda: T.nb[:, :], lambda: T.nbt[0:12, 0:16], [v("nbt")], [])
+    dma("y", lambda: T.y[:, K:2 * K], v("yb", K, 2 * K), [v("yb", K, 2 * K)], [])
+
+    know, snap, need, used = {}, [], [], set()
+    key = lambda i: (prog[i]["q"], i) if prog[i]["kind"] == "c" else (i, 0)
+    for i, r in enumerate(prog):
+        k = know.setdefault(r["q"], {}) if r["q"] else {}
+        last = {}
+        for d in r["deps"]:
+            a, n = key(d)
+            if k.get(a, -1) < n and (a not in last or key(last[a])[1] < n):
+                last[a] = d
+        ds = sorted(last.values())
+        ds = [d for d in ds if not any(e != d and snap[e].get(key(d)[0], -1) >= key(d)[1] for e in ds)]
+        for d in ds:
+            used.add(d)
+            for a, n in snap[d].items():
+                if k.get(a, -1) < n:
+                    k[a] = n
+        s = dict(k)
+        s[key(i)[0]] = key(i)[1]
+        snap.append(s)
+        need.append(ds)
+    lastc = {r["q"]: i for i, r in enumerate(prog) if r["kind"] == "c"}
+    used |= set(lastc.values())
+    total, val = {q: 0 for q in lastc}, {}
+    for i, r in enumerate(prog):
+        if r["q"] is None:
+            continue
+        e = ENG[r["q"]]
+        for d in need[i]:
+            p = prog[d]
+            if p["kind"] == "c":
+                e.wait_ge(T.sem["q_" + p["q"]], val[d])
+            else:
+                e.wait_ge(T.sem[p["sem"]], p["amount"])
+        ins = r["fn"]()
+        if r["kind"] == "c" and i in used:
+            total[r["q"]] += 1
+            val[i] = total[r["q"]]
+            ins.then_inc(T.sem["q_" + r["q"]], 1)
+        elif r["kind"] == "d":
+            ins.then_inc(T.sem[r["sem"]], 16)
+    for q in total:
+        g.wait_ge(T.sem["q_" + q], total[q])
+    for r in prog:
+        if r["kind"] in "dra":
+            g.wait_ge(T.sem[r["sem"]], r["amount"])

@@ -1,15 +1,17 @@
 from concourse.mybir import dt, AluOpType as OP, ActivationFunctionType as AF
 
 P, K, O = 512, 192, 2
-WZ, WA, WB, WY, WM, WE = 0, 32, 224, 416, 480, 672
+WB, WA, WZ, WM, WY, WE = 0, 192, 384, 416, 608, 672
 NSEM = 40
+MID = 320
+ROUND16 = 1.5 * 2.0 ** 27
 BF, F32, I32, U16, CODE, U8 = "bfloat16", "float32", "int32", "uint16", "float8_e4m3fn_x4", "uint8"
 SCRATCH = {"ps": ("psum", [128, 4096], F32)}
 PLACE = {}
 _TOP = {}
 _ALIGN = {BF: 16, F32: 8, I32: 8, U16: 16}
-_ALONE = ("ut", "urt", "grt", "wt", "nbt", "nbw", "yb")
-_CONST = ("one", "zt", "i16", "i128", "i192", "i4", "ni", "nl", "nf", "nlf", "nx", "nrept", "idt", "et", "kw", "kwb", "jv", "jw", "jf", "jwf", "dl", "dh0", "isa", "nisa", "basea", "b511")
+_ALONE = ("ut", "urt", "nurt", "grt", "wt", "nbw", "yb")
+_CONST = []
 
 
 def _buf(name, n, t):
@@ -31,34 +33,32 @@ def _mx(name, n):
 
 
 for _n, _w, _t in (
-        ("ut", 4, BF), ("urt", 512, BF), ("grt", 4 * P, BF), ("wt", 1024, BF), ("one", 512, BF), ("zt", 512, BF),
-        ("i16", 128, BF), ("i128", 128, BF), ("i192", K, BF), ("i4", 4, BF), ("ni", 4, I32), ("nl", 4, I32), ("nf", 4, F32), ("nlf", 4, F32), ("nx", 4, F32),
-        ("nrept", 1024, BF), ("idt", 128, BF), ("et", 2048, BF), ("kw", 16, F32), ("kwb", 16, F32),
-        ("jv", 3, I32), ("jw", 3, I32), ("jf", 3, F32), ("jwf", 3, F32), ("dl", 3, F32), ("dh0", 3, F32), ("isa", 3, F32), ("nisa", 3, F32), ("basea", 3, F32),
-        ("srow", P, F32), ("scol", 4, F32), ("c0t", 4 * P, BF), ("p0", 16, F32), ("junk", 128, BF), ("b511", 4, F32),
-        ("x0", 4, F32), ("x1", 4, F32), ("x2", 4, F32), ("x3", 4, F32)):
+        ("one", 512, BF), ("zt", 512, BF), ("i16", K, BF), ("i128", 128, BF), ("i192", K, BF), ("i4", 4, BF), ("idt", 128, BF), ("et", 2048, BF),
+        ("ni", 4, I32), ("nl", 4, I32), ("nf", 4, F32), ("nlf", 4, F32), ("nx", 4, F32), ("nrept", 1024, BF), ("dlt", 512, BF), ("trit", 1024, BF), ("shc", 20, BF),
+        ("kw", 16, F32), ("kwz", 16, F32), ("jv", 3, I32), ("jw", 3, I32), ("jf", 3, F32), ("jwf", 3, F32), ("dl", 3, F32), ("dh0", 3, F32),
+        ("isa", 3, F32), ("nisa", 3, F32), ("isbm", 3, F32), ("basea", 3, F32), ("b511", 4, F32),
+        ("lk", K, F32), ("lk2", K, F32), ("cb", 1, F32), ("cn", 1, F32), ("cw", 1, F32), ("cth", 1, F32), ("nl1p", 1, F32)):
+    _CONST.append(_n)
     _buf(_n, _w, _t)
-for _n, _w in (("ur", 128), ("q0", P), ("wq", 256), ("oneq", 128), ("zq", 128), ("nrep", 256), ("eq", 512), ("c0q", P), ("fin", K)):
+for _n, _w, _t in (
+        ("ut", 4, BF), ("urt", 512, BF), ("nurt", 512, BF), ("grt", 4 * P, BF), ("wt", 1024, BF),
+        ("srow", P, F32), ("scol", 4, F32), ("c0t", 4 * P, BF), ("p0", 16, F32), ("junk", 128, BF), ("junk2", 2 * K, BF),
+        ("x0", 4, F32), ("x1", 4, F32), ("x2", 4, F32), ("x3", 4, F32), ("rk0", 4, F32), ("rc0", 4, F32), ("sc", K, F32), ("off0", 12, U16),
+        ("rtt", 512, BF), ("r2", 3, F32), ("h2", 3, F32), ("l2", 3, F32), ("pj", 3, F32), ("pjt", 512, BF), ("rc1", 4, F32),
+        ("ordt", 4 * 384, BF), ("nnc", 3, F32), ("xt", 512, BF), ("ntk", 3, F32), ("ntk2", 3, F32), ("plc", 3, F32), ("nbt", 4 * 132, BF), ("nbw", K, F32), ("yb", O * K, F32)):
+    _buf(_n, _w, _t)
+for _n, _w in (("ur", 128), ("nur", 128), ("q0", P), ("wq", 256), ("oneq", 128), ("zq", 128), ("nrep", 256), ("dlq", 128), ("eq", 512), ("triq", 256), ("c0q", P),
+               ("rtq", 128), ("pjq", 128), ("ordq", 384), ("xq", 128), ("nbq", 132), ("fin", K)):
     _mx(_n, _w)
-for _s in "012":
-    for _n, _w, _t in (("ri", 4, I32), ("hli", 8, I32), ("hl", 8, F32), ("lt", 640, BF), ("off", 16, U16)):
-        _buf(_n + _s, _w, _t)
-    _mx("lq" + _s, 288)
 for _s in "01":
     for _n, _w, _t in (
-            ("ta", 8, F32), ("in_a", 4, F32), ("h16", 4, F32), ("h16b", 4, F32), ("sla", 4, F32), ("slat", 4, F32), ("tbt", 512, BF), ("tb", 8, F32),
-            ("slb", 4, F32), ("slbt", 4, F32), ("in_b", 4, F32), ("sh", 4, F32), ("at", 640, BF), ("off1", 16, U16), ("ub", 16, F32), ("ub2", 16, F32), ("offb", 16, U16),
-            ("ot", 4 * 384, BF), ("o2t", 1024, BF), ("sht", 4 * 264, BF), ("mrow", K, F32), ("nr", 384, BF),
-            ("nc", 3, F32), ("nl1", 3, F32), ("nh1", 3, F32), ("fl", 3, F32), ("fa", 3, F32), ("fo", 3, F32), ("fk", 3, F32), ("bs", 3, F32), ("bs2", 3, F32), ("bs3", 3, F32), ("fb", 3, F32), ("fb2", 3, F32), ("dhr", 3, F32),
-            ("tau", 3 * K, BF), ("ht", 4 * K, BF), ("arow", K, F32), ("acol", 3, F32), ("v", 3 * K, BF), ("ct", 1024, BF), ("cj", 2 * K, BF), ("rs", 3, F32), ("rb", 3, F32)):
+            ("tbt", 512, BF), ("td", 8, F32), ("vt", 1024, BF), ("ot", 4 * 384, BF), ("scb", K, F32), ("off1", 12, U16), ("offb", 12, U16), ("ub", 12, F32), ("ub2", 12, F32),
+            ("shm", 4, F32), ("sht", 512, BF), ("nr", 384, BF), ("inf", 24, F32), ("nc", 3, F32), ("ft", 512, BF), ("fo", 3, F32), ("fm", 3, F32), ("dhr", 3, F32), ("dht", 512, BF),
+            ("tau", 4 * K, BF), ("ht", 4 * K, BF), ("arow", K, F32), ("acol", 3, F32), ("v", 3 * K, BF), ("ct", 1024, BF), ("rs", 3, F32), ("bs", 3, F32), ("rf", 3, F32),
+            ("st", 4 * K, BF), ("scs", K, F32), ("offs", 12, U16)):
         _buf(_n + _s, _w, _t)
-    for _n, _w in (("tq", 128), ("tl", 128), ("aq", 288), ("win", WE), ("ash", K), ("bun", 256), ("oq", 384), ("o2q", 256), ("shq", 264), ("cq", 256)):
+    for _n, _w in (("tq", 128), ("tl", 136), ("valq", 256), ("oq", 384), ("win", WE), ("ash", K), ("bp", 256), ("shq", 128), ("ftq", 128), ("dhq", 128), ("tauq", K), ("cq", 256), ("sq", K)):
         _mx(_n + _s, _w)
-for _n, _w, _t in (("pjt", 512, BF), ("tj", 3, F32), ("tj2", 3, F32), ("pj", 3, F32), ("pj0", 3, F32), ("rtt", 512, BF), ("rtm", 3, F32), ("nnc", 3, F32),
-                   ("trit", 4 * 384, BF), ("xt", 512, BF), ("rf", 3, F32), ("ntk", 3, F32), ("ntk2", 3, F32), ("nbt0", 512, BF), ("nbw", 32, F32), ("nbt", 32, F32), ("yb", O * K, F32)):
-    _buf(_n, _w, _t)
-for _n, _w in (("pjq", 128), ("nbq", 160), ("rtq", 128), ("triq", 384), ("xq", 128)):
-    _mx(_n, _w)
 ARR = ["tc0", "ts0", "wc0", "ws0", "tc1", "ts1", "wc1", "ws1"]
 SEMAPHORES = ["q_v", "q_s", "q_t", "q_g"] + ["d%d" % i for i in range(NSEM)] + ["l_" + a for a in ARR] + ["a_" + a for a in ARR]
 
@@ -68,7 +68,7 @@ def rank_program(g, core, T, topo):
     if rank is None:
         return
     ENG = {"v": g.vector, "s": g.scalar, "t": g.tensor, "g": g, "y": g.sync}
-    prog, acc, nd, sent = [], {}, [0], []
+    prog, nd, sent = [], [0], {}
 
     def v(name, a=0, b=None, s=1, p=0, e=128, cast=None):
         if name == "ps":
@@ -86,6 +86,9 @@ def rank_program(g, core, T, topo):
             return r
         return r.bitcast(dt.uint8 if cast == 8 else dt.uint32)
 
+    def width(x):
+        return len(range(x[1], x[2], x[3]))
+
     def overlap(x, y):
         if x[0] == "ps":
             f = lambda r: set(c // 512 for c in range(r[1], r[2], r[3] if r[3] == 512 else 1))
@@ -96,45 +99,32 @@ def rank_program(g, core, T, topo):
             return (x[1] - y[1]) % x[3] == 0
         return True
 
-    def rec(q, fn, reads, writes, kind="c", sem=None, amount=0, after=()):
-        i = len(prog)
-        deps = set(after)
-        for regs, w in ((reads, False), (writes, True)):
-            for x in regs:
-                for (y, yw, j) in acc.get(x[0], ()):
-                    if not overlap(x, y):
-                        continue
-                    if prog[j]["q"] == q and prog[j]["kind"] == "c" and kind == "c":
-                        if q == "t" and x[0] == "ps":
-                            continue
-                        if yw:
-                            deps.add(j)
-                    elif w or yw or x[0] == "ps":
-                        deps.add(j)
-        prog.append({"q": q, "fn": fn, "deps": deps, "kind": kind, "sem": sem, "amount": amount})
-        for x in reads:
-            acc.setdefault(x[0], []).append((x, False, i))
-        for x in writes:
-            acc.setdefault(x[0], []).append((x, True, i))
-        return i
+    def rec(q, fn, reads, writes, cost, kind="c", sem=None, amount=0, after=()):
+        prog.append({"q": q, "fn": fn, "reads": reads, "writes": writes, "cost": cost, "kind": kind, "sem": sem, "amount": amount, "after": list(after)})
+        return len(prog) - 1
 
     tens = lambda *xs: [x for x in xs if isinstance(x, tuple)]
+    short = lambda x: x[0][1:] in (BF, U16) or x[0] in ("ut", "urt", "nurt", "grt", "wt")
+
+    def easy(*xs):
+        return 0.83 * max(64, width(xs[0]) * (0.5 if all(short(x) for x in xs) else 1))
 
     def ts(out, in0, s1, op0, s2=None, op1=None):
         if op1 is None:
             fn = lambda: g.vector.tensor_scalar(out=ap(out), in0=ap(in0), scalar1=ap(s1), scalar2=None, op0=op0)
         else:
             fn = lambda: g.vector.tensor_scalar(out=ap(out), in0=ap(in0), scalar1=ap(s1), scalar2=ap(s2), op0=op0, op1=op1)
-        return rec("v", fn, tens(in0, s1, s2), [out])
+        return rec("v", fn, tens(in0, s1, s2), [out], easy(out, in0))
 
     def tt(out, a, b, op):
-        rec("v", lambda: g.vector.tensor_tensor(out=ap(out), in0=ap(a), in1=ap(b), op=op), [a, b], [out])
+        f = 1 if "ps" in (a[0], b[0]) else 2
+        rec("v", lambda: g.vector.tensor_tensor(out=ap(out), in0=ap(a), in1=ap(b), op=op), [a, b], [out], 0.83 * max(64, f * width(out)))
 
     def cp(out, a):
-        rec("v", lambda: g.vector.tensor_copy(ap(out), ap(a)), [a], [out])
+        rec("v", lambda: g.vector.tensor_copy(ap(out), ap(a)), [a], [out], easy(out, a))
 
     def fill(out, c=0.0):
-        rec("v", lambda: g.vector.memset(ap(out), c), [], [out])
+        rec("v", lambda: g.vector.memset(ap(out), c), [], [out], easy(out))
 
     def act(out, a, func, bias=None, scale=None, accum=None):
         kw = {}
@@ -144,30 +134,31 @@ def rank_program(g, core, T, topo):
             kw["scale"] = scale
         if accum is not None:
             kw["accum_out"] = accum
-        rec("s", lambda: g.scalar.activation(ap(out), ap(a), func, **{k: ap(x) for k, x in kw.items()}), tens(a, bias, scale), tens(out, accum))
+        rec("s", lambda: g.scalar.activation(ap(out), ap(a), func, **{k: ap(x) for k, x in kw.items()}), tens(a, bias, scale), tens(out, accum), 0.83 * max(64, width(out)) + (20 if accum else 0))
 
     def zero(out):
-        act(out, v("zt", 0, len(range(out[1], out[2], out[3]))), AF.Copy)
+        act(out, v("zt", 0, width(out)), AF.Copy)
 
     def pl(x):
         return (x[0] + "s",) + x[1:6] + (None,)
 
     def quant(out, a):
-        return rec("v", lambda: g.vector.quantize_mx(ap(out), ap(pl(out)), ap(a)), [a], [out, pl(out)])
+        return rec("v", lambda: g.vector.quantize_mx(ap(out), ap(pl(out)), ap(a)), [a], [out, pl(out)], 12 + 0.22 * width(a))
 
     def mm(bank, l, r, start=True, stop=True):
-        out = v("ps", 512 * bank, 512 * bank + r[2] - r[1])
-        rec("t", lambda: g.tensor.matmul_mx(ap(out), ap(l), ap(pl(l)), ap(r), ap(pl(r)), start, stop), [l, pl(l), r, pl(r)], [out])
+        out = v("ps", 512 * bank, 512 * bank + width(r))
+        rec("t", lambda: g.tensor.matmul_mx(ap(out), ap(l), ap(pl(l)), ap(r), ap(pl(r)), start, stop), [l, pl(l), r, pl(r)], [out], 1.2 * (width(r) + 16))
 
     def pick(out, win, off):
         c = lambda x: x[:6] + (32,)
-        rec("v", lambda: g.vector.tensor_copy(ap(c(out)), ap(c(win)).indirect(ap(off))), [win, off], [out])
-        rec("s", lambda: g.scalar.activation(ap(pl(out)), ap(pl(win)).indirect(ap(off)), AF.Copy), [pl(win), off], [pl(out)])
+        n = 1.3 * width(out)
+        rec("v", lambda: g.vector.tensor_copy(ap(c(out)), ap(c(win)).indirect(ap(off))), [win, off], [out], 50 + n)
+        rec("s", lambda: g.scalar.activation(ap(pl(out)), ap(pl(win)).indirect(ap(off)), AF.Copy), [pl(win), off], [pl(out)], 65 + n)
 
     def dma(q, out, in_, reads, writes, after=()):
         n = nd[0]
         nd[0] += 1
-        rec(q, lambda: ENG[q].dma_start(out() if not isinstance(out, tuple) else ap(out), in_() if not isinstance(in_, tuple) else ap(in_)), reads, writes, "d", "d%d" % n, 16, after)
+        rec(q, lambda: ENG[q].dma_start(out() if not isinstance(out, tuple) else ap(out), in_() if not isinstance(in_, tuple) else ap(in_)), reads, writes, 60, "d", "d%d" % n, 16, after)
 
     def mxcopy(q, out, in_, after=()):
         c = lambda x: x[:6] + (8,)
@@ -178,8 +169,8 @@ def rank_program(g, core, T, topo):
         dst = T.cores[peer]
         rid, pid, _ = topo.addr(dst)
         m, n = topo.mask(core, dst), len(topo.engines(core, dst))
-        rec("g", lambda: g.remote_dma(ap(out), ap(in_), T.sem["a_" + key], T.sem["l_" + key], pid, rid, m), [in_], [], "r", "l_" + key, n)
-        sent.append((key, out, len(topo.engines(dst, core))))
+        i = rec("g", lambda: g.remote_dma(ap(out), ap(in_), T.sem["a_" + key], T.sem["l_" + key], pid, rid, m), [in_], [], 120, "r", "l_" + key, n)
+        sent[key] = (i, out, len(topo.engines(dst, core)))
 
     def sendmx(peer, out, in_, kc, ks):
         c = lambda x: x[:6] + (8,)
@@ -187,9 +178,8 @@ def rank_program(g, core, T, topo):
         send(peer, pl(out), pl(in_), ks)
 
     def arrive(key):
-        for k, out, n in sent:
-            if k == key:
-                rec(None, None, [], [out], "a", "a_" + key, n)
+        i, out, n = sent[key]
+        rec(None, None, [], [out], 0, "a", "a_" + key, n, [i])
 
     ps = lambda bank, a, b: v("ps", 512 * bank + a, 512 * bank + b)
     pst = lambda bank, n, c: v("ps", 512 * bank + c, 512 * (bank + n - 1) + c + 1, 512)
@@ -198,60 +188,92 @@ def rank_program(g, core, T, topo):
 
     def iota(out, pattern, base, cm, flag=True):
         kw = {"allow_small_or_imprecise_dtypes": True} if flag else {}
-        rec("g", lambda: g.iota(ap(out), pattern, base, cm, **kw), [], [out])
+        rec("g", lambda: g.iota(ap(out), pattern, base, cm, **kw), [], [out], 130 + 1.66 * width(out))
+
+    def select(out, in_, pattern, op, fillv, base, cm):
+        rec("g", lambda: g.affine_select(ap(out), ap(in_), pattern, op, fillv, base, cm), [in_], [out], 170 + 1.66 * width(out))
 
     dma("y", v("ut"), lambda: T.u[:, 0:4], [], [v("ut")])
     for c in range(4):
         x = v("grt", 512 * c, 512 * c + 512)
         dma("sy"[c % 2], x, (lambda c=c: T.gr[:, 512 * c:512 * c + 512]), [], [x])
 
-    iota(v("ni"), [[128, 4]], 0, 1, False)
-    iota(v("i16"), [[0, 8], [1, 16]], 0, 0)
-    fill(v("zt"))
     fill(v("one"), 1.0)
+    fill(v("zt"))
+    iota(v("ni"), [[128, 4]], 0, 1, False)
+    iota(v("i16"), [[0, 12], [1, 16]], 0, 0)
+    iota(v("i192"), [[1, K]], 0, 0)
+    iota(v("jv"), [[128, 3]], 0, 1, False)
+    iota(v("jw"), [[128, 3]], 16, 1, False)
+    iota(v("kw"), [[16, 16]], 0, 0)
+    iota(v("i128"), [[1, 128]], 0, 0)
+    iota(v("i4"), [[1, 4]], -2, 0)
     ts(v("nl"), v("ni"), 15, OP.bitwise_and)
     cp(v("nf"), v("ni"))
     cp(v("nlf"), v("nl"))
     ts(v("b511"), v("nf"), -1.0, OP.mult, 511.0, OP.add)
     tt(v("nx"), v("nf"), v("nlf"), OP.subtract)
     ts(v("nx"), v("nx"), -256.0, OP.add)
-    rec("g", lambda: g.affine_select(ap(v("idt")), ap(one), [[-1, 128]], OP.is_equal, 0.0, 0, 1), [one], [v("idt")])
-    for b in range(4):
-        zero(v("et", 512 * b, 512 * b + 512))
-        act(v("et", 512 * b + b, 512 * b + 512, 4), v("idt"), AF.Copy)
-    iota(v("i192"), [[1, K]], 0, 0)
-    iota(v("jv"), [[128, 3]], 0, 1, False)
-    iota(v("jw"), [[128, 3]], WA + 16, 1, False)
-    iota(v("kw"), [[16, 16]], 0, 0)
-    iota(v("i128"), [[1, 128]], 0, 0)
-    iota(v("i4"), [[1, 4]], -2, 0)
-    iota(v("sht0", 512, 1056), [[0, 544]], 0, 0)
     for t in (1, 2, 3):
         fill(v("c0t", t, 512 * t, 4))
     fill(v("p0"))
     quant(v("oneq"), v("one"))
-    quant(v("zq"), v("zt"))
-    quant(v("lq0", 160, 288), v("zt"))
-    fill(v("hli1"))
-    fill(v("hli2"))
-    fill(v("nbw"))
-    ts(v("kw"), v("kw"), v("nlf", 0, 1), OP.add)
-    ts(v("kwb"), v("kw"), float(WB), OP.add)
+    nlf = v("nlf", 0, 1)
+    ts(v("lk"), v("i16"), nlf, OP.is_equal, -1.0e6, OP.mult)
+    ts(v("nl1p"), nlf, 1.0, OP.add)
+    ts(v("lk2"), v("i16"), v("nl1p"), OP.is_equal, 4096.0, OP.mult)
+    tt(v("lk"), v("lk"), v("lk2"), OP.add)
+    ts(v("cb"), nlf, 14.5, OP.is_lt, -4096.0, OP.mult)
+    ts(v("cn"), v("cb"), 256.0, OP.add)
+    ts(v("cw"), v("cb"), float(MID), OP.add)
+    ts(v("cth"), v("cb"), -1.0, OP.mult, K - 0.5, OP.add)
+    ts(v("kw"), v("kw"), nlf, OP.add)
+    ts(v("kwz"), v("kw"), -float(WZ), OP.add)
     cp(v("jf"), v("jv"))
     ts(v("jw"), v("jw"), 31, OP.bitwise_and)
     cp(v("jwf"), v("jw"))
     ts(v("dl"), v("jwf"), -16.0, OP.add)
     tt(v("dh0"), v("jf"), v("dl"), OP.subtract)
-    ts(v("dh0"), v("dh0"), float(WA - 320), OP.add)
-    ts(v("isa"), v("jf"), K - 0.5, OP.is_lt)
+    ts(v("dh0"), v("dh0"), -float(MID), OP.add)
+    ts(v("isa"), v("jf"), K - 0.5, OP.is_gt)
     ts(v("nisa"), v("isa"), -1.0, OP.mult)
-    ts(v("basea"), v("jf"), float(K), OP.add)
-    tt(v("basea"), v("basea"), v("isa"), OP.mult)
-    fill(v("tbt0"))
-    fill(v("o2t0", 4 * K, 1024))
+    tt(v("basea"), v("jf"), v("isa"), OP.mult)
+    ts(v("isbm"), v("jf"), K - 0.5, OP.is_lt, float(WM), OP.mult)
+    select(v("trit", 1, 1024, 4), v("one", 0, 256), [[1, 256]], OP.is_gt, 0.0, 0, -1)
+    select(v("trit", 2, 1024, 4), v("one", 0, 256), [[1, 256]], OP.is_gt, 0.0, -128, -1)
+    select(v("trit", 1, 1024, 4), v("trit", 1, 1024, 4), [[1, 256]], OP.not_equal, -960.0, 0, -1)
+    select(v("trit", 2, 1024, 4), v("trit", 2, 1024, 4), [[1, 256]], OP.not_equal, -960.0, -128, -1)
+    zero(v("trit", 0, 1024, 4))
+    zero(v("trit", 3, 1024, 4))
+    select(v("idt"), one, [[-1, 128]], OP.is_equal, 0.0, 0, 1)
+    for b in range(4):
+        zero(v("et", 512 * b, 512 * b + 512))
+        act(v("et", 512 * b + b, 512 * b + 512, 4), v("idt"), AF.Copy)
+    for t in range(4):
+        act(v("nrept", t, 512, 4), one, AF.Identity, scale=v("nx", t, t + 1))
+        act(v("nrept", 512 + t, 1024, 4), one, AF.Identity, scale=v("nlf", t, t + 1))
+    zero(v("dlt", 3, 512, 4))
+    for t in range(3):
+        act(v("dlt", t, 512, 4), one, AF.Identity, scale=v("dl", t, t + 1))
+    act(v("shc", 0, 4), v("nx"), AF.Copy)
+    act(v("shc", 4, 8), v("nlf"), AF.Copy)
+    zero(v("shc", 8, 12))
+    iota(v("shc", 12, 16), [[1, 4]], -2, 0)
+    act(v("shc", 16, 20), v("one", 0, 4), AF.Identity, scale=v("nx", 2, 3))
+    for name, a, b, s in (("tbt0", 0, 512, 1), ("tbt1", 0, 512, 1), ("sht0", 0, 512, 1), ("sht1", 0, 512, 1), ("ft0", 0, 512, 1), ("ft1", 0, 512, 1),
+                          ("dht0", 3, 512, 4), ("dht1", 3, 512, 4), ("tau0", 3, 4 * K, 4), ("tau1", 3, 4 * K, 4), ("st0", 3, 4 * K, 4), ("st1", 3, 4 * K, 4),
+                          ("ct0", 3, 4 * K, 4), ("ct1", 3, 4 * K, 4), ("ct0", 4 * K, 1024, 1), ("ct1", 4 * K, 1024, 1),
+                          ("rtt", 0, 512, 1), ("pjt", 3, 512, 4), ("ordt", 3, 4 * 384, 4), ("xt", 0, 512, 1), ("nbt", 0, 264, 1), ("nbt", 264, 528, 1), ("rf0", 0, 1, 1), ("rf1", 0, 1, 1)):
+        zero(v(name, a, b, s))
+    for s in "01":
+        act(v("sht" + s, 0, 20), v("shc"), AF.Copy)
+    quant(v("zq"), v("zt"))
+
     for t in range(4):
         ts(v("urt", t, 512, 4), one, v("ut", t, t + 1), OP.mult)
     quant(v("ur"), v("urt"))
+    act(v("nurt"), v("urt"), AF.Copy, scale=-1.0)
+    quant(v("nur"), v("nurt"))
 
     def sizes(c):
         qc = v("q0", 128 * c, 128 * c + 128)
@@ -261,311 +283,318 @@ def rank_program(g, core, T, topo):
         act(v("scol", c, c + 1), ps(4 + c, 0, 1), AF.Abs)
         act(v("srow", 128 * c, 128 * c + 128), ps(c, 0, 128), AF.Abs)
 
-    def upper(blk):
-        rec("g", lambda: g.affine_select(ap(blk), ap(blk), [[1, 128]], OP.is_gt, 0.0, 0, -1), [blk], [blk])
-
     def compare(c):
         for t in [c] + list(range(c)):
             blk = v("c0t", 512 * c + t, 512 * c + 512, 4)
             ts(blk, v("srow", 128 * c, 128 * c + 128), v("scol", t, t + 1), OP.is_le)
             if t == c:
-                upper(blk)
+                select(blk, blk, [[1, 128]], OP.is_gt, 0.0, 0, -1)
 
     def count(c):
         for t in range(c + 1):
             act(v("junk"), v("c0t", 512 * c + t, 512 * c + 512, 4), AF.Copy, accum=v("p0", 4 * c + t, 4 * c + t + 1))
         quant(v("c0q", 128 * c, 128 * c + 128), v("c0t", 512 * c, 512 * c + 512))
         mm(c, v("c0q", 128 * c, 128 * c + 128), v("oneq"))
-
-    def countx(c):
         tt(v("x%d" % c), v("b511") if c == 0 else v("x%d" % (c - 1)), v("p0", 4 * c, 4 * c + 4), OP.subtract)
 
-    sizes(0)
-    sizes(1)
-    compare(0)
-    sizes(2)
-    compare(1)
-    sizes(3)
-    compare(2)
-    count(0)
-    compare(3)
-    count(1)
-    count(2)
-    countx(0)
-    countx(1)
-    count(3)
-    countx(2)
-    countx(3)
-    tt(v("ri0"), pst(0, 4, 0), v("x3"), OP.add)
+    for c in range(4):
+        sizes(c)
+    for c in range(4):
+        compare(c)
+    for c in range(4):
+        count(c)
+    tt(v("rk0"), pst(0, 4, 0), v("x3"), OP.add)
 
-    def hilo(s, n):
-        ts(v("hli" + s, 0, n), v("ri" + s, 0, n), 4, OP.arith_shift_right)
-        ts(v("hli" + s, 4, 4 + n), v("ri" + s, 0, n), 15, OP.bitwise_and)
-        cp(v("hl" + s), v("hli" + s))
-
-    def listtile(tile, n, hi, lo, values):
-        for t in range(n):
-            ts(v(tile, t, 512, 4), v("i16"), lo(t), OP.is_equal)
-        for k, val in enumerate(values):
-            for t in range(n):
-                ts(v(tile, 512 + 64 * k + t, 576 + 64 * k, 4), v("i16", 0, 16), hi(t), OP.is_equal, val(t), OP.mult)
-
-    def listmm(bank, q):
-        mm(bank, v(q, 0, 128), v(q, 128, 256), True, False)
-        mm(bank, v(q, 0, 128), v(q, 144, 272), False, True)
-
-    hilo("0", 4)
-    listtile("lt0", 4, col("hl0"), col("hl0", 4), [col("nx"), col("nlf")])
-    quant(v("lq0", 0, 160), v("lt0"))
-    listmm(4, "lq0")
-    ts(v("ta0", 0, 4), v("hl0", 0, 4), 12.0, OP.min)
-    cp(v("ta0", 4, 8), v("hl0", 4, 8))
-    cp(v("tbt0", 0, 8), v("ta0"))
-    ts(v("off0"), ps(4, 0, 16), 256.0, OP.add)
+    ts(v("rc0"), v("rk0"), float(K), OP.min)
+    ts(v("tbt0", 0, 16, 4), v("rc0"), ROUND16, OP.add, -ROUND16, OP.add)
+    tt(v("tbt0", 16, 32, 4), v("rc0"), v("tbt0", 0, 16, 4), OP.subtract)
     mark = quant(v("tq0"), v("tbt0"))
-    pick(v("win0", WA, WB), v("q0"), v("off0", 0, 12))
-    peer = rank ^ 1
-    sendmx(peer, v("tl0", 0, 2), v("tq0", 0, 2), "tc0", "ts0")
-    sendmx(peer, v("win0", WB, WY), v("win0", WA, WB), "wc0", "ws0")
-    for s in "01":
-        mxcopy("y", v("tl" + s, 2, 128), v("zq", 2, 128), [mark])
-        mxcopy("y", v("win" + s, WZ, WA), v("zq", 0, 32), [mark])
-        mxcopy("y", v("win" + s, WY, WM), v("zq", 0, 64), [mark])
-    dma("y", v("wt"), lambda: T.w[:, :], [], [v("wt")], [mark])
+    sendmx(rank ^ 1, v("tl0", 0, 8), v("tq0", 0, 8), "tc0", "ts0")
 
-    def own(s):
-        ha, la = v("ta" + s, 0, 4), v("ta" + s, 4, 8)
-        ts(v("in_a" + s), ha, 11.5, OP.is_lt)
-        ts(v("h16" + s), ha, 16.0, OP.mult, float(WA), OP.add)
-        ts(v("slat" + s), ha, 16.0, OP.mult)
-        tt(v("h16b" + s), v("h16" + s), v("in_a" + s), OP.mult)
-        tt(v("sla" + s), v("slat" + s), la, OP.add)
+    def listof(bank, digits, onehot, scan, off, shift):
+        mm(bank, digits[0], onehot, True, False)
+        mm(bank, digits[1], onehot, False, True)
+        row = ps(bank, 0, K)
+        rec("v", lambda: g.vector.tensor_tensor_scan(ap(scan), ap(v("lk")), ap(row), 0.0, OP.add, OP.max), [v("lk"), row], [scan], 0.83 * K)
+        last = (scan[0], scan[1] + 15, scan[2], 16) + scan[4:]
+        ts(off, last, shift, OP.add)
+        return last
+
+    two = lambda name: (v(name, 0, 128), v(name, 128, 256))
+
+    def place_numbers(s, scalar, a):
         for t in range(4):
-            ts(v("ot" + s, t, 4 * K, 4), v("i192"), v("sla" + s, t, t + 1), OP.is_equal)
-            ts(v("o2t" + s, t, 4 * K, 4), v("i192"), v("sla" + s, t, t + 1), OP.is_gt)
-        quant(v("oq" + s, 0, K), v("ot" + s, 0, 4 * K))
-        quant(v("o2q" + s), v("o2t" + s))
+            ts(v("ot" + s, 4 * a + t, 4 * (a + K), 4), v("i192"), scalar(t), OP.is_equal)
+        quant(v("oq" + s, a, a + K), v("ot" + s, 4 * a, 4 * (a + K)))
+
+    quant(v("nrep"), v("nrept"))
+    place_numbers("0", col("rk0"), K)
+    listof(4, two("nrep"), v("oq0", K, 2 * K), v("sc"), v("off0"), v("cn"))
+    pick(v("win0", WA, WA + K), v("q0"), v("off0"))
+    sendmx(rank ^ 1, v("win0", WB, WB + K), v("win0", WA, WA + K), "wc0", "ws0")
+    for s in "01":
+        mxcopy("y", v("tl" + s, 8, 136), v("zq"), [mark])
+        mxcopy("y", v("win" + s, WZ, WM), v("zq", 0, WM - WZ), [mark])
+        mxcopy("y", v("win" + s, WY, WE), v("zq", 0, WE - WY), [mark])
+        mxcopy("y", v("bp" + s, K, 256), v("zq", 0, 256 - K), [mark])
+    dma("y", v("wt"), lambda: T.w[:, :], [], [v("wt")], [mark])
+    quant(v("eq"), v("et"))
+    quant(v("triq"), v("trit"))
+    quant(v("dlq"), v("dlt"))
+
+    eb = lambda b: v("eq", 128 * b, 128 * b + 128)
 
     def numbers(s, bank, a):
         mm(bank, v("nrep", 0, 128), v("oq" + s, a, a + K), True, False)
         mm(bank, v("nrep", 128, 256), v("oq" + s, a, a + K), False, True)
         act(v("nr" + s, a, a + K), ps(bank, 0, K), AF.Copy)
 
+    def own(s):
+        act(v("td" + s), v("tbt" + s, 0, 32, 4), AF.Copy)
+        for t in range(4):
+            act(v("vt" + s, t, 512, 4), one, AF.Identity, scale=v("td" + s, t, t + 1))
+            act(v("vt" + s, 512 + t, 1024, 4), one, AF.Identity, scale=v("td" + s, 4 + t, 5 + t))
+        quant(v("valq" + s), v("vt" + s))
+
     def before(s, last):
+        w = "win" + s
         arrive("tc" + s)
         arrive("ts" + s)
+        mm(6, eb(0), v("tl" + s, 0, 128), True, False)
+        mm(6, eb(0), v("tl" + s, 4, 132), False, True)
+        place_numbers(s, lambda t: ps(6, t, t + 1), 0)
+        scan = listof(7, two("valq" + s), v("oq" + s, 0, K), v("scb" + s), v("off1" + s), v("cb"))
+        pick(v("ash" + s), v(w, WA, WM), v("off1" + s))
         for b in range(4):
-            mm(b, v("eq", 128 * b, 128 * b + 128), v("tl" + s))
-        hb = v("tb" + s, 0, 4)
-        listtile("at" + s, 4, lambda t: ps(t, 0, 1), lambda t: ps(t, 1, 2), [col("h16b" + s), col("ta" + s, 4)])
-        quant(v("aq" + s, 0, 160), v("at" + s))
-        cp(hb, pst(0, 4, 0))
-        cp(v("tb" + s, 4, 8), pst(0, 4, 1))
-        listmm(7, "aq" + s)
-        ts(v("in_b" + s), hb, 11.5, OP.is_lt)
-        ts(v("slbt" + s), hb, 16.0, OP.mult)
-        tt(v("sh" + s), v("in_a" + s), v("in_b" + s), OP.mult)
-        tt(v("slb" + s), v("slbt" + s), v("tb" + s, 4, 8), OP.add)
-        cp(v("sht" + s, 528, 532), v("sh" + s))
-        for t in range(4):
-            act(v("sht" + s, t, 512, 4), one, AF.Identity, scale=v("sh" + s, t, t + 1))
-        cp(v("off1" + s), ps(7, 0, 16))
-        ts(v("ub" + s), ps(7, 0, 16), WA - 0.5, OP.is_lt)
-        pick(v("ash" + s), v("win" + s, 0, WB), v("off1" + s, 0, 12))
-        for b in range(4):
-            mm(b, v("eq", 128 * b, 128 * b + 128), v("ash" + s), True, False)
-        tt(v("ub2" + s), v("ub" + s), v("kwb"), OP.mult)
-        for t in range(4):
-            ts(v("ot" + s, 4 * K + t, 8 * K, 4), v("i192"), v("slb" + s, t, t + 1), OP.is_equal)
-        cp(v("offb" + s), v("ub2" + s))
-        quant(v("oq" + s, K, 2 * K), v("ot" + s, 4 * K, 8 * K))
+            mm(b, eb(b), v("ash" + s), True, False)
+        ts(v("ub" + s), scan, v("cth"), OP.is_lt)
+        tt(v("ub2" + s), v("ub" + s), v("kwz", 0, 12), OP.mult)
+        ts(v("offb" + s), v("ub2" + s), float(WZ), OP.add)
+        tt(v("shm" + s), v("rc" + s), ps(6, 0, 4), OP.max)
+        ts(v("sht" + s, 8, 12), v("shm" + s), K - 0.5, OP.is_lt)
         quant(v("shq" + s), v("sht" + s))
-        mm(7, v("shq" + s, 0, 128), v("oq" + s, K, 2 * K))
-        act(v("mrow" + s), ps(7, 0, K), AF.Copy)
+        numbers(s, 5, 0)
         if last:
-            numbers(s, 6, K)
+            numbers(s, 4, K)
         for t in range(3):
-            mm(4 + t, v("oq" + s, 128 * t, 128 * t + 128), v("shq" + s, 128, 256), True, t == 2)
-            if t < 2:
-                mm(4 + t, v("o2q" + s, 128 * t, 128 * t + 128), v("shq" + s, 130, 258), False, True)
-        act(v("nh1" + s), pst(4, 3, 0), AF.Copy)
-        act(v("nl1" + s), pst(4, 3, 1), AF.Copy)
-        act(v("fl" + s), pst(4, 3, 4), AF.Copy)
-        act(v("bs" + s), pst(4, 3, 2), AF.Copy)
-        if last:
-            mxcopy("y", v("nbq", 128, 160), v("zq", 0, 32))
-        else:
-            act(v("tj"), pst(4, 3, 14), AF.Copy)
-        mxcopy("y", v("bun" + s, 0, 64), v("win" + s, WA + 128, WB))
-
-    def merge(s, last):
-        w, bun = "win" + s, "bun" + s
-        arrive("wc" + s)
-        arrive("ws" + s)
-        for b in range(4):
-            mm(b, v("eq", 128 * b, 128 * b + 128), v(w, WB, WY), False, True)
-        pick(v(bun, 64, 256), v(w, 0, WY), v("offb" + s, 0, 12))
-        tt(v("nc" + s), v("nh1" + s), v("nl1" + s), OP.add)
+            mm(4 + t, v("oq" + s, 128 * t, 128 * t + 128), v("shq" + s))
+            act(v("inf" + s, 8 * t, 8 * t + 8), ps(4 + t, 0, 8), AF.Copy)
+        inf = lambda k: v("inf" + s, k, 24, 8)
+        ts_a = v("ft" + s, 0, 3)
+        tt(v("nc" + s), inf(0), inf(1), OP.add)
+        tt(ts_a, inf(2), v("isa"), OP.mult)
+        ts(v("fo" + s), ts_a, 2.0, OP.mult, -0.5, OP.add)
+        quant(v("ftq" + s), v("ft" + s))
+        mm(4, v("triq", 0, 128), v("ftq" + s))
+        mm(5, v("triq", 128, 256), v("ftq" + s))
+        tt(v("bs" + s, 1, 3), v("basea", 1, 3), pst(4, 2, 0), OP.subtract)
+        for t in range(3):
+            ts(v("tau" + s, t, 4 * K, 4), v("nr" + s, 0, K), v("nc" + s, t, t + 1), OP.is_le, v("fo" + s, t, t + 1), OP.add)
+        quant(v("tauq" + s), v("tau" + s))
+        for t in range(3):
+            mm(4 + t, eb(t), v("tauq" + s))
+        tt(v("fm" + s), inf(2), v("isbm"), OP.mult)
+        tt(v("dhr" + s), v("fm" + s), v("dh0"), OP.add)
+        for t in range(3):
+            act(v("dht" + s, t, 512, 4), one, AF.Identity, scale=v("dhr" + s, t, t + 1))
+        quant(v("dhq" + s), v("dht" + s))
         if last:
             ts(v("nnc"), v("nc" + s), -1.0, OP.mult)
             for t in range(3):
-                act(v("trit", t, 4 * 384, 4), v("nr1"), AF.Sign, bias=v("nnc", t, t + 1))
-            zero(v("nbt0"))
-        for b in range(4):
-            tt(v("ht" + s, b, 4 * K, 4), ps(b, 0, K), v("mrow" + s), OP.mult)
-        mm(7, v("ur"), v(bun, 64, 256), True, False)
-        mm(0, v(w, WA, WA + 128), v("ur"))
-        act(v("acol" + s, 0, 1), ps(0, 0, 1), AF.Abs)
-        if not last:
-            numbers(s, 3, K)
-        quant(v(w, WM, WE), v("ht" + s))
-        mm(7, v("ur"), v(w, WM, WE), False, True)
-        mm(1, v(bun, 0, 128), v("ur"), True, False)
-        mm(1, v(w, WY, WY + 128), v("ur"), False, True)
-        mm(2, v(bun, 128, 256), v("ur"), True, False)
-        mm(2, v(w, WY + 128, WE), v("ur"), False, True)
-        tt(v("fa" + s), v("fl" + s), v("isa"), OP.mult)
-        ts(v("fo" + s), v("fa" + s), 2.0, OP.mult, -0.5, OP.add)
-        for t in range(3):
-            ts(v("tau" + s, K * t, K * t + K), v("nr" + s, K, 2 * K), v("nc" + s, t, t + 1), OP.is_le, v("fo" + s, t, t + 1), OP.add)
-        ts(v("fk" + s), v("fa" + s), 1000.0, OP.mult)
-        tt(v("fb" + s), v("fl" + s), v("fa" + s), OP.subtract)
-        tt(v("bs3" + s), v("basea"), v("bs" + s), OP.subtract)
-        tt(v("bs2" + s), v("fk" + s), v("bs3" + s), OP.add)
-        ts(v("fb2" + s), v("fb" + s), float(WM - WB), OP.mult)
-        tt(v("dhr" + s), v("fb2" + s), v("dh0"), OP.add)
-        if not last:
-            ts(v("tj2"), v("tj"), -128.0, OP.mult)
-            ts(v("pj0"), v("fa0"), -4096.0, OP.mult)
-            tt(v("tj2"), v("tj2"), v("nc0"), OP.add)
-            tt(v("pj"), v("tj2"), v("pj0"), OP.add)
-        act(v("arow" + s), ps(7, 0, K), AF.Abs)
-        act(v("acol" + s, 1, 3), pst(1, 2, 0), AF.Abs)
-        for t in range(3):
-            act(v("v" + s, K * t, K * t + K), v("arow" + s), AF.Sign, bias=v("acol" + s, t, t + 1), scale=-1.0)
-            tt(v("ct" + s, 256 + t, 1024, 4), v("v" + s, K * t, K * t + K), v("tau" + s, K * t, K * t + K), OP.is_gt)
-        for t in range(2):
-            act(v("cj" + s, K * t, K * t + K), v("ct" + s, 256 + t, 1024, 4), AF.Identity, scale=v("nisa", t, t + 1), accum=v("rs" + s, t, t + 1))
-        quant(v("cq" + s), v("ct" + s))
-        mm(5, v("cq" + s, 0, 128), v("oneq"))
-        mm(6, v("cq" + s, 128, 256), v("oneq"))
-        if not last:
+                act(v("ordt", t, 4 * 384, 4), v("nr" + s), AF.Sign, bias=v("nnc", t, t + 1))
+            quant(v("ordq"), v("ordt"))
+            act(v("nbt", 0, 3), inf(0), AF.Copy)
+            act(v("nbt", 8, 11), inf(1), AF.Copy)
+            quant(v("nbq"), v("nbt"))
+        else:
+            tt(v("pj"), inf(4), inf(1), OP.add)
             for t in range(3):
                 ts(v("pjt", t, 512, 4), v("i128"), v("pj", t, t + 1), OP.is_equal)
             quant(v("pjq"), v("pjt"))
-        tt(v("rb" + s, 0, 2), v("bs2" + s, 0, 2), v("rs" + s, 0, 2), OP.add)
-        cp(v("rb" + s, 2, 3), v("bs2" + s, 2, 3))
-        if last:
-            quant(v("triq"), v("trit"))
 
-    for t in range(4):
-        act(v("nrept", t, 512, 4), one, AF.Identity, scale=v("nx", t, t + 1))
-        act(v("nrept", 512 + t, 1024, 4), one, AF.Identity, scale=v("nlf", t, t + 1))
-    act(v("sht0", 512, 516), v("nx"), AF.Copy)
-    act(v("sht0", 516, 520), v("nlf"), AF.Copy)
-    zero(v("ct0", 3, 1024, 4))
-    zero(v("ct0", 0, 256))
-    zero(v("rtt"))
-    zero(v("pjt", 3, 512, 4))
-    zero(v("lt1", 3, 640, 4))
-    zero(v("tbt1"))
-    zero(v("o2t1", 4 * K, 1024))
-    quant(v("eq"), v("et"))
-    own("0")
-    quant(v("aq0", 160, 288), v("zt"))
-    quant(v("nrep"), v("nrept"))
-    for t in range(4):
-        fill(v("sht0", 568 + t, 569 + t), t - 2.0)
-    quant(v("lq1", 160, 288), v("zt"))
-    before("0", False)
-    merge("0", False)
+    def merge(s):
+        w, bp = "win" + s, "bp" + s
+        arrive("wc" + s)
+        arrive("ws" + s)
+        pick(v(bp, 0, K), v(w, 0, WM), v("offb" + s))
+        for b in range(4):
+            mm(b, eb(b), v(bp, 0, K), False, True)
+            out = v("ht" + s, b, 4 * K, 4)
+            if b % 2:
+                act(out, ps(b, 0, K), AF.Copy)
+            else:
+                cp(out, ps(b, 0, K))
+        quant(v(w, WM, WM + K), v("ht" + s))
+        ur, nur = v("ur"), v("nur")
+        mm(7, ur, v(w, 0, K), True, False)
+        mm(7, nur, v(bp, 0, K), False, False)
+        mm(7, ur, v(w, WM, WM + K), False, True)
+        for t in range(2):
+            mm(t, v(w, 128 * t, 128 * t + 128), ur, True, False)
+            mm(t, v(bp, 128 * t, 128 * t + 128), nur, False, False)
+            mm(t, v(w, WM + 128 * t, WM + 128 * t + 128), ur, False, True)
+        mm(2, v(w, 256, 384), ur)
+        act(v("acol" + s, 2, 3), ps(2, 0, 1), AF.Abs)
+        act(v("arow" + s), ps(7, 0, K), AF.Abs)
+        act(v("acol" + s, 0, 2), pst(0, 2, 0), AF.Abs)
+        for t in (2, 0, 1):
+            x = v("v" + s, K * t, K * t + K)
+            act(x, v("arow" + s), AF.Sign, bias=v("acol" + s, t, t + 1), scale=-1.0)
+            tt(v("ct" + s, t, 4 * K, 4), x, ps(4 + t, 0, K), OP.is_gt)
+        for t in (2, 1):
+            act(v("junk2", K * (t - 1), K * t), v("ct" + s, t, 4 * K, 4), AF.Identity, scale=v("nisa", t, t + 1), accum=v("rs" + s, t, t + 1))
+        quant(v("cq" + s), v("ct" + s))
+        mm(4, v("cq" + s, 0, 128), v("oneq"))
+        mm(5, v("cq" + s, 128, 256), v("oneq"))
+        tt(v("rf" + s, 1, 3), v("bs" + s, 1, 3), v("rs" + s, 1, 3), OP.add)
+        tt(v("rf" + s, 0, 2), pst(4, 2, 0), v("rf" + s, 0, 2), OP.add)
 
-    cp(v("ri1", 0, 1), v("rb0", 0, 1))
-    tt(v("ri1", 1, 3), pst(5, 2, 0), v("rb0", 1, 3), OP.add)
-    hilo("1", 3)
-    listtile("lt1", 3, col("hl1"), col("hl1", 4), [col("dhr0"), col("dl")])
-    quant(v("lq1", 0, 160), v("lt1"))
-    listmm(3, "lq1")
-    ts(v("rtm"), v("hl1", 0, 3), -12.0, OP.add, 0.0, OP.min)
-    for t in range(3):
-        ts(v("rtt", t, 16, 4), v("i4"), v("tj", t, t + 1), OP.is_equal, v("rtm", t, t + 1), OP.mult)
-        ts(v("rtt", 16 + t, 32, 4), v("i4"), v("tj", t, t + 1), OP.is_equal, v("hl1", 4 + t, 5 + t), OP.mult)
-    ts(v("off1"), ps(3, 0, 16), 320.0, OP.add)
-    quant(v("rtq"), v("rtt"))
-    pick(v("win1", WA, WB), v("win0"), v("off1", 0, 12))
-    mm(4, v("pjq"), v("rtq"))
-    ts(v("ta1", 0, 4), ps(4, 0, 4), 12.0, OP.add)
-    cp(v("ta1", 4, 8), ps(4, 4, 8))
-    cp(v("tbt1", 0, 8), v("ta1"))
-    quant(v("tq1"), v("tbt1"))
-    peer = rank ^ 2
-    sendmx(peer, v("tl1", 0, 2), v("tq1", 0, 2), "tc1", "ts1")
-    sendmx(peer, v("win1", WB, WY), v("win1", WA, WB), "wc1", "ws1")
-    act(v("sht1", 512, 1056), v("sht0", 512, 1056), AF.Copy)
-    zero(v("xt"))
-    zero(v("trit", 3, 4 * 384, 4))
-    zero(v("ct1", 3, 1024, 4))
-    zero(v("ct1", 0, 256))
-    zero(v("lt2", 3, 640, 4))
-    own("1")
-    numbers("1", 6, 0)
-    quant(v("aq1", 160, 288), v("zt"))
-    quant(v("wq"), v("wt"))
-    quant(v("lq2", 160, 288), v("zt"))
-    before("1", True)
-    merge("1", True)
-
-    cp(v("rf", 0, 1), v("rb1", 0, 1))
-    tt(v("rf", 1, 3), pst(5, 2, 0), v("rb1", 1, 3), OP.add)
-    ts(v("xt", 0, 3), v("rf"), K - 0.5, OP.is_lt, 0.5, OP.mult)
-    quant(v("xq"), v("xt"))
-    ts(v("ntk"), v("rf"), K - 0.5, OP.is_gt, 1024.0, OP.mult)
-    for c in range(3):
-        mm(4 + c, v("triq", 128 * c, 128 * c + 128), v("xq"))
-    ts(v("ntk2"), v("ntk"), (K - 1) / 2, OP.add)
-    tt(v("ri2", 0, 3), pst(4, 3, 0), v("ntk2"), OP.add)
-    hilo("2", 3)
-    listtile("lt2", 3, col("hl2"), col("hl2", 4), [col("dhr1"), col("dl")])
-    quant(v("lq2", 0, 160), v("lt2"))
-    listmm(3, "lq2")
-    for k, val in enumerate((col("nh11"), col("nl11"))):
+    def chosen(s, places, out, win):
         for t in range(3):
-            ts(v("nbt0", 64 * k + t, 64 * k + 64, 4), v("i16", 0, 16), v("hl2", t, t + 1), OP.is_equal, val(t), OP.mult)
-    ts(v("off2"), ps(3, 0, 16), 320.0, OP.add)
+            ts(v("st" + s, t, 4 * K, 4), v("i192"), places(t), OP.is_equal)
+        quant(v("sq" + s), v("st" + s))
+        listof(3, (v("dhq" + s), v("dlq")), v("sq" + s), v("scs" + s), v("offs" + s), v("cw"))
+        pick(out, win, v("offs" + s))
+
+    own("0")
+    before("0", False)
+    merge("0")
+
+    ts(v("r2"), v("rf0"), float(K), OP.min, -float(K), OP.add)
+    ts(v("h2"), v("r2"), ROUND16, OP.add, -ROUND16, OP.add)
+    tt(v("l2"), v("r2"), v("h2"), OP.subtract)
+    for t in range(3):
+        tj = v("inf0", 8 * t + 3, 8 * t + 4)
+        ts(v("rtt", t, 16, 4), v("i4"), tj, OP.is_equal, v("h2", t, t + 1), OP.mult)
+        ts(v("rtt", 16 + t, 32, 4), v("i4"), tj, OP.is_equal, v("l2", t, t + 1), OP.mult)
+    quant(v("rtq"), v("rtt"))
+    mm(6, v("pjq"), v("rtq"))
+    ts(v("tbt1", 0, 16, 4), ps(6, 0, 4), float(K), OP.add)
+    cp(v("tbt1", 16, 32, 4), ps(6, 4, 8))
+    quant(v("tq1"), v("tbt1"))
+    sendmx(rank ^ 2, v("tl1", 0, 8), v("tq1", 0, 8), "tc1", "ts1")
+    chosen("0", col("rf0"), v("win1", WA, WA + K), v("win0"))
+    sendmx(rank ^ 2, v("win1", WB, WB + K), v("win1", WA, WA + K), "wc1", "ws1")
+    own("1")
+    tt(v("rc1"), v("tbt1", 0, 16, 4), v("tbt1", 16, 32, 4), OP.add)
+    place_numbers("1", col("rc1"), K)
+    quant(v("wq"), v("wt"))
+    before("1", True)
+    merge("1")
+
+    ts(v("xt", 0, 3), v("rf1"), K - 0.5, OP.is_lt, 0.5, OP.mult)
+    quant(v("xq"), v("xt"))
+    ts(v("ntk"), v("rf1"), K - 0.5, OP.is_gt, 1024.0, OP.mult)
+    for c in range(3):
+        mm(c, v("ordq", 128 * c, 128 * c + 128), v("xq"))
+    ts(v("ntk2"), v("ntk"), (K - 1) / 2, OP.add)
+    tt(v("plc"), pst(0, 3, 0), v("ntk2"), OP.add)
     fin = v("fin")
-    pick(fin, v("win1"), v("off2", 0, 12))
-    quant(v("nbq", 0, 128), v("nbt0"))
+    chosen("1", col("plc"), fin, v("win1"))
+    mm(4, v("nbq", 0, 128), v("sq1"), True, False)
+    mm(4, v("nbq", 2, 130), v("sq1"), False, True)
+    ts(v("nbw", 0, K, 1, 0, 1), v("ps", 4 * 512, 4 * 512 + K, 1, 0, 1), 256.0, OP.add)
+    dma("y", lambda: T.nb[:, :], lambda: T.nbw[0:1, :], [v("nbw", 0, K, 1, 0, 1)], [])
     dma("y", lambda: T.oc[:, :], lambda: T.fin[:, :].bitcast(dt.uint8), [fin], [])
     for k in range(4):
         dma("sy"[k % 2], (lambda k=k: T.osc[4 * k:4 * k + 4, :]), (lambda k=k: T.fins[32 * k:32 * k + 4, :]), [pl(fin)], [])
     for o in range(O):
-        mm(o, v("wq", 128 * o, 128 * o + 128), fin)
-    mm(7, v("lq2", 0, 128), v("nbq", 0, 128), True, False)
-    mm(7, v("lq2", 0, 128), v("nbq", 16, 144), False, True)
-    act(v("yb", 0, K), ps(0, 0, K), AF.Copy)
+        mm(5 + o, v("wq", 128 * o, 128 * o + 128), fin)
+    act(v("yb", 0, K), ps(5, 0, K), AF.Copy)
+    cp(v("yb", K, 2 * K), ps(6, 0, K))
     dma("s", lambda: T.y[:, 0:K], v("yb", 0, K), [v("yb", 0, K)], [])
-    ts(v("nbw", 0, 16, 1, 0, 32), v("ps", 7 * 512, 7 * 512 + 16, 1, 0, 32), 256.0, OP.add)
-    rec("v", lambda: g.vector.transpose(T.nbt[0:32, :], T.nbw[0:32, :]), [v("nbw")], [v("nbt")])
-    cp(v("yb", K, 2 * K), ps(1, 0, K))
-    dma("y", lambda: T.nb[:, :], lambda: T.nbt[0:12, 0:16], [v("nbt")], [])
     dma("y", lambda: T.y[:, K:2 * K], v("yb", K, 2 * K), [v("yb", K, 2 * K)], [])
+
+    acc, edges = {}, []
+    for i, r in enumerate(prog):
+        e = {j: True for j in r["after"] if r["kind"] != "a"}
+        for regs, w in ((r["reads"], False), (r["writes"], True)):
+            for x in regs:
+                for (y, yw, j) in acc.get(x[0], ()):
+                    if j == i or not (w or yw or x[0] == "ps") or not overlap(x, y):
+                        continue
+                    if prog[j]["q"] == r["q"] and prog[j]["kind"] == "c" and r["kind"] == "c":
+                        wait = yw and not (r["q"] == "t" and x[0] == "ps")
+                    else:
+                        wait = w or yw or x[0] == "ps"
+                    if x[0] == "ps" and not w and not yw and prog[j]["q"] == r["q"]:
+                        continue
+                    e[j] = e.get(j, False) or wait
+        edges.append(e)
+        for x in r["reads"]:
+            acc.setdefault(x[0], []).append((x, False, i))
+        for x in r["writes"]:
+            acc.setdefault(x[0], []).append((x, True, i))
+
+    WAKE = 80.0
+    lag = {"c": 0.0, "d": 1600.0, "r": 1900.0, "a": 0.0}
+    n = len(prog)
+    preds = [dict(e) for e in edges]
+    for i, r in enumerate(prog):
+        if r["kind"] == "a":
+            preds[i][r["after"][0]] = True
+    succ = [[] for _ in prog]
+    for i, e in enumerate(preds):
+        for j, wait in e.items():
+            succ[j].append((i, wait))
+    tail = [0.0] * n
+
+    def gap(j, i, wait):
+        if not wait:
+            return 0.0
+        return lag[prog[j]["kind"]] + (WAKE if prog[j]["q"] != prog[i]["q"] or prog[j]["kind"] != "c" else 30.0)
+
+    for j in range(n - 1, -1, -1):
+        t = 0.0
+        for i, wait in succ[j]:
+            t = max(t, tail[i] + gap(j, i, wait))
+        tail[j] = t + prog[j]["cost"] + lag[prog[j]["kind"]] * (not succ[j])
+    left, ready, start = [len(e) for e in preds], {}, [0.0] * n
+    free, order = {}, []
+    for i in range(n):
+        if not left[i]:
+            ready[i] = 0.0
+    while ready:
+        best = None
+        for q in set(prog[i]["q"] for i in ready):
+            f = free.get(q, 0.0)
+            cand = [(max(f, t), i) for i, t in ready.items() if prog[i]["q"] == q]
+            first = min(cand)[0]
+            pickd = max((c for c in cand if c[0] <= first + 60.0), key=lambda c: (tail[c[1]] - c[0], -c[1]))
+            if best is None or pickd < best:
+                best = pickd
+        t, i = best
+        del ready[i]
+        q = prog[i]["q"]
+        start[i] = t
+        end = t + prog[i]["cost"]
+        if q is not None:
+            free[q] = end
+        order.append(i)
+        for k, wait in succ[i]:
+            left[k] -= 1
+            if not left[k]:
+                ready[k] = max([start[j] + prog[j]["cost"] + gap(j, k, wt) for j, wt in preds[k].items()])
+    place = {i: k for k, i in enumerate(order)}
+    deps = [sorted(place[j] for j, wait in edges[i].items() if wait) for i in order]
+    prog = [prog[i] for i in order]
 
     know, snap, need, used = {}, [], [], set()
     key = lambda i: (prog[i]["q"], i) if prog[i]["kind"] == "c" else (i, 0)
     for i, r in enumerate(prog):
         k = know.setdefault(r["q"], {}) if r["q"] else {}
         last = {}
-        for d in r["deps"]:
-            a, n = key(d)
-            if k.get(a, -1) < n and (a not in last or key(last[a])[1] < n):
+        for d in deps[i]:
+            a, m = key(d)
+            if k.get(a, -1) < m and (a not in last or key(last[a])[1] < m):
                 last[a] = d
         ds = sorted(last.values())
         ds = [d for d in ds if not any(e != d and snap[e].get(key(d)[0], -1) >= key(d)[1] for e in ds)]
         for d in ds:
             used.add(d)
-            for a, n in snap[d].items():
-                if k.get(a, -1) < n:
-                    k[a] = n
+            for a, m in snap[d].items():
+                if k.get(a, -1) < m:
+                    k[a] = m
         s = dict(k)
         s[key(i)[0]] = key(i)[1]
         snap.append(s)

@@ -12,6 +12,10 @@ _TOP = {}
 _ALIGN = {BF: 16, F32: 8, I32: 8, U16: 16}
 _ALONE = ("ut", "urt", "nurt", "grt", "wt", "nbw", "yb")
 _CONST = []
+ORDER = {}
+TRIALS, MOVES = 60, 24000
+GUESSES = ((1.0, 1.0, 100.0, 0.0, 1500.0, 1700.0), (1.2, 1.2, 60.0, 20.0, 2000.0, 2500.0), (1.0, 0.8, 200.0, 50.0, 1500.0, 2000.0), (1.3, 1.6, 100.0, 50.0, 1500.0, 2000.0))
+BASE = (33000.0, 38000.0, 36000.0, 42000.0)
 
 
 def _buf(name, n, t):
@@ -42,7 +46,7 @@ for _n, _w, _t in (
     _buf(_n, _w, _t)
 for _n, _w, _t in (
         ("ut", 4, BF), ("urt", 512, BF), ("nurt", 512, BF), ("grt", 4 * P, BF), ("wt", 1024, BF),
-        ("srow", P, F32), ("scol", 4, F32), ("c0t", 4 * P, BF), ("p0", 16, F32), ("junk", 128, BF), ("junk2", 2 * K, BF),
+        ("srow", P, F32), ("scol", 4, F32), ("c0t", 4 * P, BF), ("p0", 16, F32), ("junk", 10 * 128, BF), ("junk2", 4 * K, BF),
         ("x0", 4, F32), ("x1", 4, F32), ("x2", 4, F32), ("x3", 4, F32), ("rk0", 4, F32), ("rc0", 4, F32), ("sc", K, F32), ("off0", 12, U16),
         ("rtt", 512, BF), ("r2", 3, F32), ("h2", 3, F32), ("l2", 3, F32), ("pj", 3, F32), ("pjt", 512, BF), ("rc1", 4, F32),
         ("ordt", 4 * 384, BF), ("nnc", 3, F32), ("xt", 512, BF), ("ntk", 3, F32), ("ntk2", 3, F32), ("plc", 3, F32), ("nbt", 4 * 132, BF), ("nbw", K, F32), ("yb", O * K, F32)):
@@ -292,10 +296,12 @@ def rank_program(g, core, T, topo):
 
     def count(c):
         for t in range(c + 1):
-            act(v("junk"), v("c0t", 512 * c + t, 512 * c + 512, 4), AF.Copy, accum=v("p0", 4 * c + t, 4 * c + t + 1))
+            k = c * (c + 1) // 2 + t
+            act(v("junk", 128 * k, 128 * k + 128), v("c0t", 512 * c + t, 512 * c + 512, 4), AF.Copy, accum=v("p0", 4 * c + t, 4 * c + t + 1))
         quant(v("c0q", 128 * c, 128 * c + 128), v("c0t", 512 * c, 512 * c + 512))
         mm(c, v("c0q", 128 * c, 128 * c + 128), v("oneq"))
-        tt(v("x%d" % c), v("b511") if c == 0 else v("x%d" % (c - 1)), v("p0", 4 * c, 4 * c + 4), OP.subtract)
+        if c < 3:
+            tt(v("x%d" % c), v("b511") if c == 0 else v("x%d" % (c - 1)), v("p0", 4 * c, 4 * c + 4), OP.subtract)
 
     for c in range(4):
         sizes(c)
@@ -303,7 +309,8 @@ def rank_program(g, core, T, topo):
         compare(c)
     for c in range(4):
         count(c)
-    tt(v("rk0"), pst(0, 4, 0), v("x3"), OP.add)
+    tt(v("x3"), pst(0, 4, 0), v("x2"), OP.add)
+    tt(v("rk0"), v("x3"), v("p0", 12, 16), OP.subtract)
 
     ts(v("rc0"), v("rk0"), float(K), OP.min)
     ts(v("tbt0", 0, 16, 4), v("rc0"), ROUND16, OP.add, -ROUND16, OP.add)
@@ -380,10 +387,10 @@ def rank_program(g, core, T, topo):
             mm(4 + t, v("oq" + s, 128 * t, 128 * t + 128), v("shq" + s))
             act(v("inf" + s, 8 * t, 8 * t + 8), ps(4 + t, 0, 8), AF.Copy)
         inf = lambda k: v("inf" + s, k, 24, 8)
-        ts_a = v("ft" + s, 0, 3)
+        ftA = v("ft" + s, 0, 3)
         tt(v("nc" + s), inf(0), inf(1), OP.add)
-        tt(ts_a, inf(2), v("isa"), OP.mult)
-        ts(v("fo" + s), ts_a, 2.0, OP.mult, -0.5, OP.add)
+        tt(ftA, inf(2), v("isa"), OP.mult)
+        ts(v("fo" + s), ftA, 2.0, OP.mult, -0.5, OP.add)
         quant(v("ftq" + s), v("ft" + s))
         mm(4, v("triq", 0, 128), v("ftq" + s))
         mm(5, v("triq", 128, 256), v("ftq" + s))
@@ -442,7 +449,8 @@ def rank_program(g, core, T, topo):
             act(x, v("arow" + s), AF.Sign, bias=v("acol" + s, t, t + 1), scale=-1.0)
             tt(v("ct" + s, t, 4 * K, 4), x, ps(4 + t, 0, K), OP.is_gt)
         for t in (2, 1):
-            act(v("junk2", K * (t - 1), K * t), v("ct" + s, t, 4 * K, 4), AF.Identity, scale=v("nisa", t, t + 1), accum=v("rs" + s, t, t + 1))
+            k = 2 * int(s) + t - 1
+            act(v("junk2", K * k, K * k + K), v("ct" + s, t, 4 * K, 4), AF.Identity, scale=v("nisa", t, t + 1), accum=v("rs" + s, t, t + 1))
         quant(v("cq" + s), v("ct" + s))
         mm(4, v("cq" + s, 0, 128), v("oneq"))
         mm(5, v("cq" + s, 128, 256), v("oneq"))
@@ -526,8 +534,6 @@ def rank_program(g, core, T, topo):
         for x in r["writes"]:
             acc.setdefault(x[0], []).append((x, True, i))
 
-    WAKE = 80.0
-    lag = {"c": 0.0, "d": 1600.0, "r": 1900.0, "a": 0.0}
     n = len(prog)
     preds = [dict(e) for e in edges]
     for i, r in enumerate(prog):
@@ -537,44 +543,109 @@ def rank_program(g, core, T, topo):
     for i, e in enumerate(preds):
         for j, wait in e.items():
             succ[j].append((i, wait))
-    tail = [0.0] * n
 
-    def gap(j, i, wait):
-        if not wait:
-            return 0.0
-        return lag[prog[j]["kind"]] + (WAKE if prog[j]["q"] != prog[i]["q"] or prog[j]["kind"] != "c" else 30.0)
+    def guess(compute, product, wake, same, local, link):
+        cost = [r["cost"] * (product if r["q"] == "t" else 1.0 if r["kind"] != "c" else compute) for r in prog]
+        lag = {"c": 0.0, "d": local, "r": link, "a": 0.0}
+        gaps = [{j: (0.0 if not wait else lag[prog[j]["kind"]] + (same if prog[j]["q"] == prog[i]["q"] and prog[j]["kind"] == "c" else wake)) for j, wait in e.items()} for i, e in enumerate(preds)]
+        return cost, lag, gaps, cost, [lag[r["kind"]] for r in prog], [[(j, d) for j, d in e.items() if d] for e in gaps]
 
-    for j in range(n - 1, -1, -1):
-        t = 0.0
-        for i, wait in succ[j]:
-            t = max(t, tail[i] + gap(j, i, wait))
-        tail[j] = t + prog[j]["cost"] + lag[prog[j]["kind"]] * (not succ[j])
-    left, ready, start = [len(e) for e in preds], {}, [0.0] * n
-    free, order = {}, []
-    for i in range(n):
-        if not left[i]:
-            ready[i] = 0.0
-    while ready:
-        best = None
-        for q in set(prog[i]["q"] for i in ready):
-            f = free.get(q, 0.0)
-            cand = [(max(f, t), i) for i, t in ready.items() if prog[i]["q"] == q]
-            first = min(cand)[0]
-            pickd = max((c for c in cand if c[0] <= first + 60.0), key=lambda c: (tail[c[1]] - c[0], -c[1]))
-            if best is None or pickd < best:
-                best = pickd
-        t, i = best
-        del ready[i]
-        q = prog[i]["q"]
-        start[i] = t
-        end = t + prog[i]["cost"]
-        if q is not None:
-            free[q] = end
-        order.append(i)
-        for k, wait in succ[i]:
-            left[k] -= 1
-            if not left[k]:
-                ready[k] = max([start[j] + prog[j]["cost"] + gap(j, k, wt) for j, wt in preds[k].items()])
+    qn = {q: k for k, q in enumerate("vstgy")}
+    queue = [qn.get(r["q"], 5) for r in prog]
+
+    def length(order, model):
+        cost, lag, gaps = model[3:]
+        end, free, top = [0.0] * n, [0.0] * 6, 0.0
+        for i in order:
+            q = queue[i]
+            x = free[q] if q < 5 else 0.0
+            for j, d in gaps[i]:
+                y = end[j] + d
+                if y > x:
+                    x = y
+            x += cost[i]
+            end[i] = free[q] = x
+            if x + lag[i] > top:
+                top = x + lag[i]
+        return top
+
+    def total(order):
+        return sum([length(order, m) / b for m, b in zip(models, BASE)])
+
+    def arrange(model, weight, margin, soon):
+        cost, lag, gaps = model[:3]
+        tail = [0.0] * n
+        for j in range(n - 1, -1, -1):
+            tail[j] = max([tail[i] + gaps[i][j] for i, wait in succ[j]] + [lag[prog[j]["kind"]]]) + cost[j]
+        urge = [t * w for t, w in zip(tail, weight)]
+        left, ready, end, free, order = [len(e) for e in preds], {}, [0.0] * n, {}, []
+        for i in range(n):
+            if not left[i]:
+                ready.setdefault(prog[i]["q"], {})[i] = 0.0
+        for _ in range(n):
+            best = None
+            for q, calls in ready.items():
+                if not calls:
+                    continue
+                f = free.get(q, 0.0) if q else 0.0
+                top = max(urge[i] for i in calls)
+                c = [(max(f, t + (margin if urge[i] < top - 1500.0 else 0.0)), -urge[i], i) for i, t in calls.items()]
+                first = min(c)[0]
+                for x in sorted((x for x in c if x[0] <= first + soon), key=lambda x: x[1]):
+                    e = x[0] + cost[x[2]]
+                    if not any(y[0] < e - soon and y[1] < x[1] - 300.0 for y in c):
+                        break
+                else:
+                    x = min((y for y in c if y[0] <= first + soon), key=lambda y: y[1])
+                if best is None or x < best:
+                    best = x
+            i = best[2]
+            q = prog[i]["q"]
+            t = ready[q].pop(i)
+            end[i] = max(t, free.get(q, 0.0) if q else 0.0) + cost[i]
+            free[q] = end[i]
+            order.append(i)
+            for k, wait in succ[i]:
+                left[k] -= 1
+                if not left[k]:
+                    ready.setdefault(prog[k]["q"], {})[k] = max(end[j] + d if d else end[j] - cost[j] for j, d in gaps[k].items())
+        return order
+
+    if "order" not in ORDER:
+        models = [guess(*x) for x in GUESSES]
+        state, found = 1, None
+        for trial in range(TRIALS):
+            weight = []
+            for i in range(n):
+                state = (state * 1103515245 + 12345) % 2 ** 31
+                weight.append(1.0 + (state / 2.0 ** 31 - 0.5) * (0.0, 0.02, 0.05, 0.1)[trial % 4])
+            o = arrange(models[trial % len(models)], weight, (0.0, 80.0, 160.0, 240.0, 320.0)[trial % 5], (30.0, 60.0, 100.0)[trial % 3])
+            t = total(o)
+            if found is None or t < found[0]:
+                found = (t, o)
+        t, order = found
+        state, place = 7, {i: k for k, i in enumerate(order)}
+        for trial in range(MOVES):
+            state = (state * 1103515245 + 12345) % 2 ** 31
+            a = (state >> 8) % n
+            i = order[a]
+            lo = max([place[j] + 1 for j in preds[i]] + [a - 60, 0])
+            hi = min([place[k] - 1 for k, _ in succ[i]] + [a + 60, n - 1])
+            state = (state * 1103515245 + 12345) % 2 ** 31
+            b = lo + (state >> 8) % (hi - lo + 1)
+            if a == b:
+                continue
+            o = list(order)
+            o.pop(a)
+            o.insert(b, i)
+            t2 = total(o)
+            if t2 <= t:
+                t, order = t2, o
+                for k in range(min(a, b), max(a, b) + 1):
+                    place[o[k]] = k
+        ORDER["order"] = order
+        ORDER["found"] = t
+    order = ORDER["order"]
     place = {i: k for k, i in enumerate(order)}
     deps = [sorted(place[j] for j, wait in edges[i].items() if wait) for i in order]
     prog = [prog[i] for i in order]

@@ -1,21 +1,21 @@
 from concourse.mybir import dt, AluOpType as OP, ActivationFunctionType as AF
 
 P, K, O = 512, 192, 2
-WB, WA, WZ, WM, WY, WE = 0, 192, 384, 416, 608, 672
-NSEM = 40
-MID = 320
+WA, WB, WZ, WM, WY, WE = 32, 224, 416, 448, 640, 704
+NSEM = 48
+MID = 352
 ROUND16 = 1.5 * 2.0 ** 27
 BF, F32, I32, U16, CODE, U8 = "bfloat16", "float32", "int32", "uint16", "float8_e4m3fn_x4", "uint8"
 SCRATCH = {"ps": ("psum", [128, 4096], F32)}
 PLACE = {}
 _TOP = {}
 _ALIGN = {BF: 16, F32: 8, I32: 8, U16: 16}
-_ALONE = ("ut", "urt", "nurt", "grt", "wt", "nbw", "yb")
+_ALONE = ("ut", "urt", "grt", "wt", "nbw", "yb")
 _CONST = []
 ORDER = {}
 TRIALS, MOVES = 60, 24000
 GUESSES = ((1.0, 1.0, 100.0, 0.0, 1500.0, 1700.0), (1.2, 1.2, 60.0, 20.0, 2000.0, 2500.0), (1.0, 0.8, 200.0, 50.0, 1500.0, 2000.0), (1.3, 1.6, 100.0, 50.0, 1500.0, 2000.0))
-BASE = (33000.0, 38000.0, 36000.0, 42000.0)
+BASE = (29700.0, 35200.0, 34000.0, 40900.0)
 
 
 def _buf(name, n, t):
@@ -37,31 +37,32 @@ def _mx(name, n):
 
 
 for _n, _w, _t in (
-        ("one", 512, BF), ("zt", 512, BF), ("i16", K, BF), ("i128", 128, BF), ("i192", K, BF), ("i4", 4, BF), ("idt", 128, BF), ("et", 2048, BF),
-        ("ni", 4, I32), ("nl", 4, I32), ("nf", 4, F32), ("nlf", 4, F32), ("nx", 4, F32), ("nrept", 1024, BF), ("dlt", 512, BF), ("trit", 1024, BF), ("shc", 20, BF),
-        ("kw", 16, F32), ("kwz", 16, F32), ("jv", 3, I32), ("jw", 3, I32), ("jf", 3, F32), ("jwf", 3, F32), ("dl", 3, F32), ("dh0", 3, F32),
-        ("isa", 3, F32), ("nisa", 3, F32), ("isbm", 3, F32), ("basea", 3, F32), ("b511", 4, F32),
-        ("lk", K, F32), ("lk2", K, F32), ("cb", 1, F32), ("cn", 1, F32), ("cw", 1, F32), ("cth", 1, F32), ("nl1p", 1, F32)):
+        ("one", 512, BF), ("zt", 544, BF), ("i16", K, BF), ("i192", K, BF), ("idt", 128, BF), ("ebf", 528, BF), ("e2t", 512, BF), ("mone", 128, BF), ("tri0", 128, BF),
+        ("ni", 1, I32), ("nl", 1, I32), ("nf", 4, F32), ("nlf", 1, F32), ("nx", 4, F32), ("nrept", 1088, BF), ("dlt", 512, BF), ("trit", 1024, BF),
+        ("jx", 2, F32), ("jdt", 512, BF), ("idn", 4 * K, BF), ("zo", 8, U16),
+        ("kw", 12, F32), ("jw", 3, I32), ("jf", 3, F32), ("jwf", 3, F32), ("dl", 3, F32), ("dh0", 3, F32),
+        ("isa", 3, F32), ("nisa", 3, F32), ("basea", 3, F32), ("b511", 4, F32),
+        ("lk", K, F32), ("cn", 1, F32), ("cw", 1, F32), ("cz", 1, F32), ("cth", 1, F32)):
     _CONST.append(_n)
     _buf(_n, _w, _t)
 for _n, _w, _t in (
-        ("ut", 4, BF), ("urt", 512, BF), ("nurt", 512, BF), ("grt", 4 * P, BF), ("wt", 1024, BF),
-        ("srow", P, F32), ("scol", 4, F32), ("c0t", 4 * P, BF), ("p0", 16, F32), ("junk", 10 * 128, BF), ("junk2", 4 * K, BF),
-        ("x0", 4, F32), ("x1", 4, F32), ("x2", 4, F32), ("x3", 4, F32), ("rk0", 4, F32), ("rc0", 4, F32), ("sc", K, F32), ("off0", 12, U16),
-        ("rtt", 512, BF), ("r2", 3, F32), ("h2", 3, F32), ("l2", 3, F32), ("pj", 3, F32), ("pjt", 512, BF), ("rc1", 4, F32),
-        ("ordt", 4 * 384, BF), ("nnc", 3, F32), ("xt", 512, BF), ("ntk", 3, F32), ("ntk2", 3, F32), ("plc", 3, F32), ("nbt", 4 * 132, BF), ("nbw", K, F32), ("yb", O * K, F32)):
+        ("ut", 4, BF), ("urt", 552, BF), ("grt", 4 * P, BF), ("wt", 1024, BF),
+        ("srow", P, F32), ("scol", 4, F32), ("xd", 512, BF), ("c0t", 4 * P, BF), ("p0", 16, F32), ("junk", 10 * 128, BF), ("junk2", 4 * K, BF), ("junk3", 4 * K, BF),
+        ("x0", 4, F32), ("x1", 4, F32), ("x2", 4, F32), ("x3", 4, F32), ("rk0", 4, F32), ("ot", 4 * K, BF), ("sc", K, F32), ("off0", 12, U16),
+        ("ordt", 4 * 384, BF), ("nnc", 3, F32), ("misc", 832, BF), ("dht", 512, BF), ("tau", 4 * K, BF), ("ct", 4 * K, BF), ("st", 4 * K, BF),
+        ("ntk", 3, F32), ("ntk2", 3, F32), ("plc", 3, F32), ("nbw", K, F32), ("yb", O * K, F32)):
     _buf(_n, _w, _t)
-for _n, _w in (("ur", 128), ("nur", 128), ("q0", P), ("wq", 256), ("oneq", 128), ("zq", 128), ("nrep", 256), ("dlq", 128), ("eq", 512), ("triq", 256), ("c0q", P),
-               ("rtq", 128), ("pjq", 128), ("ordq", 384), ("xq", 128), ("nbq", 132), ("fin", K)):
+for _n, _w in (("ur", 128), ("uq", 136), ("q0", P), ("wq", 256), ("oneq", 128), ("zq", 128), ("nrep", 256), ("dlq", 128), ("eq", 640), ("triq", 256),
+               ("jdq", 128), ("idq", K), ("ndcq", 144), ("c0q", P), ("oh", 320), ("ordq", 384), ("xq", 128), ("rep", 128), ("repb", 128), ("fin", K)):
     _mx(_n, _w)
 for _s in "01":
     for _n, _w, _t in (
-            ("tbt", 512, BF), ("td", 8, F32), ("vt", 1024, BF), ("ot", 4 * 384, BF), ("scb", K, F32), ("off1", 12, U16), ("offb", 12, U16), ("ub", 12, F32), ("ub2", 12, F32),
-            ("shm", 4, F32), ("sht", 512, BF), ("nr", 384, BF), ("inf", 24, F32), ("nc", 3, F32), ("ft", 512, BF), ("fo", 3, F32), ("fm", 3, F32), ("dhr", 3, F32), ("dht", 512, BF),
-            ("tau", 4 * K, BF), ("ht", 4 * K, BF), ("arow", K, F32), ("acol", 3, F32), ("v", 3 * K, BF), ("ct", 1024, BF), ("rs", 3, F32), ("bs", 3, F32), ("rf", 3, F32),
-            ("st", 4 * K, BF), ("scs", K, F32), ("offs", 12, U16)):
+            ("na", 3, F32), ("nc", 3, F32), ("nr", 384, BF), ("mt", 4 * K, BF), ("scb", K, F32), ("off1", 12, U16), ("offb", 12, U16), ("ub", 12, F32), ("ub2", 12, F32),
+            ("bor", K, BF), ("keep", 2, F32), ("fm", 2, F32), ("dhr", 2, F32), ("du", 2, F32), ("fo", 3, F32), ("bi", 2, F32),
+            ("ht", 4 * K, BF), ("arow", K, F32), ("acol", 3, F32), ("v", 3 * K, BF), ("rs", 3, F32), ("bs", 3, F32), ("rf", 3, F32),
+            ("scs", K, F32), ("offs", 12, U16)):
         _buf(_n + _s, _w, _t)
-    for _n, _w in (("tq", 128), ("tl", 136), ("valq", 256), ("oq", 384), ("win", WE), ("ash", K), ("bp", 256), ("shq", 128), ("ftq", 128), ("dhq", 128), ("tauq", K), ("cq", 256), ("sq", K)):
+    for _n, _w in (("nbq", 128), ("tl", 128), ("mtq", 256), ("win", WE), ("an", K), ("bp", K), ("ftq", 136), ("dhq", 128), ("tauq", K), ("ndq", 136), ("cq", 256), ("sq", 320)):
         _mx(_n + _s, _w)
 ARR = ["tc0", "ts0", "wc0", "ws0", "tc1", "ts1", "wc1", "ws1"]
 SEMAPHORES = ["q_v", "q_s", "q_t", "q_g"] + ["d%d" % i for i in range(NSEM)] + ["l_" + a for a in ARR] + ["a_" + a for a in ARR]
@@ -108,7 +109,7 @@ def rank_program(g, core, T, topo):
         return len(prog) - 1
 
     tens = lambda *xs: [x for x in xs if isinstance(x, tuple)]
-    short = lambda x: x[0][1:] in (BF, U16) or x[0] in ("ut", "urt", "nurt", "grt", "wt")
+    short = lambda x: x[0][1:] in (BF, U16) or x[0] in ("ut", "urt", "grt", "wt")
 
     def easy(*xs):
         return 0.83 * max(64, width(xs[0]) * (0.5 if all(short(x) for x in xs) else 1))
@@ -185,10 +186,11 @@ def rank_program(g, core, T, topo):
         i, out, n = sent[key]
         rec(None, None, [], [out], 0, "a", "a_" + key, n, [i])
 
-    ps = lambda bank, a, b: v("ps", 512 * bank + a, 512 * bank + b)
+    ps = lambda bank, a, b, s=1: v("ps", 512 * bank + a, 512 * bank + b, s)
     pst = lambda bank, n, c: v("ps", 512 * bank + c, 512 * (bank + n - 1) + c + 1, 512)
     col = lambda name, o=0: (lambda t: v(name, o + t, o + t + 1))
     one = v("one", 0, 128)
+    eb = lambda b: v("eq", 128 * b, 128 * b + 128)
 
     def iota(out, pattern, base, cm, flag=True):
         kw = {"allow_small_or_imprecise_dtypes": True} if flag else {}
@@ -204,95 +206,104 @@ def rank_program(g, core, T, topo):
 
     fill(v("one"), 1.0)
     fill(v("zt"))
-    iota(v("ni"), [[128, 4]], 0, 1, False)
+    fill(v("zo"), 0)
+    select(v("idt"), one, [[-1, 128]], OP.is_equal, 0.0, 0, 1)
+    fill(v("mone"), -0.5)
+    select(v("tri0"), v("mone"), [[1, 128]], OP.is_gt, 2.0, 0, -1)
+    iota(v("ni"), [[0, 1]], 0, 1, False)
+    iota(v("nf"), [[128, 4]], -256, 1)
+    iota(v("b511"), [[-128, 4]], 511, -1)
     iota(v("i16"), [[0, 12], [1, 16]], 0, 0)
     iota(v("i192"), [[1, K]], 0, 0)
-    iota(v("jv"), [[128, 3]], 0, 1, False)
+    iota(v("jf"), [[128, 3]], 0, 1)
     iota(v("jw"), [[128, 3]], 16, 1, False)
-    iota(v("kw"), [[16, 16]], 0, 0)
-    iota(v("i128"), [[1, 128]], 0, 0)
-    iota(v("i4"), [[1, 4]], -2, 0)
+    iota(v("kw"), [[16, 12]], WA, 0)
     ts(v("nl"), v("ni"), 15, OP.bitwise_and)
-    cp(v("nf"), v("ni"))
     cp(v("nlf"), v("nl"))
-    ts(v("b511"), v("nf"), -1.0, OP.mult, 511.0, OP.add)
-    tt(v("nx"), v("nf"), v("nlf"), OP.subtract)
-    ts(v("nx"), v("nx"), -256.0, OP.add)
+    nlf = v("nlf")
+    ts(v("nx"), v("nf"), nlf, OP.subtract)
     for t in (1, 2, 3):
         fill(v("c0t", t, 512 * t, 4))
     fill(v("p0"))
     quant(v("oneq"), v("one"))
-    nlf = v("nlf", 0, 1)
     ts(v("lk"), v("i16"), nlf, OP.is_equal, -1.0e6, OP.mult)
-    ts(v("nl1p"), nlf, 1.0, OP.add)
-    ts(v("lk2"), v("i16"), v("nl1p"), OP.is_equal, 4096.0, OP.mult)
-    tt(v("lk"), v("lk"), v("lk2"), OP.add)
-    ts(v("cb"), nlf, 14.5, OP.is_lt, -4096.0, OP.mult)
-    ts(v("cn"), v("cb"), 256.0, OP.add)
-    ts(v("cw"), v("cb"), float(MID), OP.add)
-    ts(v("cth"), v("cb"), -1.0, OP.mult, K - 0.5, OP.add)
+    act(v("lk"), v("lk"), AF.Copy, bias=4096.0)
+    lift = lambda out, c, f=1.0: act(out, nlf, AF.Copy, scale=4096.0 * f, bias=c - 4096.0 * 15 * f)
+    lift(v("cn"), 256.0)
+    lift(v("cw"), float(MID))
+    lift(v("cz"), float(K))
+    lift(v("cth"), -0.5, -1.0)
     ts(v("kw"), v("kw"), nlf, OP.add)
-    ts(v("kwz"), v("kw"), -float(WZ), OP.add)
-    cp(v("jf"), v("jv"))
     ts(v("jw"), v("jw"), 31, OP.bitwise_and)
     cp(v("jwf"), v("jw"))
-    ts(v("dl"), v("jwf"), -16.0, OP.add)
-    tt(v("dh0"), v("jf"), v("dl"), OP.subtract)
-    ts(v("dh0"), v("dh0"), -float(MID), OP.add)
+    act(v("dl"), v("jwf"), AF.Copy, bias=-16.0)
+    tt(v("dh0"), v("jf"), v("jwf"), OP.subtract)
+    act(v("dh0"), v("dh0"), AF.Copy, bias=16.0 + WA - MID)
     ts(v("isa"), v("jf"), K - 0.5, OP.is_gt)
-    ts(v("nisa"), v("isa"), -1.0, OP.mult)
+    act(v("nisa"), v("isa"), AF.Copy, scale=-1.0)
     tt(v("basea"), v("jf"), v("isa"), OP.mult)
-    ts(v("isbm"), v("jf"), K - 0.5, OP.is_lt, float(WM), OP.mult)
     select(v("trit", 1, 1024, 4), v("one", 0, 256), [[1, 256]], OP.is_gt, 0.0, 0, -1)
     select(v("trit", 2, 1024, 4), v("one", 0, 256), [[1, 256]], OP.is_gt, 0.0, -128, -1)
     select(v("trit", 1, 1024, 4), v("trit", 1, 1024, 4), [[1, 256]], OP.not_equal, -960.0, 0, -1)
     select(v("trit", 2, 1024, 4), v("trit", 2, 1024, 4), [[1, 256]], OP.not_equal, -960.0, -128, -1)
     zero(v("trit", 0, 1024, 4))
     zero(v("trit", 3, 1024, 4))
-    select(v("idt"), one, [[-1, 128]], OP.is_equal, 0.0, 0, 1)
-    for b in range(4):
-        zero(v("et", 512 * b, 512 * b + 512))
-        act(v("et", 512 * b + b, 512 * b + 512, 4), v("idt"), AF.Copy)
+    fill(v("ebf"))
+    act(v("ebf", 8, 520, 4), v("idt"), AF.Copy)
+    select(v("e2t"), v("ebf", 8, 520), [[1, 512]], OP.not_equal, 1.0, -2, -4)
     for t in range(4):
-        act(v("nrept", t, 512, 4), one, AF.Identity, scale=v("nx", t, t + 1))
-        act(v("nrept", 512 + t, 1024, 4), one, AF.Identity, scale=v("nlf", t, t + 1))
+        act(v("nrept", 64 + t, 576, 4), one, AF.Identity, scale=v("nx", t, t + 1))
+    act(v("nrept", 576, 1088), v("one"), AF.Identity, scale=nlf)
+    fill(v("nrept", 0, 64))
+    for c in (1, 4):
+        act(v("nrept", 4 * c, 4 * c + 4), v("nx"), AF.Copy)
+        act(v("nrept", 4 * c + 8, 4 * c + 12), v("one", 0, 4), AF.Identity, scale=nlf)
+    act(v("nrept", 48, 49), v("isa", 1, 2), AF.Copy)
+    act(v("nrept", 49, 50), v("one", 0, 1), AF.Copy)
     zero(v("dlt", 3, 512, 4))
     for t in range(3):
         act(v("dlt", t, 512, 4), one, AF.Identity, scale=v("dl", t, t + 1))
-    act(v("shc", 0, 4), v("nx"), AF.Copy)
-    act(v("shc", 4, 8), v("nlf"), AF.Copy)
-    zero(v("shc", 8, 12))
-    iota(v("shc", 12, 16), [[1, 4]], -2, 0)
-    act(v("shc", 16, 20), v("one", 0, 4), AF.Identity, scale=v("nx", 2, 3))
-    for name, a, b, s in (("tbt0", 0, 512, 1), ("tbt1", 0, 512, 1), ("sht0", 0, 512, 1), ("sht1", 0, 512, 1), ("ft0", 0, 512, 1), ("ft1", 0, 512, 1),
-                          ("dht0", 3, 512, 4), ("dht1", 3, 512, 4), ("tau0", 3, 4 * K, 4), ("tau1", 3, 4 * K, 4), ("st0", 3, 4 * K, 4), ("st1", 3, 4 * K, 4),
-                          ("ct0", 3, 4 * K, 4), ("ct1", 3, 4 * K, 4), ("ct0", 4 * K, 1024, 1), ("ct1", 4 * K, 1024, 1),
-                          ("rtt", 0, 512, 1), ("pjt", 3, 512, 4), ("ordt", 3, 4 * 384, 4), ("xt", 0, 512, 1), ("nbt", 0, 264, 1), ("nbt", 264, 528, 1), ("rf0", 0, 1, 1), ("rf1", 0, 1, 1)):
-        zero(v(name, a, b, s))
-    for s in "01":
-        act(v("sht" + s, 0, 20), v("shc"), AF.Copy)
-    quant(v("zq"), v("zt"))
+    tt(v("jx", 0, 1), v("nx", 0, 1), v("isa", 1, 2), OP.mult)
+    tt(v("jx", 1, 2), nlf, v("isa", 1, 2), OP.mult)
+    for e, x in enumerate((v("jx", 0, 1), v("nx", 1, 2), v("jx", 1, 2), nlf)):
+        act(v("jdt", e, 512, 4), one, AF.Identity, scale=x)
+    for e in range(2):
+        select(v("idn", e, 4 * K, 4), v("one", 0, K), [[1, K]], OP.is_equal, 0.0, 64 - 128 * e, -1)
+        act(v("idn", 2 + e, 4 * K, 4), v("idn", e, 4 * K, 4), AF.Copy)
+    for k in range(2):
+        zero(v("misc", 416 * k, 416 * k + 416))
+    zero(v("urt", 0, 40))
+    for name, a, b, st in (("dht", 3, 512, 4), ("tau", 3, 4 * K, 4), ("st", 3, 4 * K, 4), ("ct", 3, 4 * K, 4), ("ordt", 3, 4 * 384, 4), ("rf0", 0, 1, 1), ("rf1", 0, 1, 1), ("na0", 2, 3, 1), ("na1", 2, 3, 1)):
+        zero(v(name, a, b, st))
+    act(v("dht", 2, 512, 4), one, AF.Identity, scale=v("dh0", 2, 3))
+    quant(v("zq"), v("zt", 0, 512))
+    for b in range(4):
+        quant(v("eq", 128 * b, 128 * b + 128), v("ebf", 8 - b, 520 - b))
+    quant(v("eq", 512, 640), v("e2t"))
 
     for t in range(4):
-        ts(v("urt", t, 512, 4), one, v("ut", t, t + 1), OP.mult)
-    quant(v("ur"), v("urt"))
-    act(v("nurt"), v("urt"), AF.Copy, scale=-1.0)
-    quant(v("nur"), v("nurt"))
+        ts(v("urt", 40 + t, 552, 4), one, v("ut", t, t + 1), OP.mult)
+    quant(v("ur"), v("urt", 40, 552))
 
     def sizes(c):
         qc = v("q0", 128 * c, 128 * c + 128)
-        quant(qc, v("grt", 512 * c, 512 * c + 512))
-        mm(4 + c, qc, v("ur"))
+        i = quant(qc, v("grt", 512 * c, 512 * c + 512))
+        mm(4 + c % 3, qc, v("ur"))
         mm(c, v("ur"), qc)
-        act(v("scol", c, c + 1), ps(4 + c, 0, 1), AF.Abs)
+        act(v("scol", c, c + 1), ps(4 + c % 3, 0, 1), AF.Abs)
         act(v("srow", 128 * c, 128 * c + 128), ps(c, 0, 128), AF.Abs)
+        return i
 
     def compare(c):
         for t in [c] + list(range(c)):
             blk = v("c0t", 512 * c + t, 512 * c + 512, 4)
-            ts(blk, v("srow", 128 * c, 128 * c + 128), v("scol", t, t + 1), OP.is_le)
+            row = v("srow", 128 * c, 128 * c + 128)
             if t == c:
-                select(blk, blk, [[1, 128]], OP.is_gt, 0.0, 0, -1)
+                x = v("xd", 128 * c, 128 * c + 128)
+                act(x, row, AF.Sign, bias=v("scol", c, c + 1), scale=-1.0)
+                tt(blk, x, v("tri0"), OP.is_gt)
+            else:
+                ts(blk, row, v("scol", t, t + 1), OP.is_le)
 
     def count(c):
         for t in range(c + 1):
@@ -303,8 +314,7 @@ def rank_program(g, core, T, topo):
         if c < 3:
             tt(v("x%d" % c), v("b511") if c == 0 else v("x%d" % (c - 1)), v("p0", 4 * c, 4 * c + 4), OP.subtract)
 
-    for c in range(4):
-        sizes(c)
+    early = [sizes(c) for c in range(4)]
     for c in range(4):
         compare(c)
     for c in range(4):
@@ -312,204 +322,197 @@ def rank_program(g, core, T, topo):
     tt(v("x3"), pst(0, 4, 0), v("x2"), OP.add)
     tt(v("rk0"), v("x3"), v("p0", 12, 16), OP.subtract)
 
-    ts(v("rc0"), v("rk0"), float(K), OP.min)
-    ts(v("tbt0", 0, 16, 4), v("rc0"), ROUND16, OP.add, -ROUND16, OP.add)
-    tt(v("tbt0", 16, 32, 4), v("rc0"), v("tbt0", 0, 16, 4), OP.subtract)
-    mark = quant(v("tq0"), v("tbt0"))
-    sendmx(rank ^ 1, v("tl0", 0, 8), v("tq0", 0, 8), "tc0", "ts0")
-
     def listof(bank, digits, onehot, scan, off, shift):
-        mm(bank, digits[0], onehot, True, False)
-        mm(bank, digits[1], onehot, False, True)
+        for k, d in enumerate(digits):
+            mm(bank, d, onehot, k == 0, k == len(digits) - 1)
         row = ps(bank, 0, K)
         rec("v", lambda: g.vector.tensor_tensor_scan(ap(scan), ap(v("lk")), ap(row), 0.0, OP.add, OP.max), [v("lk"), row], [scan], 0.83 * K)
         last = (scan[0], scan[1] + 15, scan[2], 16) + scan[4:]
         ts(off, last, shift, OP.add)
         return last
 
-    two = lambda name: (v(name, 0, 128), v(name, 128, 256))
+    for t in range(4):
+        ts(v("ot", t, 4 * K, 4), v("i192"), v("rk0", t, t + 1), OP.is_equal)
+    quant(v("oh", 64, 256), v("ot"))
+    for name, after in (("oh", early[0]), ("sq0", early[3])):
+        mxcopy("y", v(name, 0, 64), v("zq", 0, 64), [after])
+        mxcopy("y", v(name, 256, 320), v("zq", 0, 64), [after])
+    quant(v("nrep"), v("nrept", 64, 1088))
+    quant(v("ndcq"), v("nrept", 0, 576))
+    quant(v("idq"), v("idn"))
+    quant(v("jdq"), v("jdt"))
 
-    def place_numbers(s, scalar, a):
-        for t in range(4):
-            ts(v("ot" + s, 4 * a + t, 4 * (a + K), 4), v("i192"), scalar(t), OP.is_equal)
-        quant(v("oq" + s, a, a + K), v("ot" + s, 4 * a, 4 * (a + K)))
+    zone = {name: 48 * (6 - k) for k, name in enumerate(("nbt0", "ft0", "ndt0", "nbt1", "ft1", "ndt1", "xt"))}
+    mi = lambda name, a, b: v("misc", zone[name] + a, zone[name] + b)
 
-    quant(v("nrep"), v("nrept"))
-    place_numbers("0", col("rk0"), K)
-    listof(4, two("nrep"), v("oq0", K, 2 * K), v("sc"), v("off0"), v("cn"))
-    pick(v("win0", WA, WA + K), v("q0"), v("off0"))
-    sendmx(rank ^ 1, v("win0", WB, WB + K), v("win0", WA, WA + K), "wc0", "ws0")
-    for s in "01":
-        mxcopy("y", v("tl" + s, 8, 136), v("zq"), [mark])
-        mxcopy("y", v("win" + s, WZ, WM), v("zq", 0, WM - WZ), [mark])
-        mxcopy("y", v("win" + s, WY, WE), v("zq", 0, WE - WY), [mark])
-        mxcopy("y", v("bp" + s, K, 256), v("zq", 0, 256 - K), [mark])
-    dma("y", v("wt"), lambda: T.w[:, :], [], [v("wt")], [mark])
-    quant(v("eq"), v("et"))
-    quant(v("triq"), v("trit"))
-    quant(v("dlq"), v("dlt"))
-
-    eb = lambda b: v("eq", 128 * b, 128 * b + 128)
-
-    def numbers(s, bank, a):
-        mm(bank, v("nrep", 0, 128), v("oq" + s, a, a + K), True, False)
-        mm(bank, v("nrep", 128, 256), v("oq" + s, a, a + K), False, True)
-        act(v("nr" + s, a, a + K), ps(bank, 0, K), AF.Copy)
+    def describe(s, peer, oh, digits):
+        hi, lo = v(digits, 4, 132), v(digits, 0, 128)
+        mm(4, v(oh, 0, 128), hi, True, False)
+        mm(4, v(oh, 128, 256), lo, False, True)
+        cp(mi("nbt" + s, 0, 8), ps(4, 0, 8))
+        i = quant(v("nbq" + s), mi("nbt" + s, 0, 512))
+        sendmx(peer, v("tl" + s, 0, 8), v("nbq" + s, 0, 8), "tc" + s, "ts" + s)
+        mm(5, v(oh, 64, 192), hi, True, False)
+        mm(5, v(oh, 192, 320), lo, False, True)
+        ts(v("nc" + s, 0, 1), ps(5, 0, 1), ps(5, 2, 3), OP.add)
+        ts(v("na" + s, 1, 2), ps(5, 1, 2), ps(5, 3, 4), OP.add)
+        if s == "1":
+            pick(v("rep"), v("nbq" + s), v("zo"))
+            mm(7, v("rep"), v("idq"))
+            act(v("nr" + s, 0, K), ps(7, 0, K), AF.Copy)
+        return i
 
     def own(s):
-        act(v("td" + s), v("tbt" + s, 0, 32, 4), AF.Copy)
-        for t in range(4):
-            act(v("vt" + s, t, 512, 4), one, AF.Identity, scale=v("td" + s, t, t + 1))
-            act(v("vt" + s, 512 + t, 1024, 4), one, AF.Identity, scale=v("td" + s, 4 + t, 5 + t))
-        quant(v("valq" + s), v("vt" + s))
+        for b in range(4):
+            mm(b, eb(b), v("win" + s, WA, WB), True, False)
 
     def before(s, last):
         w = "win" + s
         arrive("tc" + s)
         arrive("ts" + s)
-        mm(6, eb(0), v("tl" + s, 0, 128), True, False)
-        mm(6, eb(0), v("tl" + s, 4, 132), False, True)
-        place_numbers(s, lambda t: ps(6, t, t + 1), 0)
-        scan = listof(7, two("valq" + s), v("oq" + s, 0, K), v("scb" + s), v("off1" + s), v("cb"))
-        pick(v("ash" + s), v(w, WA, WM), v("off1" + s))
-        for b in range(4):
-            mm(b, eb(b), v("ash" + s), True, False)
-        ts(v("ub" + s), scan, v("cth"), OP.is_lt)
-        tt(v("ub2" + s), v("ub" + s), v("kwz", 0, 12), OP.mult)
-        ts(v("offb" + s), v("ub2" + s), float(WZ), OP.add)
-        tt(v("shm" + s), v("rc" + s), ps(6, 0, 4), OP.max)
-        ts(v("sht" + s, 8, 12), v("shm" + s), K - 0.5, OP.is_lt)
-        quant(v("shq" + s), v("sht" + s))
-        numbers(s, 5, 0)
+        mm(4, eb(4), v("tl" + s))
+        for e in range(4):
+            ts(v("mt" + s, e, 4 * K, 4), v("nr" + s, 0, K), ps(4, e % 2, e % 2 + 1), OP.is_equal)
+        quant(v("mtq" + s, 0, K), v("mt" + s))
+        scan = listof(7, (v("jdq"),), v("mtq" + s, 0, K), v("scb" + s), v("off1" + s), v("cz"))
+        act(v("bor" + s), ps(7, 0, K), AF.Sign, scale=-1.0)
+        ts(v("ub" + s), scan, v("cth"), OP.is_gt)
+        tt(v("ub2" + s), v("ub" + s), v("kw"), OP.mult)
+        cp(v("offb" + s), v("ub2" + s))
+        pick(v("an" + s), v(w, 0, WB), v("offb" + s))
+        tt(v("nc" + s, 1, 3), v("na" + s, 1, 3), ps(4, 0, 2), OP.add)
+        mm(5, v("mtq" + s, 0, 128), v("ndcq", 12, 140), True, False)
+        mm(5, v("mtq" + s, 128, 256), v("ndcq", 10, 138), False, True)
+        both = ps(5, 0, 3, 2)
+        ts(v("keep" + s), both, -1.0, OP.mult, 1.0, OP.add)
+        ts(v("fm" + s), both, float(WM - WA), OP.mult)
+        tt(v("dhr" + s), v("fm" + s), v("dh0", 0, 2), OP.add)
+        for t in range(2):
+            act(v("dht", t, 512, 4), one, AF.Identity, scale=v("dhr" + s, t, t + 1))
+            k = 2 * int(s) + t
+            act(v("junk3", K * k, K * k + K), v("mt" + s, t, 4 * K, 4), AF.Copy, accum=v("du" + s, t, t + 1))
+        quant(v("dhq" + s), v("dht"))
+        tt(mi("ft" + s, 9, 11), v("du" + s), v("isa", 1, 3), OP.mult)
+        ts(v("fo" + s), mi("ft" + s, 8, 11), 2.0, OP.mult, -0.5, OP.add)
+        quant(v("ftq" + s), mi("ft" + s, 0, 544))
+        mm(6, v("triq", 0, 128), v("ftq" + s, 2, 130), True, False)
+        mm(6, v("triq", 128, 256), v("ftq" + s, 0, 128), False, True)
+        tt(v("bs" + s, 1, 3), v("basea", 1, 3), ps(6, 0, 3, 2), OP.subtract)
+        for t in range(3):
+            ts(v("tau", t, 4 * K, 4), v("nr" + s, 0, K), v("nc" + s, t, t + 1), OP.is_le, v("fo" + s, t, t + 1), OP.add)
+        quant(v("tauq" + s), v("tau"))
+        n = mi("ndt" + s, 4, 7)
+        ts(n, v("nc" + s), ROUND16, OP.add, -ROUND16, OP.add)
+        tt(mi("ndt" + s, 12, 15), v("nc" + s), n, OP.subtract)
+        act(mi("ndt" + s, 16, 19), n, AF.Copy)
+        act(mi("ndt" + s, 24, 27), mi("ndt" + s, 12, 15), AF.Copy)
+        quant(v("ndq" + s), mi("ndt" + s, 0, 544))
         if last:
-            numbers(s, 4, K)
-        for t in range(3):
-            mm(4 + t, v("oq" + s, 128 * t, 128 * t + 128), v("shq" + s))
-            act(v("inf" + s, 8 * t, 8 * t + 8), ps(4 + t, 0, 8), AF.Copy)
-        inf = lambda k: v("inf" + s, k, 24, 8)
-        ftA = v("ft" + s, 0, 3)
-        tt(v("nc" + s), inf(0), inf(1), OP.add)
-        tt(ftA, inf(2), v("isa"), OP.mult)
-        ts(v("fo" + s), ftA, 2.0, OP.mult, -0.5, OP.add)
-        quant(v("ftq" + s), v("ft" + s))
-        mm(4, v("triq", 0, 128), v("ftq" + s))
-        mm(5, v("triq", 128, 256), v("ftq" + s))
-        tt(v("bs" + s, 1, 3), v("basea", 1, 3), pst(4, 2, 0), OP.subtract)
-        for t in range(3):
-            ts(v("tau" + s, t, 4 * K, 4), v("nr" + s, 0, K), v("nc" + s, t, t + 1), OP.is_le, v("fo" + s, t, t + 1), OP.add)
-        quant(v("tauq" + s), v("tau" + s))
-        for t in range(3):
-            mm(4 + t, eb(t), v("tauq" + s))
-        tt(v("fm" + s), inf(2), v("isbm"), OP.mult)
-        tt(v("dhr" + s), v("fm" + s), v("dh0"), OP.add)
-        for t in range(3):
-            act(v("dht" + s, t, 512, 4), one, AF.Identity, scale=v("dhr" + s, t, t + 1))
-        quant(v("dhq" + s), v("dht" + s))
-        if last:
+            pick(v("repb"), v("tl" + s), v("zo"))
+            mm(6, v("repb"), v("idq"))
+            act(v("nr" + s, K, 2 * K), ps(6, 0, K), AF.Copy)
             ts(v("nnc"), v("nc" + s), -1.0, OP.mult)
             for t in range(3):
                 act(v("ordt", t, 4 * 384, 4), v("nr" + s), AF.Sign, bias=v("nnc", t, t + 1))
             quant(v("ordq"), v("ordt"))
-            act(v("nbt", 0, 3), inf(0), AF.Copy)
-            act(v("nbt", 8, 11), inf(1), AF.Copy)
-            quant(v("nbq"), v("nbt"))
-        else:
-            tt(v("pj"), inf(4), inf(1), OP.add)
-            for t in range(3):
-                ts(v("pjt", t, 512, 4), v("i128"), v("pj", t, t + 1), OP.is_equal)
-            quant(v("pjq"), v("pjt"))
+        for t in range(3):
+            mm(4 + t, eb(t), v("tauq" + s))
 
     def merge(s):
-        w, bp = "win" + s, "bp" + s
+        w, bp, an = "win" + s, "bp" + s, "an" + s
         arrive("wc" + s)
         arrive("ws" + s)
-        pick(v(bp, 0, K), v(w, 0, WM), v("offb" + s))
+        for t in range(3):
+            mm(7, v(w, WA + 128 * t, WA + 128 * t + 128), v("uq", 4 - 2 * t, 132 - 2 * t), t == 0, t == 2)
+        tt(v("bi" + s), ps(7, 0, 3, 2), v("keep" + s), OP.mult)
+        act(v("acol" + s, 2, 3), ps(7, 4, 5), AF.Abs)
+        pick(v(bp), v(w, WB, WM), v("off1" + s))
         for b in range(4):
-            mm(b, eb(b), v(bp, 0, K), False, True)
-            out = v("ht" + s, b, 4 * K, 4)
-            if b % 2:
-                act(out, ps(b, 0, K), AF.Copy)
-            else:
-                cp(out, ps(b, 0, K))
+            mm(b, eb(b), v(bp), False, True)
+            tt(v("ht" + s, b, 4 * K, 4), ps(b, 0, K), v("bor" + s), OP.mult)
         quant(v(w, WM, WM + K), v("ht" + s))
-        ur, nur = v("ur"), v("nur")
-        mm(7, ur, v(w, 0, K), True, False)
-        mm(7, nur, v(bp, 0, K), False, False)
+        ur = v("ur")
+        mm(7, ur, v(an), True, False)
         mm(7, ur, v(w, WM, WM + K), False, True)
         for t in range(2):
-            mm(t, v(w, 128 * t, 128 * t + 128), ur, True, False)
-            mm(t, v(bp, 128 * t, 128 * t + 128), nur, False, False)
-            mm(t, v(w, WM + 128 * t, WM + 128 * t + 128), ur, False, True)
-        mm(2, v(w, 256, 384), ur)
-        act(v("acol" + s, 2, 3), ps(2, 0, 1), AF.Abs)
+            mm(0, v(w, WM + 128 * t, WM + 128 * t + 128), v("uq", 4 - 2 * t, 132 - 2 * t), t == 0, t == 1)
         act(v("arow" + s), ps(7, 0, K), AF.Abs)
-        act(v("acol" + s, 0, 2), pst(0, 2, 0), AF.Abs)
+        for t in range(2):
+            act(v("acol" + s, t, t + 1), ps(0, 2 * t, 2 * t + 1), AF.Abs, bias=v("bi" + s, t, t + 1))
         for t in (2, 0, 1):
             x = v("v" + s, K * t, K * t + K)
             act(x, v("arow" + s), AF.Sign, bias=v("acol" + s, t, t + 1), scale=-1.0)
-            tt(v("ct" + s, t, 4 * K, 4), x, ps(4 + t, 0, K), OP.is_gt)
+            tt(v("ct", t, 4 * K, 4), x, ps(4 + t, 0, K), OP.is_gt)
         for t in (2, 1):
             k = 2 * int(s) + t - 1
-            act(v("junk2", K * k, K * k + K), v("ct" + s, t, 4 * K, 4), AF.Identity, scale=v("nisa", t, t + 1), accum=v("rs" + s, t, t + 1))
-        quant(v("cq" + s), v("ct" + s))
-        mm(4, v("cq" + s, 0, 128), v("oneq"))
-        mm(5, v("cq" + s, 128, 256), v("oneq"))
+            act(v("junk2", K * k, K * k + K), v("ct", t, 4 * K, 4), AF.Identity, scale=v("nisa", t, t + 1), accum=v("rs" + s, t, t + 1))
+        quant(v("cq" + s, 0, K), v("ct"))
+        mm(1, v("cq" + s, 0, 128), v("oneq"))
+        mm(2, v("cq" + s, 128, 256), v("oneq"))
         tt(v("rf" + s, 1, 3), v("bs" + s, 1, 3), v("rs" + s, 1, 3), OP.add)
-        tt(v("rf" + s, 0, 2), pst(4, 2, 0), v("rf" + s, 0, 2), OP.add)
+        tt(v("rf" + s, 0, 2), pst(1, 2, 0), v("rf" + s, 0, 2), OP.add)
 
-    def chosen(s, places, out, win):
+    def place(s, places):
         for t in range(3):
-            ts(v("st" + s, t, 4 * K, 4), v("i192"), places(t), OP.is_equal)
-        quant(v("sq" + s), v("st" + s))
-        listof(3, (v("dhq" + s), v("dlq")), v("sq" + s), v("scs" + s), v("offs" + s), v("cw"))
-        pick(out, win, v("offs" + s))
+            ts(v("st", t, 4 * K, 4), v("i192"), places(t), OP.is_equal)
+        quant(v("sq" + s, 64, 256), v("st"))
 
+    def chosen(s, out):
+        listof(6, (v("dhq" + s), v("dlq")), v("sq" + s, 64, 256), v("scs" + s), v("offs" + s), v("cw"))
+        pick(out, v("win" + s), v("offs" + s))
+
+    mark = describe("0", rank ^ 1, "oh", "ndcq")
+    listof(6, (v("nrep", 0, 128), v("nrep", 128, 256)), v("oh", 64, 256), v("sc"), v("off0"), v("cn"))
+    act(v("nr0", 0, K), ps(6, 0, K), AF.Copy)
+    pick(v("win0", WA, WB), v("q0"), v("off0"))
+    sendmx(rank ^ 1, v("win0", WB, WZ), v("win0", WA, WB), "wc0", "ws0")
+    for s in "01":
+        after = early[3] if s == "0" else mark
+        mxcopy("y", v("tl" + s, 8, 128), v("zq", 0, 120), [after])
+        mxcopy("y", v("mtq" + s, K, 256), v("zq", 0, 256 - K), [after])
+        mxcopy("y", v("cq" + s, K, 256), v("zq", 0, 256 - K), [after])
+        mxcopy("y", v("win" + s, 0, WA), v("zq", 0, WA), [after])
+        mxcopy("y", v("win" + s, WZ, WM), v("zq", 0, WM - WZ), [after])
+        mxcopy("y", v("win" + s, WY, WE), v("zq", 0, WE - WY), [after])
+    dma("y", v("wt"), lambda: T.w[:, :], [], [v("wt")], [mark])
+    act(v("urt", 16, 20), v("ut"), AF.Copy)
+    quant(v("uq"), v("urt", 0, 544))
+    quant(v("triq"), v("trit"))
+    quant(v("dlq"), v("dlt"))
     own("0")
     before("0", False)
     merge("0")
 
-    ts(v("r2"), v("rf0"), float(K), OP.min, -float(K), OP.add)
-    ts(v("h2"), v("r2"), ROUND16, OP.add, -ROUND16, OP.add)
-    tt(v("l2"), v("r2"), v("h2"), OP.subtract)
-    for t in range(3):
-        tj = v("inf0", 8 * t + 3, 8 * t + 4)
-        ts(v("rtt", t, 16, 4), v("i4"), tj, OP.is_equal, v("h2", t, t + 1), OP.mult)
-        ts(v("rtt", 16 + t, 32, 4), v("i4"), tj, OP.is_equal, v("l2", t, t + 1), OP.mult)
-    quant(v("rtq"), v("rtt"))
-    mm(6, v("pjq"), v("rtq"))
-    ts(v("tbt1", 0, 16, 4), ps(6, 0, 4), float(K), OP.add)
-    cp(v("tbt1", 16, 32, 4), ps(6, 4, 8))
-    quant(v("tq1"), v("tbt1"))
-    sendmx(rank ^ 2, v("tl1", 0, 8), v("tq1", 0, 8), "tc1", "ts1")
-    chosen("0", col("rf0"), v("win1", WA, WA + K), v("win0"))
-    sendmx(rank ^ 2, v("win1", WB, WB + K), v("win1", WA, WA + K), "wc1", "ws1")
-    own("1")
-    tt(v("rc1"), v("tbt1", 0, 16, 4), v("tbt1", 16, 32, 4), OP.add)
-    place_numbers("1", col("rc1"), K)
+    place("0", col("rf0"))
+    describe("1", rank ^ 2, "sq0", "ndq0")
+    chosen("0", v("win1", WA, WB))
+    sendmx(rank ^ 2, v("win1", WB, WZ), v("win1", WA, WB), "wc1", "ws1")
     quant(v("wq"), v("wt"))
+    own("1")
     before("1", True)
     merge("1")
 
-    ts(v("xt", 0, 3), v("rf1"), K - 0.5, OP.is_lt, 0.5, OP.mult)
-    quant(v("xq"), v("xt"))
+    ts(mi("xt", 0, 3), v("rf1"), K - 0.5, OP.is_lt, 0.5, OP.mult)
+    quant(v("xq"), mi("xt", 0, 512))
     ts(v("ntk"), v("rf1"), K - 0.5, OP.is_gt, 1024.0, OP.mult)
     for c in range(3):
         mm(c, v("ordq", 128 * c, 128 * c + 128), v("xq"))
     ts(v("ntk2"), v("ntk"), (K - 1) / 2, OP.add)
     tt(v("plc"), pst(0, 3, 0), v("ntk2"), OP.add)
     fin = v("fin")
-    chosen("1", col("plc"), fin, v("win1"))
-    mm(4, v("nbq", 0, 128), v("sq1"), True, False)
-    mm(4, v("nbq", 2, 130), v("sq1"), False, True)
+    place("1", col("plc"))
+    chosen("1", fin)
+    mm(4, v("ndq1", 4, 132), v("sq1", 64, 256), True, False)
+    mm(4, v("ndq1", 6, 134), v("sq1", 64, 256), False, True)
     ts(v("nbw", 0, K, 1, 0, 1), v("ps", 4 * 512, 4 * 512 + K, 1, 0, 1), 256.0, OP.add)
     dma("y", lambda: T.nb[:, :], lambda: T.nbw[0:1, :], [v("nbw", 0, K, 1, 0, 1)], [])
     dma("y", lambda: T.oc[:, :], lambda: T.fin[:, :].bitcast(dt.uint8), [fin], [])
     for k in range(4):
         dma("sy"[k % 2], (lambda k=k: T.osc[4 * k:4 * k + 4, :]), (lambda k=k: T.fins[32 * k:32 * k + 4, :]), [pl(fin)], [])
     for o in range(O):
-        mm(5 + o, v("wq", 128 * o, 128 * o + 128), fin)
+        mm(5 + 2 * o, v("wq", 128 * o, 128 * o + 128), fin)
     act(v("yb", 0, K), ps(5, 0, K), AF.Copy)
-    cp(v("yb", K, 2 * K), ps(6, 0, K))
+    cp(v("yb", K, 2 * K), ps(7, 0, K))
     dma("s", lambda: T.y[:, 0:K], v("yb", 0, K), [v("yb", 0, K)], [])
     dma("y", lambda: T.y[:, K:2 * K], v("yb", K, 2 * K), [v("yb", K, 2 * K)], [])
 

from concourse.mybir import dt, AluOpType as OP, ActivationFunctionType as AF

P, K, O = 512, 192, 2
WA, WB, WZ, WM, WY, WE = 32, 224, 416, 448, 640, 704
NSEM = 48
MID = 352
ROUND16 = 1.5 * 2.0 ** 27
BF, F32, I32, U16, CODE, U8 = "bfloat16", "float32", "int32", "uint16", "float8_e4m3fn_x4", "uint8"
SCRATCH = {"ps": ("psum", [128, 4096], F32)}
PLACE = {}
_TOP = {}
_ALIGN = {BF: 16, F32: 8, I32: 8, U16: 16}
_ALONE = ("ut", "urt", "grt", "wt", "nbw", "yb")
_CONST = []
ORDER = {}
TRIALS, MOVES = 60, 24000
GUESSES = ((1.0, 1.0, 100.0, 0.0, 1500.0, 1700.0), (1.2, 1.2, 60.0, 20.0, 2000.0, 2500.0), (1.0, 0.8, 200.0, 50.0, 1500.0, 2000.0), (1.3, 1.6, 100.0, 50.0, 1500.0, 2000.0))
BASE = (29700.0, 35200.0, 34000.0, 40900.0)


def _buf(name, n, t):
    assert name not in PLACE, name
    if t in _ALIGN and name not in _ALONE:
        home = ("k" if name in _CONST else "m") + t
        top = _TOP.get(home, 0)
        PLACE[name] = (home, top, n)
        _TOP[home] = -(-(top + n) // _ALIGN[t]) * _ALIGN[t]
        SCRATCH[home] = ("sbuf", [128, _TOP[home]], t)
    else:
        SCRATCH[name] = ("sbuf", [128, n], t)
        PLACE[name] = (name, 0, n)


def _mx(name, n):
    _buf(name, n, CODE)
    _buf(name + "s", n, U8)


for _n, _w, _t in (
        ("one", 512, BF), ("zt", 544, BF), ("i16", K, BF), ("i192", K, BF), ("idt", 128, BF), ("ebf", 528, BF), ("e2t", 512, BF), ("mone", 128, BF), ("tri0", 128, BF),
        ("ni", 1, I32), ("nl", 1, I32), ("nf", 4, F32), ("nlf", 1, F32), ("nx", 4, F32), ("nrept", 1088, BF), ("dlt", 512, BF), ("trit", 1024, BF),
        ("jx", 2, F32), ("jdt", 512, BF), ("idn", 4 * K, BF), ("zo", 8, U16),
        ("kw", 12, F32), ("jw", 3, I32), ("jf", 3, F32), ("jwf", 3, F32), ("dl", 3, F32), ("dh0", 3, F32),
        ("isa", 3, F32), ("nisa", 3, F32), ("basea", 3, F32), ("b511", 4, F32),
        ("lk", K, F32), ("cn", 1, F32), ("cw", 1, F32), ("cz", 1, F32), ("cth", 1, F32)):
    _CONST.append(_n)
    _buf(_n, _w, _t)
for _n, _w, _t in (
        ("ut", 4, BF), ("urt", 552, BF), ("grt", 4 * P, BF), ("wt", 1024, BF),
        ("srow", P, F32), ("scol", 4, F32), ("xd", 512, BF), ("c0t", 4 * P, BF), ("p0", 16, F32), ("junk", 10 * 128, BF), ("junk2", 4 * K, BF), ("junk3", 4 * K, BF),
        ("x0", 4, F32), ("x1", 4, F32), ("x2", 4, F32), ("x3", 4, F32), ("rk0", 4, F32), ("ot", 4 * K, BF), ("sc", K, F32), ("off0", 12, U16),
        ("ordt", 4 * 384, BF), ("nnc", 3, F32), ("misc", 832, BF), ("dht", 512, BF), ("tau", 4 * K, BF), ("ct", 4 * K, BF), ("st", 4 * K, BF),
        ("ntk", 3, F32), ("ntk2", 3, F32), ("plc", 3, F32), ("nbw", K, F32), ("yb", O * K, F32)):
    _buf(_n, _w, _t)
for _n, _w in (("ur", 128), ("uq", 136), ("q0", P), ("wq", 256), ("oneq", 128), ("zq", 128), ("nrep", 256), ("dlq", 128), ("eq", 640), ("triq", 256),
               ("jdq", 128), ("idq", K), ("ndcq", 144), ("c0q", P), ("oh", 320), ("ordq", 384), ("xq", 128), ("rep", 128), ("repb", 128), ("fin", K)):
    _mx(_n, _w)
for _s in "01":
    for _n, _w, _t in (
            ("na", 3, F32), ("nc", 3, F32), ("nr", 384, BF), ("mt", 4 * K, BF), ("scb", K, F32), ("off1", 12, U16), ("offb", 12, U16), ("ub", 12, F32), ("ub2", 12, F32),
            ("bor", K, BF), ("keep", 2, F32), ("fm", 2, F32), ("dhr", 2, F32), ("du", 2, F32), ("fo", 3, F32), ("bi", 2, F32),
            ("ht", 4 * K, BF), ("arow", K, F32), ("acol", 3, F32), ("v", 3 * K, BF), ("rs", 3, F32), ("bs", 3, F32), ("rf", 3, F32),
            ("scs", K, F32), ("offs", 12, U16)):
        _buf(_n + _s, _w, _t)
    for _n, _w in (("nbq", 128), ("tl", 128), ("mtq", 256), ("win", WE), ("an", K), ("bp", K), ("ftq", 136), ("dhq", 128), ("tauq", K), ("ndq", 136), ("cq", 256), ("sq", 320)):
        _mx(_n + _s, _w)
ARR = ["tc0", "ts0", "wc0", "ws0", "tc1", "ts1", "wc1", "ws1"]
SEMAPHORES = ["q_v", "q_s", "q_t", "q_g"] + ["d%d" % i for i in range(NSEM)] + ["l_" + a for a in ARR] + ["a_" + a for a in ARR]


def rank_program(g, core, T, topo):
    rank = T.rank_of(core)
    if rank is None:
        return
    ENG = {"v": g.vector, "s": g.scalar, "t": g.tensor, "g": g, "y": g.sync}
    prog, nd, sent = [], [0], {}

    def v(name, a=0, b=None, s=1, p=0, e=128, cast=None):
        if name == "ps":
            return (name, a, b, s, p, e, cast)
        home, o, n = PLACE[name]
        return (home, o + a, o + (n if b is None else b), s, p, e, cast)

    def ap(x):
        if not isinstance(x, tuple):
            return x
        name, a, b, s, p, e, cast = x
        t = T[name]
        r = t[p:e, a:b] if s == 1 else t[p:e, a:b:s]
        if cast is None:
            return r
        return r.bitcast(dt.uint8 if cast == 8 else dt.uint32)

    def width(x):
        return len(range(x[1], x[2], x[3]))

    def overlap(x, y):
        if x[0] == "ps":
            f = lambda r: set(c // 512 for c in range(r[1], r[2], r[3] if r[3] == 512 else 1))
            return bool(f(x) & f(y))
        if x[1] >= y[2] or y[1] >= x[2]:
            return False
        if x[3] == y[3] and x[3] > 1:
            return (x[1] - y[1]) % x[3] == 0
        return True

    def rec(q, fn, reads, writes, cost, kind="c", sem=None, amount=0, after=()):
        prog.append({"q": q, "fn": fn, "reads": reads, "writes": writes, "cost": cost, "kind": kind, "sem": sem, "amount": amount, "after": list(after)})
        return len(prog) - 1

    tens = lambda *xs: [x for x in xs if isinstance(x, tuple)]
    short = lambda x: x[0][1:] in (BF, U16) or x[0] in ("ut", "urt", "grt", "wt")

    def easy(*xs):
        return 0.83 * max(64, width(xs[0]) * (0.5 if all(short(x) for x in xs) else 1))

    def ts(out, in0, s1, op0, s2=None, op1=None):
        if op1 is None:
            fn = lambda: g.vector.tensor_scalar(out=ap(out), in0=ap(in0), scalar1=ap(s1), scalar2=None, op0=op0)
        else:
            fn = lambda: g.vector.tensor_scalar(out=ap(out), in0=ap(in0), scalar1=ap(s1), scalar2=ap(s2), op0=op0, op1=op1)
        return rec("v", fn, tens(in0, s1, s2), [out], easy(out, in0))

    def tt(out, a, b, op):
        f = 1 if "ps" in (a[0], b[0]) else 2
        rec("v", lambda: g.vector.tensor_tensor(out=ap(out), in0=ap(a), in1=ap(b), op=op), [a, b], [out], 0.83 * max(64, f * width(out)))

    def cp(out, a):
        rec("v", lambda: g.vector.tensor_copy(ap(out), ap(a)), [a], [out], easy(out, a))

    def fill(out, c=0.0):
        rec("v", lambda: g.vector.memset(ap(out), c), [], [out], easy(out))

    def act(out, a, func, bias=None, scale=None, accum=None):
        kw = {}
        if bias is not None:
            kw["bias"] = bias
        if scale is not None:
            kw["scale"] = scale
        if accum is not None:
            kw["accum_out"] = accum
        rec("s", lambda: g.scalar.activation(ap(out), ap(a), func, **{k: ap(x) for k, x in kw.items()}), tens(a, bias, scale), tens(out, accum), 0.83 * max(64, width(out)) + (20 if accum else 0))

    def zero(out):
        act(out, v("zt", 0, width(out)), AF.Copy)

    def pl(x):
        return (x[0] + "s",) + x[1:6] + (None,)

    def quant(out, a):
        return rec("v", lambda: g.vector.quantize_mx(ap(out), ap(pl(out)), ap(a)), [a], [out, pl(out)], 12 + 0.22 * width(a))

    def mm(bank, l, r, start=True, stop=True):
        out = v("ps", 512 * bank, 512 * bank + width(r))
        rec("t", lambda: g.tensor.matmul_mx(ap(out), ap(l), ap(pl(l)), ap(r), ap(pl(r)), start, stop), [l, pl(l), r, pl(r)], [out], 1.2 * (width(r) + 16))

    def pick(out, win, off):
        c = lambda x: x[:6] + (32,)
        n = 1.3 * width(out)
        rec("v", lambda: g.vector.tensor_copy(ap(c(out)), ap(c(win)).indirect(ap(off))), [win, off], [out], 50 + n)
        rec("s", lambda: g.scalar.activation(ap(pl(out)), ap(pl(win)).indirect(ap(off)), AF.Copy), [pl(win), off], [pl(out)], 65 + n)

    def dma(q, out, in_, reads, writes, after=()):
        n = nd[0]
        nd[0] += 1
        rec(q, lambda: ENG[q].dma_start(out() if not isinstance(out, tuple) else ap(out), in_() if not isinstance(in_, tuple) else ap(in_)), reads, writes, 60, "d", "d%d" % n, 16, after)

    def mxcopy(q, out, in_, after=()):
        c = lambda x: x[:6] + (8,)
        dma(q, c(out), c(in_), [in_], [out], after)
        dma(q, pl(out), pl(in_), [pl(in_)], [pl(out)], after)

    def send(peer, out, in_, key):
        dst = T.cores[peer]
        rid, pid, _ = topo.addr(dst)
        m, n = topo.mask(core, dst), len(topo.engines(core, dst))
        i = rec("g", lambda: g.remote_dma(ap(out), ap(in_), T.sem["a_" + key], T.sem["l_" + key], pid, rid, m), [in_], [], 120, "r", "l_" + key, n)
        sent[key] = (i, out, len(topo.engines(dst, core)))

    def sendmx(peer, out, in_, kc, ks):
        c = lambda x: x[:6] + (8,)
        send(peer, c(out), c(in_), kc)
        send(peer, pl(out), pl(in_), ks)

    def arrive(key):
        i, out, n = sent[key]
        rec(None, None, [], [out], 0, "a", "a_" + key, n, [i])

    ps = lambda bank, a, b, s=1: v("ps", 512 * bank + a, 512 * bank + b, s)
    pst = lambda bank, n, c: v("ps", 512 * bank + c, 512 * (bank + n - 1) + c + 1, 512)
    col = lambda name, o=0: (lambda t: v(name, o + t, o + t + 1))
    one = v("one", 0, 128)
    eb = lambda b: v("eq", 128 * b, 128 * b + 128)

    def iota(out, pattern, base, cm, flag=True):
        kw = {"allow_small_or_imprecise_dtypes": True} if flag else {}
        rec("g", lambda: g.iota(ap(out), pattern, base, cm, **kw), [], [out], 130 + 1.66 * width(out))

    def select(out, in_, pattern, op, fillv, base, cm):
        rec("g", lambda: g.affine_select(ap(out), ap(in_), pattern, op, fillv, base, cm), [in_], [out], 170 + 1.66 * width(out))

    dma("y", v("ut"), lambda: T.u[:, 0:4], [], [v("ut")])
    for c in range(4):
        x = v("grt", 512 * c, 512 * c + 512)
        dma("sy"[c % 2], x, (lambda c=c: T.gr[:, 512 * c:512 * c + 512]), [], [x])

    fill(v("one"), 1.0)
    fill(v("zt"))
    fill(v("zo"), 0)
    select(v("idt"), one, [[-1, 128]], OP.is_equal, 0.0, 0, 1)
    fill(v("mone"), -0.5)
    select(v("tri0"), v("mone"), [[1, 128]], OP.is_gt, 2.0, 0, -1)
    iota(v("ni"), [[0, 1]], 0, 1, False)
    iota(v("nf"), [[128, 4]], -256, 1)
    iota(v("b511"), [[-128, 4]], 511, -1)
    iota(v("i16"), [[0, 12], [1, 16]], 0, 0)
    iota(v("i192"), [[1, K]], 0, 0)
    iota(v("jf"), [[128, 3]], 0, 1)
    iota(v("jw"), [[128, 3]], 16, 1, False)
    iota(v("kw"), [[16, 12]], WA, 0)
    ts(v("nl"), v("ni"), 15, OP.bitwise_and)
    cp(v("nlf"), v("nl"))
    nlf = v("nlf")
    ts(v("nx"), v("nf"), nlf, OP.subtract)
    for t in (1, 2, 3):
        fill(v("c0t", t, 512 * t, 4))
    fill(v("p0"))
    quant(v("oneq"), v("one"))
    ts(v("lk"), v("i16"), nlf, OP.is_equal, -1.0e6, OP.mult)
    act(v("lk"), v("lk"), AF.Copy, bias=4096.0)
    lift = lambda out, c, f=1.0: act(out, nlf, AF.Copy, scale=4096.0 * f, bias=c - 4096.0 * 15 * f)
    lift(v("cn"), 256.0)
    lift(v("cw"), float(MID))
    lift(v("cz"), float(K))
    lift(v("cth"), -0.5, -1.0)
    ts(v("kw"), v("kw"), nlf, OP.add)
    ts(v("jw"), v("jw"), 31, OP.bitwise_and)
    cp(v("jwf"), v("jw"))
    act(v("dl"), v("jwf"), AF.Copy, bias=-16.0)
    tt(v("dh0"), v("jf"), v("jwf"), OP.subtract)
    act(v("dh0"), v("dh0"), AF.Copy, bias=16.0 + WA - MID)
    ts(v("isa"), v("jf"), K - 0.5, OP.is_gt)
    act(v("nisa"), v("isa"), AF.Copy, scale=-1.0)
    tt(v("basea"), v("jf"), v("isa"), OP.mult)
    select(v("trit", 1, 1024, 4), v("one", 0, 256), [[1, 256]], OP.is_gt, 0.0, 0, -1)
    select(v("trit", 2, 1024, 4), v("one", 0, 256), [[1, 256]], OP.is_gt, 0.0, -128, -1)
    select(v("trit", 1, 1024, 4), v("trit", 1, 1024, 4), [[1, 256]], OP.not_equal, -960.0, 0, -1)
    select(v("trit", 2, 1024, 4), v("trit", 2, 1024, 4), [[1, 256]], OP.not_equal, -960.0, -128, -1)
    zero(v("trit", 0, 1024, 4))
    zero(v("trit", 3, 1024, 4))
    fill(v("ebf"))
    act(v("ebf", 8, 520, 4), v("idt"), AF.Copy)
    select(v("e2t"), v("ebf", 8, 520), [[1, 512]], OP.not_equal, 1.0, -2, -4)
    for t in range(4):
        act(v("nrept", 64 + t, 576, 4), one, AF.Identity, scale=v("nx", t, t + 1))
    act(v("nrept", 576, 1088), v("one"), AF.Identity, scale=nlf)
    fill(v("nrept", 0, 64))
    for c in (1, 4):
        act(v("nrept", 4 * c, 4 * c + 4), v("nx"), AF.Copy)
        act(v("nrept", 4 * c + 8, 4 * c + 12), v("one", 0, 4), AF.Identity, scale=nlf)
    act(v("nrept", 48, 49), v("isa", 1, 2), AF.Copy)
    act(v("nrept", 49, 50), v("one", 0, 1), AF.Copy)
    zero(v("dlt", 3, 512, 4))
    for t in range(3):
        act(v("dlt", t, 512, 4), one, AF.Identity, scale=v("dl", t, t + 1))
    tt(v("jx", 0, 1), v("nx", 0, 1), v("isa", 1, 2), OP.mult)
    tt(v("jx", 1, 2), nlf, v("isa", 1, 2), OP.mult)
    for e, x in enumerate((v("jx", 0, 1), v("nx", 1, 2), v("jx", 1, 2), nlf)):
        act(v("jdt", e, 512, 4), one, AF.Identity, scale=x)
    for e in range(2):
        select(v("idn", e, 4 * K, 4), v("one", 0, K), [[1, K]], OP.is_equal, 0.0, 64 - 128 * e, -1)
        act(v("idn", 2 + e, 4 * K, 4), v("idn", e, 4 * K, 4), AF.Copy)
    for k in range(2):
        zero(v("misc", 416 * k, 416 * k + 416))
    zero(v("urt", 0, 40))
    for name, a, b, st in (("dht", 3, 512, 4), ("tau", 3, 4 * K, 4), ("st", 3, 4 * K, 4), ("ct", 3, 4 * K, 4), ("ordt", 3, 4 * 384, 4), ("rf0", 0, 1, 1), ("rf1", 0, 1, 1), ("na0", 2, 3, 1), ("na1", 2, 3, 1)):
        zero(v(name, a, b, st))
    act(v("dht", 2, 512, 4), one, AF.Identity, scale=v("dh0", 2, 3))
    quant(v("zq"), v("zt", 0, 512))
    for b in range(4):
        quant(v("eq", 128 * b, 128 * b + 128), v("ebf", 8 - b, 520 - b))
    quant(v("eq", 512, 640), v("e2t"))

    for t in range(4):
        ts(v("urt", 40 + t, 552, 4), one, v("ut", t, t + 1), OP.mult)
    quant(v("ur"), v("urt", 40, 552))

    def sizes(c):
        qc = v("q0", 128 * c, 128 * c + 128)
        i = quant(qc, v("grt", 512 * c, 512 * c + 512))
        mm(4 + c % 3, qc, v("ur"))
        mm(c, v("ur"), qc)
        act(v("scol", c, c + 1), ps(4 + c % 3, 0, 1), AF.Abs)
        act(v("srow", 128 * c, 128 * c + 128), ps(c, 0, 128), AF.Abs)
        return i

    def compare(c):
        for t in [c] + list(range(c)):
            blk = v("c0t", 512 * c + t, 512 * c + 512, 4)
            row = v("srow", 128 * c, 128 * c + 128)
            if t == c:
                x = v("xd", 128 * c, 128 * c + 128)
                act(x, row, AF.Sign, bias=v("scol", c, c + 1), scale=-1.0)
                tt(blk, x, v("tri0"), OP.is_gt)
            else:
                ts(blk, row, v("scol", t, t + 1), OP.is_le)

    def count(c):
        for t in range(c + 1):
            k = c * (c + 1) // 2 + t
            act(v("junk", 128 * k, 128 * k + 128), v("c0t", 512 * c + t, 512 * c + 512, 4), AF.Copy, accum=v("p0", 4 * c + t, 4 * c + t + 1))
        quant(v("c0q", 128 * c, 128 * c + 128), v("c0t", 512 * c, 512 * c + 512))
        mm(c, v("c0q", 128 * c, 128 * c + 128), v("oneq"))
        if c < 3:
            tt(v("x%d" % c), v("b511") if c == 0 else v("x%d" % (c - 1)), v("p0", 4 * c, 4 * c + 4), OP.subtract)

    early = [sizes(c) for c in range(4)]
    for c in range(4):
        compare(c)
    for c in range(4):
        count(c)
    tt(v("x3"), pst(0, 4, 0), v("x2"), OP.add)
    tt(v("rk0"), v("x3"), v("p0", 12, 16), OP.subtract)

    def listof(bank, digits, onehot, scan, off, shift):
        for k, d in enumerate(digits):
            mm(bank, d, onehot, k == 0, k == len(digits) - 1)
        row = ps(bank, 0, K)
        rec("v", lambda: g.vector.tensor_tensor_scan(ap(scan), ap(v("lk")), ap(row), 0.0, OP.add, OP.max), [v("lk"), row], [scan], 0.83 * K)
        last = (scan[0], scan[1] + 15, scan[2], 16) + scan[4:]
        ts(off, last, shift, OP.add)
        return last

    for t in range(4):
        ts(v("ot", t, 4 * K, 4), v("i192"), v("rk0", t, t + 1), OP.is_equal)
    quant(v("oh", 64, 256), v("ot"))
    for name, after in (("oh", early[0]), ("sq0", early[3])):
        mxcopy("y", v(name, 0, 64), v("zq", 0, 64), [after])
        mxcopy("y", v(name, 256, 320), v("zq", 0, 64), [after])
    quant(v("nrep"), v("nrept", 64, 1088))
    quant(v("ndcq"), v("nrept", 0, 576))
    quant(v("idq"), v("idn"))
    quant(v("jdq"), v("jdt"))

    zone = {name: 48 * (6 - k) for k, name in enumerate(("nbt0", "ft0", "ndt0", "nbt1", "ft1", "ndt1", "xt"))}
    mi = lambda name, a, b: v("misc", zone[name] + a, zone[name] + b)

    def describe(s, peer, oh, digits):
        hi, lo = v(digits, 4, 132), v(digits, 0, 128)
        mm(4, v(oh, 0, 128), hi, True, False)
        mm(4, v(oh, 128, 256), lo, False, True)
        cp(mi("nbt" + s, 0, 8), ps(4, 0, 8))
        i = quant(v("nbq" + s), mi("nbt" + s, 0, 512))
        sendmx(peer, v("tl" + s, 0, 8), v("nbq" + s, 0, 8), "tc" + s, "ts" + s)
        mm(5, v(oh, 64, 192), hi, True, False)
        mm(5, v(oh, 192, 320), lo, False, True)
        ts(v("nc" + s, 0, 1), ps(5, 0, 1), ps(5, 2, 3), OP.add)
        ts(v("na" + s, 1, 2), ps(5, 1, 2), ps(5, 3, 4), OP.add)
        if s == "1":
            pick(v("rep"), v("nbq" + s), v("zo"))
            mm(7, v("rep"), v("idq"))
            act(v("nr" + s, 0, K), ps(7, 0, K), AF.Copy)
        return i

    def own(s):
        for b in range(4):
            mm(b, eb(b), v("win" + s, WA, WB), True, False)

    def before(s, last):
        w = "win" + s
        arrive("tc" + s)
        arrive("ts" + s)
        mm(4, eb(4), v("tl" + s))
        for e in range(4):
            ts(v("mt" + s, e, 4 * K, 4), v("nr" + s, 0, K), ps(4, e % 2, e % 2 + 1), OP.is_equal)
        quant(v("mtq" + s, 0, K), v("mt" + s))
        scan = listof(7, (v("jdq"),), v("mtq" + s, 0, K), v("scb" + s), v("off1" + s), v("cz"))
        act(v("bor" + s), ps(7, 0, K), AF.Sign, scale=-1.0)
        ts(v("ub" + s), scan, v("cth"), OP.is_gt)
        tt(v("ub2" + s), v("ub" + s), v("kw"), OP.mult)
        cp(v("offb" + s), v("ub2" + s))
        pick(v("an" + s), v(w, 0, WB), v("offb" + s))
        tt(v("nc" + s, 1, 3), v("na" + s, 1, 3), ps(4, 0, 2), OP.add)
        mm(5, v("mtq" + s, 0, 128), v("ndcq", 12, 140), True, False)
        mm(5, v("mtq" + s, 128, 256), v("ndcq", 10, 138), False, True)
        both = ps(5, 0, 3, 2)
        ts(v("keep" + s), both, -1.0, OP.mult, 1.0, OP.add)
        ts(v("fm" + s), both, float(WM - WA), OP.mult)
        tt(v("dhr" + s), v("fm" + s), v("dh0", 0, 2), OP.add)
        for t in range(2):
            act(v("dht", t, 512, 4), one, AF.Identity, scale=v("dhr" + s, t, t + 1))
            k = 2 * int(s) + t
            act(v("junk3", K * k, K * k + K), v("mt" + s, t, 4 * K, 4), AF.Copy, accum=v("du" + s, t, t + 1))
        quant(v("dhq" + s), v("dht"))
        tt(mi("ft" + s, 9, 11), v("du" + s), v("isa", 1, 3), OP.mult)
        ts(v("fo" + s), mi("ft" + s, 8, 11), 2.0, OP.mult, -0.5, OP.add)
        quant(v("ftq" + s), mi("ft" + s, 0, 544))
        mm(6, v("triq", 0, 128), v("ftq" + s, 2, 130), True, False)
        mm(6, v("triq", 128, 256), v("ftq" + s, 0, 128), False, True)
        tt(v("bs" + s, 1, 3), v("basea", 1, 3), ps(6, 0, 3, 2), OP.subtract)
        for t in range(3):
            ts(v("tau", t, 4 * K, 4), v("nr" + s, 0, K), v("nc" + s, t, t + 1), OP.is_le, v("fo" + s, t, t + 1), OP.add)
        quant(v("tauq" + s), v("tau"))
        n = mi("ndt" + s, 4, 7)
        ts(n, v("nc" + s), ROUND16, OP.add, -ROUND16, OP.add)
        tt(mi("ndt" + s, 12, 15), v("nc" + s), n, OP.subtract)
        act(mi("ndt" + s, 16, 19), n, AF.Copy)
        act(mi("ndt" + s, 24, 27), mi("ndt" + s, 12, 15), AF.Copy)
        quant(v("ndq" + s), mi("ndt" + s, 0, 544))
        if last:
            pick(v("repb"), v("tl" + s), v("zo"))
            mm(6, v("repb"), v("idq"))
            act(v("nr" + s, K, 2 * K), ps(6, 0, K), AF.Copy)
            ts(v("nnc"), v("nc" + s), -1.0, OP.mult)
            for t in range(3):
                act(v("ordt", t, 4 * 384, 4), v("nr" + s), AF.Sign, bias=v("nnc", t, t + 1))
            quant(v("ordq"), v("ordt"))
        for t in range(3):
            mm(4 + t, eb(t), v("tauq" + s))

    def merge(s):
        w, bp, an = "win" + s, "bp" + s, "an" + s
        arrive("wc" + s)
        arrive("ws" + s)
        for t in range(3):
            mm(7, v(w, WA + 128 * t, WA + 128 * t + 128), v("uq", 4 - 2 * t, 132 - 2 * t), t == 0, t == 2)
        tt(v("bi" + s), ps(7, 0, 3, 2), v("keep" + s), OP.mult)
        act(v("acol" + s, 2, 3), ps(7, 4, 5), AF.Abs)
        pick(v(bp), v(w, WB, WM), v("off1" + s))
        for b in range(4):
            mm(b, eb(b), v(bp), False, True)
            tt(v("ht" + s, b, 4 * K, 4), ps(b, 0, K), v("bor" + s), OP.mult)
        quant(v(w, WM, WM + K), v("ht" + s))
        ur = v("ur")
        mm(7, ur, v(an), True, False)
        mm(7, ur, v(w, WM, WM + K), False, True)
        for t in range(2):
            mm(0, v(w, WM + 128 * t, WM + 128 * t + 128), v("uq", 4 - 2 * t, 132 - 2 * t), t == 0, t == 1)
        act(v("arow" + s), ps(7, 0, K), AF.Abs)
        for t in range(2):
            act(v("acol" + s, t, t + 1), ps(0, 2 * t, 2 * t + 1), AF.Abs, bias=v("bi" + s, t, t + 1))
        for t in (2, 0, 1):
            x = v("v" + s, K * t, K * t + K)
            act(x, v("arow" + s), AF.Sign, bias=v("acol" + s, t, t + 1), scale=-1.0)
            tt(v("ct", t, 4 * K, 4), x, ps(4 + t, 0, K), OP.is_gt)
        for t in (2, 1):
            k = 2 * int(s) + t - 1
            act(v("junk2", K * k, K * k + K), v("ct", t, 4 * K, 4), AF.Identity, scale=v("nisa", t, t + 1), accum=v("rs" + s, t, t + 1))
        quant(v("cq" + s, 0, K), v("ct"))
        mm(1, v("cq" + s, 0, 128), v("oneq"))
        mm(2, v("cq" + s, 128, 256), v("oneq"))
        tt(v("rf" + s, 1, 3), v("bs" + s, 1, 3), v("rs" + s, 1, 3), OP.add)
        tt(v("rf" + s, 0, 2), pst(1, 2, 0), v("rf" + s, 0, 2), OP.add)

    def place(s, places):
        for t in range(3):
            ts(v("st", t, 4 * K, 4), v("i192"), places(t), OP.is_equal)
        quant(v("sq" + s, 64, 256), v("st"))

    def chosen(s, out):
        listof(6, (v("dhq" + s), v("dlq")), v("sq" + s, 64, 256), v("scs" + s), v("offs" + s), v("cw"))
        pick(out, v("win" + s), v("offs" + s))

    mark = describe("0", rank ^ 1, "oh", "ndcq")
    listof(6, (v("nrep", 0, 128), v("nrep", 128, 256)), v("oh", 64, 256), v("sc"), v("off0"), v("cn"))
    act(v("nr0", 0, K), ps(6, 0, K), AF.Copy)
    pick(v("win0", WA, WB), v("q0"), v("off0"))
    sendmx(rank ^ 1, v("win0", WB, WZ), v("win0", WA, WB), "wc0", "ws0")
    for s in "01":
        after = early[3] if s == "0" else mark
        mxcopy("y", v("tl" + s, 8, 128), v("zq", 0, 120), [after])
        mxcopy("y", v("mtq" + s, K, 256), v("zq", 0, 256 - K), [after])
        mxcopy("y", v("cq" + s, K, 256), v("zq", 0, 256 - K), [after])
        mxcopy("y", v("win" + s, 0, WA), v("zq", 0, WA), [after])
        mxcopy("y", v("win" + s, WZ, WM), v("zq", 0, WM - WZ), [after])
        mxcopy("y", v("win" + s, WY, WE), v("zq", 0, WE - WY), [after])
    dma("y", v("wt"), lambda: T.w[:, :], [], [v("wt")], [mark])
    act(v("urt", 16, 20), v("ut"), AF.Copy)
    quant(v("uq"), v("urt", 0, 544))
    quant(v("triq"), v("trit"))
    quant(v("dlq"), v("dlt"))
    own("0")
    before("0", False)
    merge("0")

    place("0", col("rf0"))
    describe("1", rank ^ 2, "sq0", "ndq0")
    chosen("0", v("win1", WA, WB))
    sendmx(rank ^ 2, v("win1", WB, WZ), v("win1", WA, WB), "wc1", "ws1")
    quant(v("wq"), v("wt"))
    own("1")
    before("1", True)
    merge("1")

    ts(mi("xt", 0, 3), v("rf1"), K - 0.5, OP.is_lt, 0.5, OP.mult)
    quant(v("xq"), mi("xt", 0, 512))
    ts(v("ntk"), v("rf1"), K - 0.5, OP.is_gt, 1024.0, OP.mult)
    for c in range(3):
        mm(c, v("ordq", 128 * c, 128 * c + 128), v("xq"))
    ts(v("ntk2"), v("ntk"), (K - 1) / 2, OP.add)
    tt(v("plc"), pst(0, 3, 0), v("ntk2"), OP.add)
    fin = v("fin")
    place("1", col("plc"))
    chosen("1", fin)
    mm(4, v("ndq1", 4, 132), v("sq1", 64, 256), True, False)
    mm(4, v("ndq1", 6, 134), v("sq1", 64, 256), False, True)
    ts(v("nbw", 0, K, 1, 0, 1), v("ps", 4 * 512, 4 * 512 + K, 1, 0, 1), 256.0, OP.add)
    dma("y", lambda: T.nb[:, :], lambda: T.nbw[0:1, :], [v("nbw", 0, K, 1, 0, 1)], [])
    dma("y", lambda: T.oc[:, :], lambda: T.fin[:, :].bitcast(dt.uint8), [fin], [])
    for k in range(4):
        dma("sy"[k % 2], (lambda k=k: T.osc[4 * k:4 * k + 4, :]), (lambda k=k: T.fins[32 * k:32 * k + 4, :]), [pl(fin)], [])
    for o in range(O):
        mm(5 + 2 * o, v("wq", 128 * o, 128 * o + 128), fin)
    act(v("yb", 0, K), ps(5, 0, K), AF.Copy)
    cp(v("yb", K, 2 * K), ps(7, 0, K))
    dma("s", lambda: T.y[:, 0:K], v("yb", 0, K), [v("yb", 0, K)], [])
    dma("y", lambda: T.y[:, K:2 * K], v("yb", K, 2 * K), [v("yb", K, 2 * K)], [])

    acc, edges = {}, []
    for i, r in enumerate(prog):
        e = {j: True for j in r["after"] if r["kind"] != "a"}
        for regs, w in ((r["reads"], False), (r["writes"], True)):
            for x in regs:
                for (y, yw, j) in acc.get(x[0], ()):
                    if j == i or not (w or yw or x[0] == "ps") or not overlap(x, y):
                        continue
                    if prog[j]["q"] == r["q"] and prog[j]["kind"] == "c" and r["kind"] == "c":
                        wait = yw and not (r["q"] == "t" and x[0] == "ps")
                    else:
                        wait = w or yw or x[0] == "ps"
                    if x[0] == "ps" and not w and not yw and prog[j]["q"] == r["q"]:
                        continue
                    e[j] = e.get(j, False) or wait
        edges.append(e)
        for x in r["reads"]:
            acc.setdefault(x[0], []).append((x, False, i))
        for x in r["writes"]:
            acc.setdefault(x[0], []).append((x, True, i))

    n = len(prog)
    preds = [dict(e) for e in edges]
    for i, r in enumerate(prog):
        if r["kind"] == "a":
            preds[i][r["after"][0]] = True
    succ = [[] for _ in prog]
    for i, e in enumerate(preds):
        for j, wait in e.items():
            succ[j].append((i, wait))

    def guess(compute, product, wake, same, local, link):
        cost = [r["cost"] * (product if r["q"] == "t" else 1.0 if r["kind"] != "c" else compute) for r in prog]
        lag = {"c": 0.0, "d": local, "r": link, "a": 0.0}
        gaps = [{j: (0.0 if not wait else lag[prog[j]["kind"]] + (same if prog[j]["q"] == prog[i]["q"] and prog[j]["kind"] == "c" else wake)) for j, wait in e.items()} for i, e in enumerate(preds)]
        return cost, lag, gaps, cost, [lag[r["kind"]] for r in prog], [[(j, d) for j, d in e.items() if d] for e in gaps]

    qn = {q: k for k, q in enumerate("vstgy")}
    queue = [qn.get(r["q"], 5) for r in prog]

    def length(order, model):
        cost, lag, gaps = model[3:]
        end, free, top = [0.0] * n, [0.0] * 6, 0.0
        for i in order:
            q = queue[i]
            x = free[q] if q < 5 else 0.0
            for j, d in gaps[i]:
                y = end[j] + d
                if y > x:
                    x = y
            x += cost[i]
            end[i] = free[q] = x
            if x + lag[i] > top:
                top = x + lag[i]
        return top

    def total(order):
        return sum([length(order, m) / b for m, b in zip(models, BASE)])

    def arrange(model, weight, margin, soon):
        cost, lag, gaps = model[:3]
        tail = [0.0] * n
        for j in range(n - 1, -1, -1):
            tail[j] = max([tail[i] + gaps[i][j] for i, wait in succ[j]] + [lag[prog[j]["kind"]]]) + cost[j]
        urge = [t * w for t, w in zip(tail, weight)]
        left, ready, end, free, order = [len(e) for e in preds], {}, [0.0] * n, {}, []
        for i in range(n):
            if not left[i]:
                ready.setdefault(prog[i]["q"], {})[i] = 0.0
        for _ in range(n):
            best = None
            for q, calls in ready.items():
                if not calls:
                    continue
                f = free.get(q, 0.0) if q else 0.0
                top = max(urge[i] for i in calls)
                c = [(max(f, t + (margin if urge[i] < top - 1500.0 else 0.0)), -urge[i], i) for i, t in calls.items()]
                first = min(c)[0]
                for x in sorted((x for x in c if x[0] <= first + soon), key=lambda x: x[1]):
                    e = x[0] + cost[x[2]]
                    if not any(y[0] < e - soon and y[1] < x[1] - 300.0 for y in c):
                        break
                else:
                    x = min((y for y in c if y[0] <= first + soon), key=lambda y: y[1])
                if best is None or x < best:
                    best = x
            i = best[2]
            q = prog[i]["q"]
            t = ready[q].pop(i)
            end[i] = max(t, free.get(q, 0.0) if q else 0.0) + cost[i]
            free[q] = end[i]
            order.append(i)
            for k, wait in succ[i]:
                left[k] -= 1
                if not left[k]:
                    ready.setdefault(prog[k]["q"], {})[k] = max(end[j] + d if d else end[j] - cost[j] for j, d in gaps[k].items())
        return order

    if "order" not in ORDER:
        models = [guess(*x) for x in GUESSES]
        state, found = 1, None
        for trial in range(TRIALS):
            weight = []
            for i in range(n):
                state = (state * 1103515245 + 12345) % 2 ** 31
                weight.append(1.0 + (state / 2.0 ** 31 - 0.5) * (0.0, 0.02, 0.05, 0.1)[trial % 4])
            o = arrange(models[trial % len(models)], weight, (0.0, 80.0, 160.0, 240.0, 320.0)[trial % 5], (30.0, 60.0, 100.0)[trial % 3])
            t = total(o)
            if found is None or t < found[0]:
                found = (t, o)
        t, order = found
        state, place = 7, {i: k for k, i in enumerate(order)}
        for trial in range(MOVES):
            state = (state * 1103515245 + 12345) % 2 ** 31
            a = (state >> 8) % n
            i = order[a]
            lo = max([place[j] + 1 for j in preds[i]] + [a - 60, 0])
            hi = min([place[k] - 1 for k, _ in succ[i]] + [a + 60, n - 1])
            state = (state * 1103515245 + 12345) % 2 ** 31
            b = lo + (state >> 8) % (hi - lo + 1)
            if a == b:
                continue
            o = list(order)
            o.pop(a)
            o.insert(b, i)
            t2 = total(o)
            if t2 <= t:
                t, order = t2, o
                for k in range(min(a, b), max(a, b) + 1):
                    place[o[k]] = k
        ORDER["order"] = order
        ORDER["found"] = t
    order = ORDER["order"]
    place = {i: k for k, i in enumerate(order)}
    deps = [sorted(place[j] for j, wait in edges[i].items() if wait) for i in order]
    prog = [prog[i] for i in order]

    know, snap, need, used = {}, [], [], set()
    key = lambda i: (prog[i]["q"], i) if prog[i]["kind"] == "c" else (i, 0)
    for i, r in enumerate(prog):
        k = know.setdefault(r["q"], {}) if r["q"] else {}
        last = {}
        for d in deps[i]:
            a, m = key(d)
            if k.get(a, -1) < m and (a not in last or key(last[a])[1] < m):
                last[a] = d
        ds = sorted(last.values())
        ds = [d for d in ds if not any(e != d and snap[e].get(key(d)[0], -1) >= key(d)[1] for e in ds)]
        for d in ds:
            used.add(d)
            for a, m in snap[d].items():
                if k.get(a, -1) < m:
                    k[a] = m
        s = dict(k)
        s[key(i)[0]] = key(i)[1]
        snap.append(s)
        need.append(ds)
    lastc = {r["q"]: i for i, r in enumerate(prog) if r["kind"] == "c"}
    used |= set(lastc.values())
    total, val = {q: 0 for q in lastc}, {}
    for i, r in enumerate(prog):
        if r["q"] is None:
            continue
        e = ENG[r["q"]]
        for d in need[i]:
            p = prog[d]
            if p["kind"] == "c":
                e.wait_ge(T.sem["q_" + p["q"]], val[d])
            else:
                e.wait_ge(T.sem[p["sem"]], p["amount"])
        ins = r["fn"]()
        if r["kind"] == "c" and i in used:
            total[r["q"]] += 1
            val[i] = total[r["q"]]
            ins.then_inc(T.sem["q_" + r["q"]], 1)
        elif r["kind"] == "d":
            ins.then_inc(T.sem[r["sem"]], 16)
    for q in total:
        g.wait_ge(T.sem["q_" + q], total[q])
    for r in prog:
        if r["kind"] in "dra":
            g.wait_ge(T.sem[r["sem"]], r["amount"])
